import numpy as np
import ml_dtypes


def mxq(x, axis, fmt="e4m3"):
    dtype, down = {"e4m3": (ml_dtypes.float8_e4m3fn, 7), "e5m2": (ml_dtypes.float8_e5m2, 14)}[fmt]
    v = np.moveaxis(np.asarray(x, np.float32).astype(ml_dtypes.bfloat16).astype(np.float64), axis, -1)
    blocks = v.reshape(v.shape[:-1] + (-1, 32))
    amax = np.abs(blocks).max(-1, keepdims=True)
    byte = np.maximum(np.where(amax > 0, np.frexp(amax)[1] - 1 + 127, 0) - down, 1)
    scale = np.exp2(byte - 127.0)
    codes = (blocks / scale).astype(np.float32).astype(dtype).astype(np.float64)
    return np.moveaxis((codes * scale).reshape(v.shape), -1, axis)


WIDE = False


def mx_kscale(k):
    if not WIDE:
        return np.ones(k)
    levels = np.array([10, -10, 5, -5, 0])
    if k % 512:
        return np.exp2(np.random.permutation(np.resize(levels, k // 32))).repeat(32)
    a = np.empty((k // 512, 16))
    for p in range(k // 512):
        a[p, :8] = np.random.permutation(np.resize(levels, 8))
        for g in range(8):
            far = levels[np.abs(levels - a[p, g]) >= 10]
            a[p, g + 8] = far[np.random.randint(len(far))]
    return np.exp2(a.ravel()).repeat(32)


def f64(x):
    return np.asarray(x).astype(np.float64)


def striped(idx):
    return np.tile(idx.reshape(-1, 16).T, (8, 1)).astype(np.uint16)


def unstriped(offs):
    return offs[:16].T.reshape(-1).astype(np.int64)


E2M1 = np.array([0.0, 0.5, 1.0, 1.5, 2.0, 3.0, 4.0, 6.0, -0.0, -0.5, -1.0, -1.5, -2.0, -3.0, -4.0, -6.0])


def pack_weight(w, fmt):
    k, n = w.shape
    w = f64(np.asarray(w, np.float32).astype(ml_dtypes.bfloat16)).reshape(k // 32, 32, n)
    amax = np.abs(w).max(1)
    if fmt == "e4m3":
        byte = np.frexp(amax)[1] - 1 + 127 - 7
    else:
        mant, ex = np.frexp(amax / 6.0)
        byte = np.where(mant > 0.5, ex, ex - 1) + 127
    byte = np.clip(np.where(amax > 0, byte, 1), 1, 254)
    scaled = (w * np.exp2(127.0 - byte)[:, None, :]).reshape(k, n).astype(np.float32)
    by_word = np.ascontiguousarray(scaled.reshape(k // 512, 128, 4, n).transpose(0, 1, 3, 2))
    if fmt == "e4m3":
        words = by_word.astype(ml_dtypes.float8_e4m3fn).view(np.uint8)
    else:
        c = by_word.astype(ml_dtypes.float4_e2m1fn).view(np.uint8) & 0xF
        words = (c[..., 0::2] | (c[..., 1::2] << 4)).reshape(k // 512, 128, 2 * n)
    return np.ascontiguousarray(words), np.ascontiguousarray(byte.astype(np.uint8).reshape(k // 512, 16, n))


def unpack_weight(words, scales, fmt):
    g, _, n = scales.shape
    words = np.ascontiguousarray(words).reshape(g, 128, n, -1)
    if fmt == "e4m3":
        vals = words.view(ml_dtypes.float8_e4m3fn).astype(np.float64)
    else:
        nib = np.empty((g, 128, n, 4), np.uint8)
        nib[..., 0::2] = words & 0xF
        nib[..., 1::2] = words >> 4
        vals = E2M1[nib]
    vals = vals * np.repeat(np.exp2(scales.astype(np.float64) - 127.0), 8, axis=1)[..., None]
    return vals.transpose(0, 1, 3, 2).reshape(g * 512, n)


def gelu(v):
    return 0.5 * v * (1.0 + np.tanh(np.sqrt(2.0 / np.pi) * (v + 0.044715 * v**3)))


def bf(x):
    return np.asarray(x, np.float32).astype(ml_dtypes.bfloat16)


def planes(Y):
    n, m = Y.shape
    b = f64(bf(Y)).reshape(n // 32, 32, m)
    amax = np.abs(b).max(1)
    byte = np.clip(np.where(amax > 0, np.frexp(amax)[1] - 1 + 127 - 7, 1), 1, 254)
    codes = (b * np.exp2(127.0 - byte)[:, None, :]).reshape(n, m).astype(np.float32).astype(ml_dtypes.float8_e4m3fn).view(np.uint8)
    words = codes.reshape(n // 512, 128, 4, m).transpose(0, 1, 3, 2)
    return np.ascontiguousarray(words), np.ascontiguousarray(byte.astype(np.uint8).reshape(n // 512, 16, m))


K, H, N, T, S, T2, P = 1024, 512, 512, 4096, 1024, 2048, 1024

def setup_inputs():
    n = np.random.standard_normal
    s = mx_kscale(K)[:, None]
    u = mx_kscale(H)[:, None]
    tab_words, tab_scales = pack_weight(n((K, T)) * s, "e4m3")
    we_words, we_scales = pack_weight(n((K, H)) / np.sqrt(K) / s, "e2m1")
    wd_words, wd_scales = pack_weight(n((K, H)) / np.sqrt(K) / s * u.T, "e4m3")
    wr = n((K, H)) / np.sqrt(K) / s * u.T
    wo = n((H, N)) / np.sqrt(H) / u * np.exp(0.8 * n(N))
    return {
        "tab_words": tab_words, "tab_scales": tab_scales,
        "offs": striped(np.random.permutation(T)[:S]),
        "offs2": striped(np.random.permutation(T2)[:S]),
        "offs3": striped(np.random.permutation(T2)[:P]),
        "we_words": we_words, "we_scales": we_scales,
        "wd_words": wd_words, "wd_scales": wd_scales,
        "wr": wr.astype(np.float32),
        "wgs": np.exp(0.3 * n((128, S))).astype(np.float32),
        "tol": (0.5 * np.exp(0.4 * n((H, P))) * u).astype(np.float32),
        "wo": wo.astype(np.float32),
    }

def reference(tab_words, tab_scales, offs, offs2, offs3, we_words, we_scales,
              wd_words, wd_scales, wr, wgs, tol, wo):
    v = unpack_weight(tab_words, tab_scales, "e4m3")[:, unstriped(offs)]
    e = np.tanh(unpack_weight(we_words, we_scales, "e2m1").T @ v)
    rec = e * (unpack_weight(wd_words, wd_scales, "e4m3").T @ v)
    h = (mxq(f64(wr), 0, "e4m3").T @ v) - rec
    page = np.zeros((H, T2))
    page[:, unstriped(offs2)] = np.tile(f64(wgs), (H // 128, 1)) * h
    x = page[:, unstriped(offs3)]
    z = mxq(np.abs(x) - f64(tol), 0, "e4m3")
    y = mxq(f64(wo), 0, "e4m3").T @ z
    words, scales = planes(y)
    return y, words, scales

@@ -1,0 +1,281 @@
+from contextlib import ExitStack
+
+import concourse.mybir as mybir
+from concourse.masks import make_identity
+
+K, H, N, T, S, T2, M = 1024, 512, 512, 4096, 1024, 2048, 1024
+FLOPS = 2 * 3 * K * H * S + 2 * H * N * M
+
+F32 = mybir.dt.float32
+BF16 = mybir.dt.bfloat16
+I32 = mybir.dt.int32
+U32 = mybir.dt.uint32
+U16 = mybir.dt.uint16
+U8 = mybir.dt.uint8
+FP8X4 = mybir.dt.float8_e4m3fn_x4
+FP4X4 = mybir.dt.float4_e2m1fn_x4
+ACT = mybir.ActivationFunctionType
+ALU = mybir.AluOpType
+
+P = 128
+PASSES = K // 512
+PAGES = H // P
+HALF = 512
+CHUNK = 256
+CHUNKS = M // CHUNK
+
+
+def tile_list_handshake_anomaly_scores_kernel(
+    tc, tab_words, tab_scales, offs, offs2, offs3, we_words, we_scales,
+    wd_words, wd_scales, wr, wgs, tol, wo, out_0, out_1, out_2,
+):
+    nc = tc.nc
+    with ExitStack() as ctx:
+        lists = ctx.enter_context(tc.tile_pool(name="lists", bufs=1))
+        keep = ctx.enter_context(tc.tile_pool(name="keep", bufs=1))
+        ring = ctx.enter_context(tc.tile_pool(name="ring", bufs=2))
+        reuse = ctx.enter_context(tc.tile_pool(name="reuse", bufs=1))
+        psum = ctx.enter_context(tc.psum_pool(name="psum", bufs=2))
+
+        idx = lists.tile([P, S // 16], U16, name="idx")
+        idx2 = lists.tile([P, S // 16], U16, name="idx2")
+        idx3 = lists.tile([P, M // 16], U16, name="idx3")
+
+        def kept(shape, dtype, name):
+            return keep.tile(shape, dtype, name=name, align_bytes=64)
+
+        def ringed(shape, dtype, name):
+            return ring.tile(shape, dtype, name=name, align_bytes=64)
+
+        tw = [kept([P, T], U32, "tw0"), reuse.tile([P, T], U32, name="tw1", offset=0, align_bytes=64)]
+        ts = kept([P, PASSES * T], U8, "ts")
+        wes = kept([P, PASSES * H], U8, "wes")
+        wds = kept([P, PASSES * H], U8, "wds")
+        wew = kept([P, PASSES * 2 * H], U8, "wew")
+        wdw = kept([P, PASSES * H], U32, "wdw")
+        wgs_sb = kept([P, S], F32, "wgs_sb")
+        pages = [kept([P, T2], F32, f"page{a}") for a in range(PAGES)]
+        ident = kept([P, P], F32, "ident")
+
+        nc.vector.memset(ts[:].bitcast(I32), 0)
+        make_identity(nc, ident[:])
+        nc.gpsimd.memset(wes[:].bitcast(I32), 0)
+        nc.gpsimd.memset(wds[:].bitcast(I32), 0)
+
+        def load_scales(tile, src, rows):
+            for r in rows:
+                nc.sync.dma_start(
+                    out=tile[r:P:32, :].bitcast(I32).rearrange("p (a c) -> p a c", a=PASSES),
+                    in_=src[:, r:16:4, :].rearrange("a q c -> q a c").bitcast(I32),
+                )
+
+        def load_table(a, lo, hi):
+            words = tab_words[a].rearrange("p t i -> p (t i)").bitcast(I32)
+            nc.sync.dma_start(out=tw[a][:, lo:hi].bitcast(I32), in_=words[:, lo:hi])
+
+        def staged(name, shape, slot):
+            return reuse.tile(shape, F32, name=name, offset=4096 * slot, align_bytes=64)
+
+        def load_wr(s, a, tile):
+            nc.sync.dma_start(out=tile, in_=wr[512 * a : 512 * (a + 1), s * P : (s + 1) * P].rearrange("(p j) c -> p j c", j=4))
+
+        nc.sync.dma_start(idx[:], offs)
+        load_table(0, 0, T)
+        load_scales(ts, tab_scales, range(4))
+        wr_first = [kept([P, 4, P], F32, f"wr_first{a}") for a in range(PASSES)]
+        for a in range(PASSES):
+            load_wr(0, a, wr_first[a][:])
+        nc.sync.dma_start(
+            out=wew[:].bitcast(I32).rearrange("p (a c) -> p a c", a=PASSES),
+            in_=we_words.rearrange("a p c -> p a c").bitcast(I32),
+        )
+        load_table(1, 0, T // 2)
+        load_scales(wes, we_scales, range(4))
+        load_scales(wds, wd_scales, range(2))
+        load_table(1, T // 2, T)
+        load_scales(wds, wd_scales, range(2, 4))
+        nc.sync.dma_start(
+            out=wdw[:].bitcast(I32).rearrange("p (a c) -> p a c", a=PASSES),
+            in_=wd_words.rearrange("a p c i -> p a (c i)").bitcast(I32),
+        )
+        nc.sync.dma_start(out=wgs_sb[:], in_=wgs)
+        nc.sync.dma_start(idx2[:], offs2)
+        nc.sync.dma_start(idx3[:], offs3)
+
+        for a in range(PAGES):
+            nc.vector.memset(pages[a][:], 0.0)
+
+        vw = [[kept([P, HALF], U32, f"vw{a}{h}") for h in range(2)] for a in range(PASSES)]
+        vs = [[kept([P, HALF], U8, f"vs{a}{h}") for h in range(2)] for a in range(PASSES)]
+
+        def half_of(lst, h):
+            return lst[:, h * (HALF // 16) : (h + 1) * (HALF // 16)]
+
+        def gather_scales(a, h):
+            nc.vector.tensor_copy(vs[a][h][:], ts[:, a * T : (a + 1) * T].indirect(half_of(idx, h)))
+
+        def gather_words(a, h):
+            nc.vector.tensor_copy(vw[a][h][:], tw[a][:].indirect(half_of(idx, h)))
+
+        wrc = [kept([P, PASSES * P], U32, f"wrc{s}") for s in range(PAGES)]
+        wrs = [kept([P, PASSES * P], U8, f"wrs{s}") for s in range(PAGES)]
+
+        def quantize_wr(s):
+            grouped = ringed([P, PASSES, P, 4], BF16, "wr_grouped")
+            if s == 0:
+                raws = [tile[:] for tile in wr_first]
+            else:
+                both = staged(f"wr_raw{s}", [P, PASSES, 4, P], s - 1)
+                raws = [both[:, a] for a in range(PASSES)]
+                for a in range(PASSES):
+                    load_wr(s, a, raws[a])
+            for a in range(PASSES):
+                raw = raws[a]
+                nc.scalar.activation(
+                    grouped[:, a].rearrange("p (c i) j -> p c j i", i=4),
+                    raw.rearrange("p j (c i) -> p c j i", i=4),
+                    ACT.Copy,
+                )
+            nc.vector.quantize_mx(out=wrc[s][:].bitcast(FP8X4), scales=wrs[s][:], in_=grouped[:].rearrange("p a c j -> p (a c j)"))
+
+        gather_scales(0, 0)
+        gather_scales(1, 0)
+        gather_words(0, 0)
+        gather_scales(0, 1)
+        gather_scales(1, 1)
+        quantize_wr(0)
+        gather_words(1, 0)
+        gather_words(0, 1)
+        gather_words(1, 1)
+
+        def product(tag, codes_of, scale_of, h):
+            acc = psum.tile([P, HALF], F32, name=tag)
+            for a in range(PASSES):
+                nc.tensor.matmul_mx(
+                    out=acc[:], lhsT=codes_of(a), lhsT_scale=scale_of(a),
+                    rhs=vw[a][h][:].bitcast(FP8X4), rhs_scale=vs[a][h][:],
+                    start=(a == 0), stop=(a == PASSES - 1),
+                )
+            return acc
+
+        def reconstruct(s, h):
+            acc_e = product("bank_e", lambda a: wew[:, 2 * (a * H + s * P) : 2 * (a * H + (s + 1) * P)].bitcast(FP4X4),
+                            lambda a: wes[:, a * H + s * P : a * H + (s + 1) * P], h)
+            acc_d = product("bank_d", lambda a: wdw[:, a * H + s * P : a * H + (s + 1) * P].bitcast(FP8X4),
+                            lambda a: wds[:, a * H + s * P : a * H + (s + 1) * P], h)
+            e = ringed([P, HALF], F32, "e")
+            nc.scalar.activation(e[:], acc_e[:], ACT.Tanh)
+            rec = ringed([P, HALF], F32, "rec")
+            nc.vector.tensor_tensor(rec[:], acc_d[:], e[:], ALU.mult)
+            return rec
+
+        def residual(s, h, rec):
+            acc_r = product("bank_r", lambda a: wrc[s][:, a * P : (a + 1) * P].bitcast(FP8X4),
+                            lambda a: wrs[s][:, a * P : (a + 1) * P], h)
+            res = ringed([P, HALF], F32, "res")
+            nc.vector.tensor_tensor(res[:], acc_r[:], rec[:], ALU.subtract)
+            return res
+
+        def scatter(s, h, res):
+            nc.vector.tensor_tensor(pages[s][:].indirect(half_of(idx2, h)), res[:], wgs_sb[:, h * HALF : (h + 1) * HALF], ALU.mult)
+
+        zt = [kept([P, 2, 2, P, 2], BF16, f"zt{c}") for c in range(CHUNKS)]
+
+        def negated_tol(s):
+            raw = staged(f"tol_raw{s}", [P, M], (s + 3) % 4)
+            nc.sync.dma_start(out=raw[:], in_=tol[s * P : (s + 1) * P, :])
+            neg = ringed([P, M], F32, "tol_neg")
+            nc.scalar.activation(neg[:], raw[:], ACT.Copy, scale=-1.0)
+            return neg
+
+        def excess(s, neg, m0, width):
+            x = ring.tile([P, width], F32, name="x", tag=f"x{width}", align_bytes=64)
+            nc.vector.tensor_copy(x[:], pages[s][:].indirect(idx3[:, m0 // 16 : (m0 + width) // 16]))
+            mag = ring.tile([P, width], F32, name="mag", tag=f"mag{width}", align_bytes=64)
+            nc.scalar.activation(mag[:], x[:], ACT.Abs)
+            for c0 in range(0, width, CHUNK):
+                c = (m0 + c0) // CHUNK
+                bank = psum.tile([P, HALF], F32, name="bank_t")
+                for i in range(2):
+                    lo = c0 + i * P
+                    nc.tensor.matmul(bank[:, i * P : (i + 1) * P], neg[:, m0 + lo : m0 + lo + P], ident[:], start=True, stop=False, is_transpose=True)
+                    nc.tensor.matmul(bank[:, i * P : (i + 1) * P], mag[:, lo : lo + P], ident[:], start=False, stop=True, is_transpose=True)
+                nc.scalar.copy(
+                    zt[c][:, :, :, 32 * s : 32 * (s + 1), :].rearrange("m i u p e -> m u i p e"),
+                    bank[:, 0 : 2 * P].rearrange("m (i p u e) -> m u i p e", i=2, u=2, e=2),
+                )
+
+        woc = kept([P, N], U32, "woc")
+        wos = kept([P, N], U8, "wos")
+
+        def quantize_wo():
+            raw = staged("wo_raw", [P, 4, N], 3)
+            nc.sync.dma_start(out=raw[:], in_=wo.rearrange("(p j) n -> p j n", j=4))
+            grouped = kept([P, 4, P, 4], BF16, "wo_grouped")
+            nc.scalar.copy(grouped[:].rearrange("p t c j -> p c j t"), raw[:].rearrange("p j (c t) -> p c j t", t=4))
+            nc.vector.quantize_mx(out=woc[:].bitcast(FP8X4), scales=wos[:], in_=grouped[:].rearrange("p t c j -> p (t c j)"))
+
+        yc = kept([P, M], U32, "yc")
+        ys = kept([P, M], U8, "ys")
+        out_rows = out_0.rearrange("(p t) m -> p t m", t=4)
+        out_words = out_1[0].rearrange("p m t -> p (m t)").bitcast(I32)
+
+        def scores(c):
+            cols = slice(c * CHUNK, (c + 1) * CHUNK)
+            words = zt[c][:].rearrange("m i u p e -> m (i u p e)").bitcast(F32)
+            bank = psum.tile([P, HALF], F32, name="bank_e")
+            for j in range(4):
+                nc.tensor.transpose(bank[:, j * P : (j + 1) * P], words[:, j * P : (j + 1) * P], ident[:])
+            z = ringed([P, CHUNK * 4], BF16, "z")
+            nc.scalar.copy(
+                z[:].bitcast(F32).rearrange("p (i m u) -> p i m u", i=2, u=2),
+                bank[:].rearrange("p (i u m) -> p i m u", i=2, u=2),
+            )
+            zc = ringed([P, CHUNK], U32, "zc")
+            zs = ringed([P, CHUNK], U8, "zs")
+            nc.vector.quantize_mx(out=zc[:].bitcast(FP8X4), scales=zs[:], in_=z[:])
+            y = ring.tile([P, 4, CHUNK], F32, name="y", bufs=3, align_bytes=64)
+            for pair, tag in enumerate(("bank_d", "bank_r")):
+                acc = psum.tile([P, HALF], F32, name=tag)
+                for i in range(2):
+                    t = 2 * pair + i
+                    nc.tensor.matmul_mx(
+                        out=acc[:, i * CHUNK : (i + 1) * CHUNK], lhsT=woc[:, t * P : (t + 1) * P].bitcast(FP8X4),
+                        lhsT_scale=wos[:, t * P : (t + 1) * P], rhs=zc[:].bitcast(FP8X4), rhs_scale=zs[:],
+                        start=True, stop=True,
+                    )
+                nc.scalar.copy(y[:, 2 * pair : 2 * pair + 2, :].rearrange("p t m -> p (t m)"), acc[:])
+            nc.sync.dma_start(out=out_rows[:, :, cols], in_=y[:])
+            grouped = ringed([P, CHUNK, 4], BF16, "y_grouped")
+            nc.vector.tensor_copy(grouped[:].rearrange("p (c i) t -> p c t i", i=4), y[:].rearrange("p t (c i) -> p c t i", i=4))
+            nc.vector.quantize_mx(out=yc[:, cols].bitcast(FP8X4), scales=ys[:, cols], in_=grouped[:].rearrange("p m t -> p (m t)"))
+            nc.sync.dma_start(out=out_words[:, cols], in_=yc[:, cols].bitcast(I32))
+
+        units = [(s, h) for s in range(PAGES) for h in range(2)]
+        rec = reconstruct(*units[0])
+        res = residual(*units[0], rec)
+        negs = []
+        for u, (s, h) in enumerate(units):
+            last = u + 1 == len(units)
+            if h == 0:
+                if s + 1 < PAGES:
+                    quantize_wr(s + 1)
+                else:
+                    quantize_wo()
+            if not last:
+                rec = reconstruct(*units[u + 1])
+            if s > 0:
+                excess(s - 1, negs[s - 1], h * HALF, HALF)
+            scatter(s, h, res)
+            if not last:
+                res = residual(*units[u + 1], rec)
+            if h == 1:
+                negs.append(negated_tol(s))
+        neg = negs[PAGES - 1]
+        for c in range(CHUNKS):
+            excess(PAGES - 1, neg, c * CHUNK, CHUNK)
+            if c > 0:
+                scores(c - 1)
+        scores(CHUNKS - 1)
+        for q in range(4):
+            nc.sync.dma_start(out=out_2[0, 4 * q : 4 * q + 4, :].bitcast(I32), in_=ys[32 * q : 32 * q + 4, :].bitcast(I32))

@@ -47,20 +47,26 @@ def tile_list_handshake_anomaly_scores_kernel(
         def ringed(shape, dtype, name):
             return ring.tile(shape, dtype, name=name, align_bytes=64)
 
-        tw = [kept([P, T], U32, "tw0"), reuse.tile([P, T], U32, name="tw1", offset=0, align_bytes=64)]
-        ts = kept([P, PASSES * T], U8, "ts")
+        def placed(shape, dtype, name, offset):
+            return reuse.tile(shape, dtype, name=name, offset=offset, align_bytes=64)
+
+        WDW_AT, TS_AT, TW1_AT = 0, 2048, 5120
+        WR0_AT = TW1_AT + 5 * 4096
+        RES_AT = WR0_AT + 4096
+        tw = [kept([P, T], U32, "tw0"), placed([P, T], U32, "tw1", TW1_AT)]
+        ts = placed([P, T], U8, "ts", TS_AT)
         wes = kept([P, PASSES * H], U8, "wes")
         wds = kept([P, PASSES * H], U8, "wds")
         wew = kept([P, PASSES * 2 * H], U8, "wew")
-        wdw = kept([P, PASSES * H], U32, "wdw")
-        wgs_sb = kept([P, S], F32, "wgs_sb")
+        wd_first = kept([P, PASSES, P], U32, "wd_first")
+        wd_rest = placed([P, PASSES, H - P], U32, "wd_rest", WDW_AT)
+        wgs_sb = placed([P, S], F32, "wgs_sb", WR0_AT)
         pages = [kept([P, T2], F32, f"page{a}") for a in range(PAGES)]
         ident = kept([P, P], F32, "ident")
 
-        nc.vector.memset(ts[:].bitcast(I32), 0)
+        nc.vector.memset(ts[32:64, :].bitcast(I32), 0)
+        nc.vector.memset(ts[64:P, :].bitcast(I32), 0)
         make_identity(nc, ident[:])
-        nc.gpsimd.memset(wes[:].bitcast(I32), 0)
-        nc.gpsimd.memset(wds[:].bitcast(I32), 0)
 
         def load_scales(tile, src, rows):
             for r in rows:
@@ -74,50 +80,44 @@ def tile_list_handshake_anomaly_scores_kernel(
             nc.sync.dma_start(out=tw[a][:, lo:hi].bitcast(I32), in_=words[:, lo:hi])
 
         def staged(name, shape, slot):
-            return reuse.tile(shape, F32, name=name, offset=4096 * slot, align_bytes=64)
+            return placed(shape, F32, name, TW1_AT + 4096 * slot)
 
         def load_wr(s, a, tile):
             nc.sync.dma_start(out=tile, in_=wr[512 * a : 512 * (a + 1), s * P : (s + 1) * P].rearrange("(p j) c -> p j c", j=4))
 
         nc.sync.dma_start(idx[:], offs)
+        nc.sync.dma_start(out=ts[0:32, :].bitcast(I32), in_=tab_scales.rearrange("a q t -> (a q) t").bitcast(I32))
+        load_scales(wes, we_scales, range(4))
         load_table(0, 0, T)
-        load_scales(ts, tab_scales, range(4))
-        wr_first = [kept([P, 4, P], F32, f"wr_first{a}") for a in range(PASSES)]
+        wr_first = [placed([P, 4, P], F32, f"wr_first{a}", WR0_AT + 2048 * a) for a in range(PASSES)]
         for a in range(PASSES):
             load_wr(0, a, wr_first[a][:])
         nc.sync.dma_start(
             out=wew[:].bitcast(I32).rearrange("p (a c) -> p a c", a=PASSES),
             in_=we_words.rearrange("a p c -> p a c").bitcast(I32),
         )
-        load_table(1, 0, T // 2)
-        load_scales(wes, we_scales, range(4))
-        load_scales(wds, wd_scales, range(2))
-        load_table(1, T // 2, T)
-        load_scales(wds, wd_scales, range(2, 4))
-        nc.sync.dma_start(
-            out=wdw[:].bitcast(I32).rearrange("p (a c) -> p a c", a=PASSES),
-            in_=wd_words.rearrange("a p c i -> p a (c i)").bitcast(I32),
-        )
-        nc.sync.dma_start(out=wgs_sb[:], in_=wgs)
-        nc.sync.dma_start(idx2[:], offs2)
-        nc.sync.dma_start(idx3[:], offs3)
-
-        for a in range(PAGES):
-            nc.vector.memset(pages[a][:], 0.0)
+        wd_all = wd_words.rearrange("a p c i -> p a (c i)").bitcast(I32)
+        nc.sync.dma_start(out=wd_first[:].bitcast(I32), in_=wd_all[:, :, 0:P])
+        load_scales(wds, wd_scales, range(3))
+        nc.vector.memset(pages[0][:], 0.0)
 
         vw = [[kept([P, HALF], U32, f"vw{a}{h}") for h in range(2)] for a in range(PASSES)]
-        vs = [[kept([P, HALF], U8, f"vs{a}{h}") for h in range(2)] for a in range(PASSES)]
+        vs = [kept([P, S], U8, f"vs{a}") for a in range(PASSES)]
 
         def half_of(lst, h):
             return lst[:, h * (HALF // 16) : (h + 1) * (HALF // 16)]
 
-        def gather_scales(a, h):
-            nc.vector.tensor_copy(vs[a][h][:], ts[:, a * T : (a + 1) * T].indirect(half_of(idx, h)))
+        picked = kept([P, S], U8, "picked")
+
+        def move_scales(rows):
+            for a, r in rows:
+                nc.sync.dma_start(out=vs[a][r:P:32, :].bitcast(I32), in_=picked[16 * a + r : 16 * (a + 1) : 4, :].bitcast(I32))
 
         def gather_words(a, h):
             nc.vector.tensor_copy(vw[a][h][:], tw[a][:].indirect(half_of(idx, h)))
 
-        wrc = [kept([P, PASSES * P], U32, f"wrc{s}") for s in range(PAGES)]
+        wrc = [kept([P, PASSES * P], U32, "wrc0")]
+        wrc.extend(placed([P, PASSES * P], U32, f"wrc{s}", RES_AT + 2048 * (s - 1)) for s in range(1, PAGES))
         wrs = [kept([P, PASSES * P], U8, f"wrs{s}") for s in range(PAGES)]
 
         def quantize_wr(s):
@@ -138,22 +138,31 @@ def tile_list_handshake_anomaly_scores_kernel(
                 )
             nc.vector.quantize_mx(out=wrc[s][:].bitcast(FP8X4), scales=wrs[s][:], in_=grouped[:].rearrange("p a c j -> p (a c j)"))
 
-        gather_scales(0, 0)
-        gather_scales(1, 0)
+        nc.vector.tensor_copy(picked[:], ts[:].indirect(idx[:]))
+        rows = [(a, r) for a in range(PASSES) for r in range(4)]
+        load_table(1, 0, T // 2)
+        load_scales(wds, wd_scales, range(3, 4))
+        move_scales(rows[:5])
+        load_table(1, T // 2, T)
+        move_scales(rows[5:])
+        nc.sync.dma_start(idx2[:], offs2)
         gather_words(0, 0)
-        gather_scales(0, 1)
-        gather_scales(1, 1)
-        quantize_wr(0)
-        gather_words(1, 0)
         gather_words(0, 1)
+        quantize_wr(0)
+        nc.sync.dma_start(out=wgs_sb[:], in_=wgs)
+        nc.sync.dma_start(out=wd_rest[:].bitcast(I32), in_=wd_all[:, :, P:H])
+        nc.sync.dma_start(idx3[:], offs3)
+        gather_words(1, 0)
         gather_words(1, 1)
+        for a in range(1, PAGES):
+            nc.vector.memset(pages[a][:], 0.0)
 
         def product(tag, codes_of, scale_of, h):
             acc = psum.tile([P, HALF], F32, name=tag)
             for a in range(PASSES):
                 nc.tensor.matmul_mx(
                     out=acc[:], lhsT=codes_of(a), lhsT_scale=scale_of(a),
-                    rhs=vw[a][h][:].bitcast(FP8X4), rhs_scale=vs[a][h][:],
+                    rhs=vw[a][h][:].bitcast(FP8X4), rhs_scale=vs[a][:, h * HALF : (h + 1) * HALF],
                     start=(a == 0), stop=(a == PASSES - 1),
                 )
             return acc
@@ -161,18 +170,24 @@ def tile_list_handshake_anomaly_scores_kernel(
         def reconstruct(s, h):
             acc_e = product("bank_e", lambda a: wew[:, 2 * (a * H + s * P) : 2 * (a * H + (s + 1) * P)].bitcast(FP4X4),
                             lambda a: wes[:, a * H + s * P : a * H + (s + 1) * P], h)
-            acc_d = product("bank_d", lambda a: wdw[:, a * H + s * P : a * H + (s + 1) * P].bitcast(FP8X4),
+            acc_d = product("bank_d", lambda a: (wd_first[:, a] if s == 0 else wd_rest[:, a, (s - 1) * P : s * P]).bitcast(FP8X4),
                             lambda a: wds[:, a * H + s * P : a * H + (s + 1) * P], h)
             e = ringed([P, HALF], F32, "e")
             nc.scalar.activation(e[:], acc_e[:], ACT.Tanh)
-            rec = ringed([P, HALF], F32, "rec")
+            if (s, h) == (0, 1):
+                rec = placed([P, HALF], F32, "rec01", RES_AT)
+            else:
+                rec = ringed([P, HALF], F32, "rec")
             nc.vector.tensor_tensor(rec[:], acc_d[:], e[:], ALU.mult)
             return rec
 
         def residual(s, h, rec):
             acc_r = product("bank_r", lambda a: wrc[s][:, a * P : (a + 1) * P].bitcast(FP8X4),
                             lambda a: wrs[s][:, a * P : (a + 1) * P], h)
-            res = ringed([P, HALF], F32, "res")
+            if h == 0 and s + 1 < PAGES:
+                res = placed([P, HALF], F32, f"res{s}", RES_AT + 2048 * s)
+            else:
+                res = ringed([P, HALF], F32, "res")
             nc.vector.tensor_tensor(res[:], acc_r[:], rec[:], ALU.subtract)
             return res
 
@@ -196,10 +211,13 @@ def tile_list_handshake_anomaly_scores_kernel(
             for c0 in range(0, width, CHUNK):
                 c = (m0 + c0) // CHUNK
                 bank = psum.tile([P, HALF], F32, name="bank_t")
-                for i in range(2):
-                    lo = c0 + i * P
-                    nc.tensor.matmul(bank[:, i * P : (i + 1) * P], neg[:, m0 + lo : m0 + lo + P], ident[:], start=True, stop=False, is_transpose=True)
-                    nc.tensor.matmul(bank[:, i * P : (i + 1) * P], mag[:, lo : lo + P], ident[:], start=False, stop=True, is_transpose=True)
+                terms = [neg[:, m0 + c0 : m0 + c0 + CHUNK], mag[:, c0 : c0 + CHUNK]]
+                for n, term in enumerate(terms):
+                    for i in range(2):
+                        nc.tensor.matmul(
+                            bank[:, i * P : (i + 1) * P], term[:, i * P : (i + 1) * P], ident[:],
+                            start=(n == 0 and i == 0), stop=(n == 1 and i == 1), is_transpose=True,
+                        )
                 nc.scalar.copy(
                     zt[c][:, :, :, 32 * s : 32 * (s + 1), :].rearrange("m i u p e -> m u i p e"),
                     bank[:, 0 : 2 * P].rearrange("m (i p u e) -> m u i p e", i=2, u=2, e=2),
@@ -220,33 +238,37 @@ def tile_list_handshake_anomaly_scores_kernel(
         out_rows = out_0.rearrange("(p t) m -> p t m", t=4)
         out_words = out_1[0].rearrange("p m t -> p (m t)").bitcast(I32)
 
-        def scores(c):
-            cols = slice(c * CHUNK, (c + 1) * CHUNK)
+        def quantize_z(c):
             words = zt[c][:].rearrange("m i u p e -> m (i u p e)").bitcast(F32)
             bank = psum.tile([P, HALF], F32, name="bank_e")
             for j in range(4):
                 nc.tensor.transpose(bank[:, j * P : (j + 1) * P], words[:, j * P : (j + 1) * P], ident[:])
             z = ringed([P, CHUNK * 4], BF16, "z")
-            nc.scalar.copy(
+            (nc.scalar.copy if c % 2 == 0 else nc.vector.tensor_copy)(
                 z[:].bitcast(F32).rearrange("p (i m u) -> p i m u", i=2, u=2),
                 bank[:].rearrange("p (i u m) -> p i m u", i=2, u=2),
             )
             zc = ringed([P, CHUNK], U32, "zc")
             zs = ringed([P, CHUNK], U8, "zs")
             nc.vector.quantize_mx(out=zc[:].bitcast(FP8X4), scales=zs[:], in_=z[:])
-            y = ring.tile([P, 4, CHUNK], F32, name="y", bufs=3, align_bytes=64)
-            for pair, tag in enumerate(("bank_d", "bank_r")):
+            return zc, zs
+
+        def scores(zc, zs, m0, lo, width):
+            cols = slice(m0 + lo, m0 + lo + width)
+            y = ring.tile([P, 4, width], F32, name="y", bufs=3, align_bytes=64)
+            per_bank = HALF // width
+            for first, tag in zip(range(0, 4, per_bank), ("bank_d", "bank_r")):
                 acc = psum.tile([P, HALF], F32, name=tag)
-                for i in range(2):
-                    t = 2 * pair + i
+                for i in range(per_bank):
+                    t = first + i
                     nc.tensor.matmul_mx(
-                        out=acc[:, i * CHUNK : (i + 1) * CHUNK], lhsT=woc[:, t * P : (t + 1) * P].bitcast(FP8X4),
-                        lhsT_scale=wos[:, t * P : (t + 1) * P], rhs=zc[:].bitcast(FP8X4), rhs_scale=zs[:],
-                        start=True, stop=True,
+                        out=acc[:, i * width : (i + 1) * width], lhsT=woc[:, t * P : (t + 1) * P].bitcast(FP8X4),
+                        lhsT_scale=wos[:, t * P : (t + 1) * P], rhs=zc[:, lo : lo + width].bitcast(FP8X4),
+                        rhs_scale=zs[:, lo : lo + width], start=True, stop=True,
                     )
-                nc.scalar.copy(y[:, 2 * pair : 2 * pair + 2, :].rearrange("p t m -> p (t m)"), acc[:])
+                nc.scalar.copy(y[:, first : first + per_bank, :].rearrange("p t m -> p (t m)"), acc[:])
             nc.sync.dma_start(out=out_rows[:, :, cols], in_=y[:])
-            grouped = ringed([P, CHUNK, 4], BF16, "y_grouped")
+            grouped = ringed([P, width, 4], BF16, "y_grouped")
             nc.vector.tensor_copy(grouped[:].rearrange("p (c i) t -> p c t i", i=4), y[:].rearrange("p t (c i) -> p c t i", i=4))
             nc.vector.quantize_mx(out=yc[:, cols].bitcast(FP8X4), scales=ys[:, cols], in_=grouped[:].rearrange("p m t -> p (m t)"))
             nc.sync.dma_start(out=out_words[:, cols], in_=yc[:, cols].bitcast(I32))
@@ -257,16 +279,19 @@ def tile_list_handshake_anomaly_scores_kernel(
         negs = []
         for u, (s, h) in enumerate(units):
             last = u + 1 == len(units)
+            if u == 0:
+                scatter(s, h, res)
+            if not last:
+                rec = reconstruct(*units[u + 1])
+            if s > 0:
+                excess(s - 1, negs[s - 1], h * HALF, HALF)
+            if u > 0:
+                scatter(s, h, res)
             if h == 0:
                 if s + 1 < PAGES:
                     quantize_wr(s + 1)
                 else:
                     quantize_wo()
-            if not last:
-                rec = reconstruct(*units[u + 1])
-            if s > 0:
-                excess(s - 1, negs[s - 1], h * HALF, HALF)
-            scatter(s, h, res)
             if not last:
                 res = residual(*units[u + 1], rec)
             if h == 1:
@@ -275,7 +300,9 @@ def tile_list_handshake_anomaly_scores_kernel(
         for c in range(CHUNKS):
             excess(PAGES - 1, neg, c * CHUNK, CHUNK)
             if c > 0:
-                scores(c - 1)
-        scores(CHUNKS - 1)
+                scores(*quantize_z(c - 1), (c - 1) * CHUNK, 0, CHUNK)
+        zc, zs = quantize_z(CHUNKS - 1)
+        for lo in range(0, CHUNK, P):
+            scores(zc, zs, M - CHUNK, lo, P)
         for q in range(4):
             nc.sync.dma_start(out=out_2[0, 4 * q : 4 * q + 4, :].bitcast(I32), in_=ys[32 * q : 32 * q + 4, :].bitcast(I32))

@@ -50,18 +50,22 @@ def tile_list_handshake_anomaly_scores_kernel(
         def placed(shape, dtype, name, offset):
             return reuse.tile(shape, dtype, name=name, offset=offset, align_bytes=64)
 
-        WDW_AT, TS_AT, TW1_AT = 0, 2048, 5120
-        WR0_AT = TW1_AT + 5 * 4096
-        RES_AT = WR0_AT + 4096
-        tw = [kept([P, T], U32, "tw0"), placed([P, T], U32, "tw1", TW1_AT)]
+        PAGE1_AT, TS_AT, TW1_AT = 0, 7168, 10240
+        WGS_AT = TW1_AT + 5 * 4096
+        WR0_AT = WGS_AT + 3072
+        WDW_AT = WR0_AT + 3072
+        RES_AT = WDW_AT + 3072
+        TW0_AT = RES_AT + 3 * 2048
+        tw = [placed([P, T], U32, "tw0", TW0_AT), placed([P, T], U32, "tw1", TW1_AT)]
         ts = placed([P, T], U8, "ts", TS_AT)
         wes = kept([P, PASSES * H], U8, "wes")
         wds = kept([P, PASSES * H], U8, "wds")
         wew = kept([P, PASSES * 2 * H], U8, "wew")
         wd_first = kept([P, PASSES, P], U32, "wd_first")
         wd_rest = placed([P, PASSES, H - P], U32, "wd_rest", WDW_AT)
-        wgs_sb = placed([P, S], F32, "wgs_sb", WR0_AT)
-        pages = [kept([P, T2], F32, f"page{a}") for a in range(PAGES)]
+        wgs_sb = placed([P, S], F32, "wgs_sb", WGS_AT)
+        pages = [kept([P, T2], F32, "page0")]
+        pages.extend(placed([P, T2], F32, f"page{a + 1}", at) for a, at in enumerate((PAGE1_AT, TW0_AT, TW0_AT + 8192)))
         ident = kept([P, P], F32, "ident")
 
         nc.vector.memset(ts[32:64, :].bitcast(I32), 0)
@@ -132,8 +136,8 @@ def tile_list_handshake_anomaly_scores_kernel(
             for a in range(PASSES):
                 raw = raws[a]
                 nc.scalar.activation(
-                    grouped[:, a].rearrange("p (c i) j -> p c j i", i=4),
-                    raw.rearrange("p j (c i) -> p c j i", i=4),
+                    grouped[:, a],
+                    raw.rearrange("p j c -> p c j"),
                     ACT.Copy,
                 )
             nc.vector.quantize_mx(out=wrc[s][:].bitcast(FP8X4), scales=wrs[s][:], in_=grouped[:].rearrange("p a c j -> p (a c j)"))
@@ -230,7 +234,8 @@ def tile_list_handshake_anomaly_scores_kernel(
             raw = staged("wo_raw", [P, 4, N], 3)
             nc.sync.dma_start(out=raw[:], in_=wo.rearrange("(p j) n -> p j n", j=4))
             grouped = kept([P, 4, P, 4], BF16, "wo_grouped")
-            nc.scalar.copy(grouped[:].rearrange("p t c j -> p c j t"), raw[:].rearrange("p j (c t) -> p c j t", t=4))
+            for t in range(4):
+                nc.scalar.copy(grouped[:, t], raw[:].rearrange("p j (c t) -> p t c j", t=4)[:, t])
             nc.vector.quantize_mx(out=woc[:].bitcast(FP8X4), scales=wos[:], in_=grouped[:].rearrange("p t c j -> p (t c j)"))
 
         yc = kept([P, M], U32, "yc")
@@ -269,7 +274,7 @@ def tile_list_handshake_anomaly_scores_kernel(
                 nc.scalar.copy(y[:, first : first + per_bank, :].rearrange("p t m -> p (t m)"), acc[:])
             nc.sync.dma_start(out=out_rows[:, :, cols], in_=y[:])
             grouped = ringed([P, width, 4], BF16, "y_grouped")
-            nc.vector.tensor_copy(grouped[:].rearrange("p (c i) t -> p c t i", i=4), y[:].rearrange("p t (c i) -> p c t i", i=4))
+            nc.vector.tensor_copy(grouped[:], y[:].rearrange("p t m -> p m t"))
             nc.vector.quantize_mx(out=yc[:, cols].bitcast(FP8X4), scales=ys[:, cols], in_=grouped[:].rearrange("p m t -> p (m t)"))
             nc.sync.dma_start(out=out_words[:, cols], in_=yc[:, cols].bitcast(I32))
 

@@ -23,6 +23,8 @@ PAGES = H // P
 HALF = 512
 CHUNK = 256
 CHUNKS = M // CHUNK
+STAGE = 96
+WE_AT, WD_AT, PLANE = S, S + H, S + 2 * H
 
 
 def tile_list_handshake_anomaly_scores_kernel(
@@ -35,7 +37,7 @@ def tile_list_handshake_anomaly_scores_kernel(
         keep = ctx.enter_context(tc.tile_pool(name="keep", bufs=1))
         ring = ctx.enter_context(tc.tile_pool(name="ring", bufs=2))
         reuse = ctx.enter_context(tc.tile_pool(name="reuse", bufs=1))
-        psum = ctx.enter_context(tc.psum_pool(name="psum", bufs=2))
+        psum = ctx.enter_context(tc.psum_pool(name="psum", bufs=1))
 
         idx = lists.tile([P, S // 16], U16, name="idx")
         idx2 = lists.tile([P, S // 16], U16, name="idx2")
@@ -44,198 +46,218 @@ def tile_list_handshake_anomaly_scores_kernel(
         def kept(shape, dtype, name):
             return keep.tile(shape, dtype, name=name, align_bytes=64)
 
-        def ringed(shape, dtype, name):
-            return ring.tile(shape, dtype, name=name, align_bytes=64)
+        def ringed(shape, dtype, name, bufs=2):
+            return ring.tile(shape, dtype, name=name, bufs=bufs, align_bytes=64)
 
         def placed(shape, dtype, name, offset):
             return reuse.tile(shape, dtype, name=name, offset=offset, align_bytes=64)
 
-        PAGE1_AT, TS_AT, TW1_AT = 0, 7168, 10240
-        WGS_AT = TW1_AT + 5 * 4096
-        WR0_AT = WGS_AT + 3072
-        WDW_AT = WR0_AT + 3072
-        RES_AT = WDW_AT + 3072
-        TW0_AT = RES_AT + 3 * 2048
+        def bank_tile(name, bank):
+            return psum.tile([P, HALF], F32, name=name, offset=2048 * bank)
+
+        PAGE2_AT = 0
+        TW0_AT = PAGE2_AT + 8192 - 512
+        WR0_AT = TW0_AT + 512
+        WGS_AT = WR0_AT + 4096
+        WR1_AT = WGS_AT + 4096
+        PAGE3_AT = WR1_AT + 4096
+        TW1_AT = PAGE3_AT + 8192
+        SWAP_AT = TW1_AT
+        PICKED_AT = TW1_AT + 16384 - 512
+        PAGE1_AT = PICKED_AT + 512
+        WR2_AT = PAGE1_AT + 8192
+        STAGED_AT = WR2_AT + 3072
+        WO_AT = WR2_AT + 8192
+        TOL0_AT = WO_AT + 8192
+        WD_WORDS_AT = TOL0_AT - 1024
+        TOL1_AT = TOL0_AT + 4096
+        WE_WORDS_AT = TOL1_AT + 3072
         tw = [placed([P, T], U32, "tw0", TW0_AT), placed([P, T], U32, "tw1", TW1_AT)]
-        ts = placed([P, T], U8, "ts", TS_AT)
-        wes = kept([P, PASSES * H], U8, "wes")
-        wds = kept([P, PASSES * H], U8, "wds")
-        wew = kept([P, PASSES * 2 * H], U8, "wew")
-        wd_first = kept([P, PASSES, P], U32, "wd_first")
-        wd_rest = placed([P, PASSES, H - P], U32, "wd_rest", WDW_AT)
-        wgs_sb = placed([P, S], F32, "wgs_sb", WGS_AT)
+        ts = kept([P, T], U8, "ts")
+        staged = placed([P, PLANE], U8, "staged", STAGED_AT)
+        wew = placed([P, PASSES * 2 * H], U8, "wew", WE_WORDS_AT)
+        wdw = placed([P, PASSES, H], U32, "wdw", WD_WORDS_AT)
         pages = [kept([P, T2], F32, "page0")]
-        pages.extend(placed([P, T2], F32, f"page{a + 1}", at) for a, at in enumerate((PAGE1_AT, TW0_AT, TW0_AT + 8192)))
+        pages.extend(placed([P, T2], F32, f"page{s + 1}", at) for s, at in enumerate((PAGE1_AT, PAGE2_AT, PAGE3_AT)))
         ident = kept([P, P], F32, "ident")
 
-        nc.vector.memset(ts[32:64, :].bitcast(I32), 0)
-        nc.vector.memset(ts[64:P, :].bitcast(I32), 0)
+        nc.vector.memset(ts[0:STAGE, :].bitcast(I32), 0)
         make_identity(nc, ident[:])
+        nc.vector.memset(pages[0][:], 0.0)
 
-        def load_scales(tile, src, rows):
-            for r in rows:
-                nc.sync.dma_start(
-                    out=tile[r:P:32, :].bitcast(I32).rearrange("p (a c) -> p a c", a=PASSES),
-                    in_=src[:, r:16:4, :].rearrange("a q c -> q a c").bitcast(I32),
-                )
+        def stage_rows(dst, src):
+            nc.sync.dma_start(out=dst.bitcast(I32), in_=src.rearrange("a q c -> (a q) c").bitcast(I32))
 
-        def load_table(a, lo, hi):
-            words = tab_words[a].rearrange("p t i -> p (t i)").bitcast(I32)
-            nc.sync.dma_start(out=tw[a][:, lo:hi].bitcast(I32), in_=words[:, lo:hi])
+        def load_table(a):
+            nc.sync.dma_start(out=tw[a][:].bitcast(I32), in_=tab_words[a].rearrange("p t i -> p (t i)").bitcast(I32))
 
-        def staged(name, shape, slot):
-            return placed(shape, F32, name, TW1_AT + 4096 * slot)
-
-        def load_wr(s, a, tile):
-            nc.sync.dma_start(out=tile, in_=wr[512 * a : 512 * (a + 1), s * P : (s + 1) * P].rearrange("(p j) c -> p j c", j=4))
+        def load_wr(tile, a, lo, hi):
+            nc.sync.dma_start(out=tile[:], in_=wr[512 * a : 512 * (a + 1), lo:hi].rearrange("(p j) c -> p j c", j=4))
 
         nc.sync.dma_start(idx[:], offs)
-        nc.sync.dma_start(out=ts[0:32, :].bitcast(I32), in_=tab_scales.rearrange("a q t -> (a q) t").bitcast(I32))
-        load_scales(wes, we_scales, range(4))
-        load_table(0, 0, T)
-        wr_first = [placed([P, 4, P], F32, f"wr_first{a}", WR0_AT + 2048 * a) for a in range(PASSES)]
-        for a in range(PASSES):
-            load_wr(0, a, wr_first[a][:])
+        stage_rows(ts[STAGE:P, :], tab_scales)
+        stage_rows(staged[STAGE:P, WE_AT:WD_AT], we_scales)
+        stage_rows(staged[STAGE:P, WD_AT:PLANE], wd_scales)
+        nc.sync.dma_start(idx2[:], offs2)
+        nc.sync.dma_start(idx3[:], offs3)
+        load_table(0)
         nc.sync.dma_start(
             out=wew[:].bitcast(I32).rearrange("p (a c) -> p a c", a=PASSES),
             in_=we_words.rearrange("a p c -> p a c").bitcast(I32),
         )
-        wd_all = wd_words.rearrange("a p c i -> p a (c i)").bitcast(I32)
-        nc.sync.dma_start(out=wd_first[:].bitcast(I32), in_=wd_all[:, :, 0:P])
-        load_scales(wds, wd_scales, range(3))
-        nc.vector.memset(pages[0][:], 0.0)
+        nc.sync.dma_start(out=wdw[:].bitcast(I32), in_=wd_words.rearrange("a p c i -> p a (c i)").bitcast(I32))
 
         vw = [[kept([P, HALF], U32, f"vw{a}{h}") for h in range(2)] for a in range(PASSES)]
-        vs = [kept([P, S], U8, f"vs{a}") for a in range(PASSES)]
+        planes = [kept([P, PLANE], U8, f"plane{a}") for a in range(PASSES)]
+        picked = placed([P, S], U8, "picked", PICKED_AT)
 
         def half_of(lst, h):
             return lst[:, h * (HALF // 16) : (h + 1) * (HALF // 16)]
 
-        picked = kept([P, S], U8, "picked")
-
-        def move_scales(rows):
-            for a, r in rows:
-                nc.sync.dma_start(out=vs[a][r:P:32, :].bitcast(I32), in_=picked[16 * a + r : 16 * (a + 1) : 4, :].bitcast(I32))
-
         def gather_words(a, h):
             nc.vector.tensor_copy(vw[a][h][:], tw[a][:].indirect(half_of(idx, h)))
 
-        wrc = [kept([P, PASSES * P], U32, "wrc0")]
-        wrc.extend(placed([P, PASSES * P], U32, f"wrc{s}", RES_AT + 2048 * (s - 1)) for s in range(1, PAGES))
+        nc.vector.tensor_copy(picked[:], ts[:].indirect(idx[:]))
+        nc.vector.tensor_copy(staged[STAGE:P, 0:S].bitcast(I32), picked[STAGE:P, :].bitcast(I32))
+
+        def move_scales(a):
+            for r in range(4):
+                rows = staged[STAGE + 16 * a + r : STAGE + 16 * (a + 1) : 4, :]
+                nc.sync.dma_start(out=planes[a][r:P:32, :].bitcast(I32), in_=rows.bitcast(I32))
+
+        move_scales(0)
+        load_table(1)
+        move_scales(1)
+        nc.vector.memset(pages[1][:], 0.0)
+
+        wrc = [kept([P, PASSES * P], U32, f"wrc{s}") for s in range(PAGES)]
         wrs = [kept([P, PASSES * P], U8, f"wrs{s}") for s in range(PAGES)]
 
-        def quantize_wr(s):
+        def quantize_wr(s, raws, copy):
             grouped = ringed([P, PASSES, P, 4], BF16, "wr_grouped")
-            if s == 0:
-                raws = [tile[:] for tile in wr_first]
-            else:
-                both = staged(f"wr_raw{s}", [P, PASSES, 4, P], s - 1)
-                raws = [both[:, a] for a in range(PASSES)]
-                for a in range(PASSES):
-                    load_wr(s, a, raws[a])
             for a in range(PASSES):
-                raw = raws[a]
-                nc.scalar.activation(
-                    grouped[:, a],
-                    raw.rearrange("p j c -> p c j"),
-                    ACT.Copy,
-                )
+                copy(grouped[:, a], raws[a].rearrange("p j c -> p c j"))
             nc.vector.quantize_mx(out=wrc[s][:].bitcast(FP8X4), scales=wrs[s][:], in_=grouped[:].rearrange("p a c j -> p (a c j)"))
 
-        nc.vector.tensor_copy(picked[:], ts[:].indirect(idx[:]))
-        rows = [(a, r) for a in range(PASSES) for r in range(4)]
-        load_table(1, 0, T // 2)
-        load_scales(wds, wd_scales, range(3, 4))
-        move_scales(rows[:5])
-        load_table(1, T // 2, T)
-        move_scales(rows[5:])
-        nc.sync.dma_start(idx2[:], offs2)
         gather_words(0, 0)
         gather_words(0, 1)
-        quantize_wr(0)
+        wr_first = [placed([P, 4, P], F32, f"wr_first{a}", WR0_AT + 2048 * a) for a in range(PASSES)]
+        for a in range(PASSES):
+            load_wr(wr_first[a], a, 0, P)
+        wgs_sb = placed([P, S], F32, "wgs_sb", WGS_AT)
         nc.sync.dma_start(out=wgs_sb[:], in_=wgs)
-        nc.sync.dma_start(out=wd_rest[:].bitcast(I32), in_=wd_all[:, :, P:H])
-        nc.sync.dma_start(idx3[:], offs3)
+        wr_second = [placed([P, 4, P], F32, f"wr_second{a}", WR1_AT + 2048 * a) for a in range(PASSES)]
+        for a in range(PASSES):
+            load_wr(wr_second[a], a, P, 2 * P)
+        for page in pages[2:]:
+            nc.vector.memset(page[:], 0.0)
         gather_words(1, 0)
         gather_words(1, 1)
-        for a in range(1, PAGES):
-            nc.vector.memset(pages[a][:], 0.0)
+        quantize_wr(0, [tile[:] for tile in wr_first], nc.vector.tensor_copy)
+        wr_rest = [placed([P, 4, 2 * P], F32, f"wr_rest{a}", WR2_AT + 4096 * a) for a in range(PASSES)]
+        for a in range(PASSES):
+            load_wr(wr_rest[a], a, 2 * P, H)
+        tol_raw = []
 
-        def product(tag, codes_of, scale_of, h):
-            acc = psum.tile([P, HALF], F32, name=tag)
+        def load_tol(s):
+            tol_raw.append(placed([P, M], F32, f"tol_raw{s}", (TOL0_AT, TOL1_AT, TOL1_AT + 4096, WR2_AT + 4096)[s]))
+            nc.sync.dma_start(out=tol_raw[s][:], in_=tol[s * P : (s + 1) * P, :])
+
+        def product(out, jt, codes_of, scale_of):
+            h, lo = divmod(jt * P, HALF)
             for a in range(PASSES):
                 nc.tensor.matmul_mx(
-                    out=acc[:], lhsT=codes_of(a), lhsT_scale=scale_of(a),
-                    rhs=vw[a][h][:].bitcast(FP8X4), rhs_scale=vs[a][:, h * HALF : (h + 1) * HALF],
-                    start=(a == 0), stop=(a == PASSES - 1),
+                    out=out, lhsT=vw[a][h][:, lo : lo + P].bitcast(FP8X4), lhsT_scale=planes[a][:, jt * P : (jt + 1) * P],
+                    rhs=codes_of(a), rhs_scale=scale_of(a), start=(a == 0), stop=(a == PASSES - 1),
                 )
-            return acc
 
-        def reconstruct(s, h):
-            acc_e = product("bank_e", lambda a: wew[:, 2 * (a * H + s * P) : 2 * (a * H + (s + 1) * P)].bitcast(FP4X4),
-                            lambda a: wes[:, a * H + s * P : a * H + (s + 1) * P], h)
-            acc_d = product("bank_d", lambda a: (wd_first[:, a] if s == 0 else wd_rest[:, a, (s - 1) * P : s * P]).bitcast(FP8X4),
-                            lambda a: wds[:, a * H + s * P : a * H + (s + 1) * P], h)
-            e = ringed([P, HALF], F32, "e")
-            nc.scalar.activation(e[:], acc_e[:], ACT.Tanh)
-            if (s, h) == (0, 1):
-                rec = placed([P, HALF], F32, "rec01", RES_AT)
-            else:
-                rec = ringed([P, HALF], F32, "rec")
-            nc.vector.tensor_tensor(rec[:], acc_d[:], e[:], ALU.mult)
-            return rec
+        def add_turned(bank, blocks, start, stop):
+            for i, block in enumerate(blocks):
+                nc.tensor.matmul(bank[:, i * P : (i + 1) * P], block, ident[:], start=(start and i == 0),
+                                 stop=(stop and i == len(blocks) - 1), is_transpose=True)
 
-        def residual(s, h, rec):
-            acc_r = product("bank_r", lambda a: wrc[s][:, a * P : (a + 1) * P].bitcast(FP8X4),
-                            lambda a: wrs[s][:, a * P : (a + 1) * P], h)
-            if h == 0 and s + 1 < PAGES:
-                res = placed([P, HALF], F32, f"res{s}", RES_AT + 2048 * s)
-            else:
-                res = ringed([P, HALF], F32, "res")
-            nc.vector.tensor_tensor(res[:], acc_r[:], rec[:], ALU.subtract)
-            return res
+        recs = [kept([P, H], F32, f"rec{jt}") for jt in range(S // P)]
 
-        def scatter(s, h, res):
-            nc.vector.tensor_tensor(pages[s][:].indirect(half_of(idx2, h)), res[:], wgs_sb[:, h * HALF : (h + 1) * HALF], ALU.mult)
+        def reconstruct(jt, bank_e, bank_d):
+            acc_e = bank_tile(f"acc_e{jt}", bank_e)
+            product(acc_e[:], jt, lambda a: wew[:, 2 * a * H : 2 * (a + 1) * H].bitcast(FP4X4), lambda a: planes[a][:, WE_AT:WD_AT])
+            acc_d = bank_tile(f"acc_d{jt}", bank_d)
+            product(acc_d[:], jt, lambda a: wdw[:, a].bitcast(FP8X4), lambda a: planes[a][:, WD_AT:PLANE])
+            e = ringed([P, H], F32, "e", bufs=4)
+            nc.scalar.activation(e[:], acc_e[:], ACT.Tanh, scale=-1.0)
+            nc.vector.tensor_tensor(recs[jt][:], acc_d[:], e[:], ALU.mult)
+
+        units = [(0, 0), (1, 0), (0, 1), (2, 0), (1, 1), (3, 0), (2, 1), (3, 1)]
+
+        def residual(u, parts=1):
+            s, h = units[u]
+            feat_bank, sum_bank = (1, 6) if u % 2 else (0, 2)
+            acc = bank_tile(f"acc_r{u}", feat_bank)
+            for i in range(4):
+                product(acc[:, i * P : (i + 1) * P], 4 * h + i, lambda a: wrc[s][:, a * P : (a + 1) * P].bitcast(FP8X4),
+                        lambda a: wrs[s][:, a * P : (a + 1) * P])
+            feat = placed([P, HALF], F32, f"feat{u}", SWAP_AT + 2048 * u)
+            nc.scalar.copy(feat[:], acc[:])
+            out = []
+            for part in range(parts):
+                blocks = range(part * 4 // parts, (part + 1) * 4 // parts)
+                bank = bank_tile(f"acc_h{u}_{part}", sum_bank + 2 * part)
+                add_turned(bank, [feat[:, i * P : (i + 1) * P] for i in blocks], True, False)
+                add_turned(bank, [recs[4 * h + i][:, s * P : (s + 1) * P] for i in blocks], False, True)
+                width = HALF // parts
+                res = ring.tile([P, width], F32, name="res", tag=f"res{width}", bufs=7 if parts == 1 else 2, align_bytes=64)
+                nc.scalar.copy(res[:], bank[:, 0:width])
+                out.append((h * HALF + part * width, res))
+            return out
+
+        def scatter(s, parts):
+            for lo, res in parts:
+                hi = lo + res.shape[1]
+                nc.vector.tensor_tensor(pages[s][:].indirect(idx2[:, lo // 16 : hi // 16]), res[:], wgs_sb[:, lo:hi], ALU.mult)
 
         zt = [kept([P, 2, 2, P, 2], BF16, f"zt{c}") for c in range(CHUNKS)]
 
-        def negated_tol(s):
-            raw = staged(f"tol_raw{s}", [P, M], (s + 3) % 4)
-            nc.sync.dma_start(out=raw[:], in_=tol[s * P : (s + 1) * P, :])
-            neg = ringed([P, M], F32, "tol_neg")
-            nc.scalar.activation(neg[:], raw[:], ACT.Copy, scale=-1.0)
+        def negated_tol(s, h):
+            neg = ringed([P, HALF], F32, "tol_neg", bufs=8)
+            nc.scalar.activation(neg[:], tol_raw[s][:, h * HALF : (h + 1) * HALF], ACT.Copy, scale=-1.0)
             return neg
 
-        def excess(s, neg, m0, width):
-            x = ring.tile([P, width], F32, name="x", tag=f"x{width}", align_bytes=64)
-            nc.vector.tensor_copy(x[:], pages[s][:].indirect(idx3[:, m0 // 16 : (m0 + width) // 16]))
-            mag = ring.tile([P, width], F32, name="mag", tag=f"mag{width}", align_bytes=64)
-            nc.scalar.activation(mag[:], x[:], ACT.Abs)
-            for c0 in range(0, width, CHUNK):
-                c = (m0 + c0) // CHUNK
-                bank = psum.tile([P, HALF], F32, name="bank_t")
-                terms = [neg[:, m0 + c0 : m0 + c0 + CHUNK], mag[:, c0 : c0 + CHUNK]]
-                for n, term in enumerate(terms):
-                    for i in range(2):
-                        nc.tensor.matmul(
-                            bank[:, i * P : (i + 1) * P], term[:, i * P : (i + 1) * P], ident[:],
-                            start=(n == 0 and i == 0), stop=(n == 1 and i == 1), is_transpose=True,
-                        )
-                nc.scalar.copy(
-                    zt[c][:, :, :, 32 * s : 32 * (s + 1), :].rearrange("m i u p e -> m u i p e"),
-                    bank[:, 0 : 2 * P].rearrange("m (i p u e) -> m u i p e", i=2, u=2, e=2),
-                )
+        def blocks_of(ap):
+            return [ap[:, lo : lo + P] for lo in range(0, ap.shape[1], P)]
+
+        def open_excess(name, at, negs):
+            bank = bank_tile(name, at)
+            add_turned(bank, [block for neg in negs for block in blocks_of(neg)], True, False)
+            return bank
+
+        def close_excess(bank, picks):
+            mags = []
+            for s, x, m0 in picks:
+                width = x.shape[1]
+                nc.vector.tensor_copy(x[:], pages[s][:].indirect(idx3[:, m0 // 16 : (m0 + width) // 16]))
+                mag = ring.tile([P, width], F32, name="mag", tag=f"mag{width}", align_bytes=64)
+                nc.scalar.activation(mag[:], x[:], ACT.Abs)
+                mags.append(mag)
+            col = 0
+            for n, mag in enumerate(mags):
+                add_turned(bank[:, col:HALF], blocks_of(mag[:]), False, n + 1 == len(mags))
+                col = col + mag.shape[1]
+            col = 0
+            for s, x, m0 in picks:
+                for c0 in range(0, x.shape[1], CHUNK):
+                    nc.scalar.copy(
+                        zt[(m0 + c0) // CHUNK][:, :, :, 32 * s : 32 * (s + 1), :].rearrange("m i u p e -> m u i p e"),
+                        bank[:, col : col + CHUNK].rearrange("m (i p u e) -> m u i p e", i=2, u=2, e=2),
+                    )
+                    col = col + CHUNK
 
         woc = kept([P, N], U32, "woc")
         wos = kept([P, N], U8, "wos")
 
         def quantize_wo():
-            raw = staged("wo_raw", [P, 4, N], 3)
-            nc.sync.dma_start(out=raw[:], in_=wo.rearrange("(p j) n -> p j n", j=4))
             grouped = kept([P, 4, P, 4], BF16, "wo_grouped")
             for t in range(4):
-                nc.scalar.copy(grouped[:, t], raw[:].rearrange("p j (c t) -> p t c j", t=4)[:, t])
+                nc.scalar.copy(grouped[:, t], wo_raw[:].rearrange("p j (c t) -> p t c j", t=4)[:, t])
             nc.vector.quantize_mx(out=woc[:].bitcast(FP8X4), scales=wos[:], in_=grouped[:].rearrange("p t c j -> p (t c j)"))
 
         yc = kept([P, M], U32, "yc")
@@ -245,11 +267,11 @@ def tile_list_handshake_anomaly_scores_kernel(
 
         def quantize_z(c):
             words = zt[c][:].rearrange("m i u p e -> m (i u p e)").bitcast(F32)
-            bank = psum.tile([P, HALF], F32, name="bank_e")
+            bank = bank_tile(f"back{c}", 2 * (c % 2))
             for j in range(4):
                 nc.tensor.transpose(bank[:, j * P : (j + 1) * P], words[:, j * P : (j + 1) * P], ident[:])
             z = ringed([P, CHUNK * 4], BF16, "z")
-            (nc.scalar.copy if c % 2 == 0 else nc.vector.tensor_copy)(
+            (nc.scalar.copy if c == 1 else nc.vector.tensor_copy)(
                 z[:].bitcast(F32).rearrange("p (i m u) -> p i m u", i=2, u=2),
                 bank[:].rearrange("p (i u m) -> p i m u", i=2, u=2),
             )
@@ -258,12 +280,12 @@ def tile_list_handshake_anomaly_scores_kernel(
             nc.vector.quantize_mx(out=zc[:].bitcast(FP8X4), scales=zs[:], in_=z[:])
             return zc, zs
 
-        def scores(zc, zs, m0, lo, width):
+        def scores(banks, zc, zs, m0, lo, width):
             cols = slice(m0 + lo, m0 + lo + width)
             y = ring.tile([P, 4, width], F32, name="y", bufs=3, align_bytes=64)
             per_bank = HALF // width
-            for first, tag in zip(range(0, 4, per_bank), ("bank_d", "bank_r")):
-                acc = psum.tile([P, HALF], F32, name=tag)
+            for first, at in zip(range(0, 4, per_bank), banks):
+                acc = bank_tile(f"acc_y{m0 + lo}_{first}", at)
                 for i in range(per_bank):
                     t = first + i
                     nc.tensor.matmul_mx(
@@ -278,36 +300,46 @@ def tile_list_handshake_anomaly_scores_kernel(
             nc.vector.quantize_mx(out=yc[:, cols].bitcast(FP8X4), scales=ys[:, cols], in_=grouped[:].rearrange("p m t -> p (m t)"))
             nc.sync.dma_start(out=out_words[:, cols], in_=yc[:, cols].bitcast(I32))
 
-        units = [(s, h) for s in range(PAGES) for h in range(2)]
-        rec = reconstruct(*units[0])
-        res = residual(*units[0], rec)
-        negs = []
+        for jt in range(4):
+            reconstruct(jt, 2 * jt, 2 * jt + 1)
+        ready = [residual(0, parts=2)]
+        quantize_wr(1, [tile[:] for tile in wr_second], nc.scalar.copy)
+        for jt, bank_e, bank_d in ((4, 1, 3), (5, 6, 5), (6, 0, 7), (7, 2, 4)):
+            reconstruct(jt, bank_e, bank_d)
+        load_tol(0)
+        load_tol(1)
+        wo_raw = placed([P, 4, N], F32, "wo_raw", WO_AT)
+        nc.sync.dma_start(out=wo_raw[:], in_=wo.rearrange("(p j) n -> p j n", j=4))
+        load_tol(2)
+        ready.append(residual(1))
         for u, (s, h) in enumerate(units):
-            last = u + 1 == len(units)
-            if u == 0:
-                scatter(s, h, res)
-            if not last:
-                rec = reconstruct(*units[u + 1])
-            if s > 0:
-                excess(s - 1, negs[s - 1], h * HALF, HALF)
-            if u > 0:
-                scatter(s, h, res)
-            if h == 0:
-                if s + 1 < PAGES:
-                    quantize_wr(s + 1)
-                else:
-                    quantize_wo()
-            if not last:
-                res = residual(*units[u + 1], rec)
-            if h == 1:
-                negs.append(negated_tol(s))
-        neg = negs[PAGES - 1]
+            scatter(s, ready[u])
+            if u in (0, 2):
+                quantize_wr(u // 2 + 2, [tile[:, :, u // 2 * P : (u // 2 + 1) * P] for tile in wr_rest], nc.scalar.copy)
+            if u == 4:
+                load_tol(3)
+                quantize_wo()
+            if u + 2 < len(units):
+                ready.append(residual(u + 2))
+        for n, slot in enumerate((4, 3, 6, 5, 7)):
+            s, half = divmod(n, 2)
+            bank = open_excess(f"acc_t{n}", (3, 5, 7, 4)[n % 4], [negated_tol(s, half)[:]])
+            close_excess(bank, [(s, placed([P, HALF], F32, f"x{n}", SWAP_AT + 2048 * slot), half * HALF)])
+        last = PAGES - 1
+        negs = {(s, h): negated_tol(s, h) for s, h in ((last, 0), (last - 1, 1), (last, 1))}
+        left = [[last] if c < 2 else [last - 1, last] for c in range(CHUNKS)]
+        banks = [
+            open_excess(f"acc_last{c}", (5, 7, 4, 3)[c], [negs[s, c // 2][:, (c % 2) * CHUNK : (c % 2 + 1) * CHUNK] for s in left[c]])
+            for c in range(CHUNKS)
+        ]
         for c in range(CHUNKS):
-            excess(PAGES - 1, neg, c * CHUNK, CHUNK)
-            if c > 0:
-                scores(*quantize_z(c - 1), (c - 1) * CHUNK, 0, CHUNK)
-        zc, zs = quantize_z(CHUNKS - 1)
-        for lo in range(0, CHUNK, P):
-            scores(zc, zs, M - CHUNK, lo, P)
+            close_excess(banks[c], [(s, ringed([P, CHUNK], F32, "x_last", bufs=6), c * CHUNK) for s in left[c]])
+        codes = [quantize_z(0)]
+        for c in range(CHUNKS - 1):
+            codes.append(quantize_z(c + 1))
+            scores(((1, 6), (5, 7), (4, 3))[c], *codes[c], c * CHUNK, 0, CHUNK)
+        for lo, at in ((0, 1), (P, 6)):
+            scores((at,), *codes[-1], M - CHUNK, lo, P)
         for q in range(4):
-            nc.sync.dma_start(out=out_2[0, 4 * q : 4 * q + 4, :].bitcast(I32), in_=ys[32 * q : 32 * q + 4, :].bitcast(I32))
+            queue = nc.sync if q % 2 == 0 else nc.scalar
+            queue.dma_start(out=out_2[0, 4 * q : 4 * q + 4, :].bitcast(I32), in_=ys[32 * q : 32 * q + 4, :].bitcast(I32))

@@ -25,6 +25,7 @@ CHUNK = 256
 CHUNKS = M // CHUNK
 STAGE = 96
 WE_AT, WD_AT, PLANE = S, S + H, S + 2 * H
+LAP = 64
 
 
 def tile_list_handshake_anomaly_scores_kernel(
@@ -56,27 +57,23 @@ def tile_list_handshake_anomaly_scores_kernel(
             return psum.tile([P, HALF], F32, name=name, offset=2048 * bank)
 
         PAGE2_AT = 0
-        TW0_AT = PAGE2_AT + 8192 - 512
-        WR0_AT = TW0_AT + 512
-        WGS_AT = WR0_AT + 4096
-        WR1_AT = WGS_AT + 4096
-        PAGE3_AT = WR1_AT + 4096
-        TW1_AT = PAGE3_AT + 8192
-        SWAP_AT = TW1_AT
+        TW0_AT = PAGE2_AT + 8192 - LAP
+        WR_AT = PAGE2_AT + 8192
+        PAGE3_AT = WR_AT + 16384
+        WO_AT = PAGE3_AT + 8192
+        TW1_AT = WO_AT + 8192 - LAP
+        WGS0_AT = WO_AT + 8192
         PICKED_AT = TW1_AT + 16384 - 512
-        PAGE1_AT = PICKED_AT + 512
-        WR2_AT = PAGE1_AT + 8192
-        STAGED_AT = WR2_AT + 3072
-        WO_AT = WR2_AT + 8192
-        TOL0_AT = WO_AT + 8192
-        WD_WORDS_AT = TOL0_AT - 1024
-        TOL1_AT = TOL0_AT + 4096
-        WE_WORDS_AT = TOL1_AT + 3072
-        tw = [placed([P, T], U32, "tw0", TW0_AT), placed([P, T], U32, "tw1", TW1_AT)]
+        PAGE1_AT = PICKED_AT + 1024 - LAP
+        STAGED_AT = PAGE1_AT + 8192
+        WGS1_AT = STAGED_AT + 2048 - LAP
+        HELD_AT = {1: WGS1_AT + 12288, 3: WGS1_AT + 8192}
+        MAG1_AT = WGS1_AT + 16384
+        tw = [placed([P, T + 2 * LAP // 4], U32, "tw0", TW0_AT), placed([P, T], U32, "tw1", TW1_AT)]
         ts = kept([P, T], U8, "ts")
         staged = placed([P, PLANE], U8, "staged", STAGED_AT)
-        wew = placed([P, PASSES * 2 * H], U8, "wew", WE_WORDS_AT)
-        wdw = placed([P, PASSES, H], U32, "wdw", WD_WORDS_AT)
+        wew = kept([P, PASSES * 2 * H], U8, "wew")
+        wdw = kept([P, PASSES, H], U32, "wdw")
         pages = [kept([P, T2], F32, "page0")]
         pages.extend(placed([P, T2], F32, f"page{s + 1}", at) for s, at in enumerate((PAGE1_AT, PAGE2_AT, PAGE3_AT)))
         ident = kept([P, P], F32, "ident")
@@ -88,24 +85,22 @@ def tile_list_handshake_anomaly_scores_kernel(
         def stage_rows(dst, src):
             nc.sync.dma_start(out=dst.bitcast(I32), in_=src.rearrange("a q c -> (a q) c").bitcast(I32))
 
-        def load_table(a):
-            nc.sync.dma_start(out=tw[a][:].bitcast(I32), in_=tab_words[a].rearrange("p t i -> p (t i)").bitcast(I32))
-
-        def load_wr(tile, a, lo, hi):
-            nc.sync.dma_start(out=tile[:], in_=wr[512 * a : 512 * (a + 1), lo:hi].rearrange("(p j) c -> p j c", j=4))
+        def load_table(a, lo, hi):
+            nc.sync.dma_start(out=tw[a][:, lo:hi].bitcast(I32), in_=tab_words[a].rearrange("p t i -> p (t i)").bitcast(I32)[:, lo:hi])
 
         nc.sync.dma_start(idx[:], offs)
         stage_rows(ts[STAGE:P, :], tab_scales)
-        stage_rows(staged[STAGE:P, WE_AT:WD_AT], we_scales)
-        stage_rows(staged[STAGE:P, WD_AT:PLANE], wd_scales)
-        nc.sync.dma_start(idx2[:], offs2)
-        nc.sync.dma_start(idx3[:], offs3)
-        load_table(0)
+        load_table(0, 0, T)
         nc.sync.dma_start(
             out=wew[:].bitcast(I32).rearrange("p (a c) -> p a c", a=PASSES),
             in_=we_words.rearrange("a p c -> p a c").bitcast(I32),
         )
+
         nc.sync.dma_start(out=wdw[:].bitcast(I32), in_=wd_words.rearrange("a p c i -> p a (c i)").bitcast(I32))
+        stage_rows(staged[STAGE:P, WE_AT:WD_AT], we_scales)
+        stage_rows(staged[STAGE:P, WD_AT:PLANE], wd_scales)
+        nc.sync.dma_start(idx2[:], offs2)
+        nc.sync.dma_start(idx3[:], offs3)
 
         vw = [[kept([P, HALF], U32, f"vw{a}{h}") for h in range(2)] for a in range(PASSES)]
         planes = [kept([P, PLANE], U8, f"plane{a}") for a in range(PASSES)]
@@ -115,7 +110,7 @@ def tile_list_handshake_anomaly_scores_kernel(
             return lst[:, h * (HALF // 16) : (h + 1) * (HALF // 16)]
 
         def gather_words(a, h):
-            nc.vector.tensor_copy(vw[a][h][:], tw[a][:].indirect(half_of(idx, h)))
+            nc.vector.tensor_copy(vw[a][h][:], tw[a][:, 0:T].indirect(half_of(idx, h)))
 
         nc.vector.tensor_copy(picked[:], ts[:].indirect(idx[:]))
         nc.vector.tensor_copy(staged[STAGE:P, 0:S].bitcast(I32), picked[STAGE:P, :].bitcast(I32))
@@ -125,43 +120,55 @@ def tile_list_handshake_anomaly_scores_kernel(
                 rows = staged[STAGE + 16 * a + r : STAGE + 16 * (a + 1) : 4, :]
                 nc.sync.dma_start(out=planes[a][r:P:32, :].bitcast(I32), in_=rows.bitcast(I32))
 
+        load_table(1, 0, T // 2)
         move_scales(0)
-        load_table(1)
+        load_table(1, T // 2, T)
         move_scales(1)
-        nc.vector.memset(pages[1][:], 0.0)
-
-        wrc = [kept([P, PASSES * P], U32, f"wrc{s}") for s in range(PAGES)]
-        wrs = [kept([P, PASSES * P], U8, f"wrs{s}") for s in range(PAGES)]
-
-        def quantize_wr(s, raws, copy):
-            grouped = ringed([P, PASSES, P, 4], BF16, "wr_grouped")
-            for a in range(PASSES):
-                copy(grouped[:, a], raws[a].rearrange("p j c -> p c j"))
-            nc.vector.quantize_mx(out=wrc[s][:].bitcast(FP8X4), scales=wrs[s][:], in_=grouped[:].rearrange("p a c j -> p (a c j)"))
+        nc.gpsimd.memset(pages[1][:], 0.0)
 
         gather_words(0, 0)
         gather_words(0, 1)
-        wr_first = [placed([P, 4, P], F32, f"wr_first{a}", WR0_AT + 2048 * a) for a in range(PASSES)]
+        wr_raw = [placed([P, 4, H], F32, f"wr_raw{a}", WR_AT + 8192 * a) for a in range(PASSES)]
         for a in range(PASSES):
-            load_wr(wr_first[a], a, 0, P)
-        wgs_sb = placed([P, S], F32, "wgs_sb", WGS_AT)
-        nc.sync.dma_start(out=wgs_sb[:], in_=wgs)
-        wr_second = [placed([P, 4, P], F32, f"wr_second{a}", WR1_AT + 2048 * a) for a in range(PASSES)]
-        for a in range(PASSES):
-            load_wr(wr_second[a], a, P, 2 * P)
-        for page in pages[2:]:
-            nc.vector.memset(page[:], 0.0)
+            nc.sync.dma_start(out=wr_raw[a][:], in_=wr[512 * a : 512 * (a + 1), :].rearrange("(p j) c -> p j c", j=4))
+        nc.gpsimd.memset(pages[2][:], 0.0)
+        nc.vector.memset(pages[3][:], 0.0)
         gather_words(1, 0)
         gather_words(1, 1)
-        quantize_wr(0, [tile[:] for tile in wr_first], nc.vector.tensor_copy)
-        wr_rest = [placed([P, 4, 2 * P], F32, f"wr_rest{a}", WR2_AT + 4096 * a) for a in range(PASSES)]
-        for a in range(PASSES):
-            load_wr(wr_rest[a], a, 2 * P, H)
-        tol_raw = []
 
-        def load_tol(s):
-            tol_raw.append(placed([P, M], F32, f"tol_raw{s}", (TOL0_AT, TOL1_AT, TOL1_AT + 4096, WR2_AT + 4096)[s]))
-            nc.sync.dma_start(out=tol_raw[s][:], in_=tol[s * P : (s + 1) * P, :])
+        wgs_sb = [placed([P, 2, S], F32, f"wgs{u}", at) for u, at in enumerate((WGS0_AT, WGS1_AT))]
+
+        def load_wgs(first, count):
+            u, e = divmod(first, 2)
+            rows = wgs.rearrange("(i t) j -> i t j", t=PAGES)[:, first : first + count, :]
+            for q in (0, 2, 1, 3):
+                nc.sync.dma_start(out=wgs_sb[u][32 * q : 32 * (q + 1), e : e + count], in_=rows)
+
+        load_wgs(0, 1)
+        load_wgs(1, 1)
+        wo_raw = placed([P, 4, N], F32, "wo_raw", WO_AT)
+        nc.sync.dma_start(out=wo_raw[:], in_=wo.rearrange("(p j) n -> p j n", j=4))
+        load_wgs(2, 2)
+
+        wo_grouped = placed([P, 4, P, 4], BF16, "wo_grouped", HELD_AT[3])
+        woc = kept([P, N], U32, "woc")
+        wos = kept([P, N], U8, "wos")
+
+        wr_grouped = [kept([P, 2, PASSES, P, 4], BF16, "wr_grouped0"), placed([P, 2, PASSES, P, 4], BF16, "wr_grouped1", HELD_AT[1])]
+        wrc = [kept([P, 2, PASSES, P], U32, "wrc0"), placed([P, 2, PASSES, P], U32, "wrc1", MAG1_AT)]
+        wrs = [kept([P, 2, PASSES, P], U8, f"wrs{u}") for u in range(2)]
+
+        def group_wr(u, a, copy):
+            copy(wr_grouped[u][:, :, a].rearrange("p e i j -> p i e j"),
+                 wr_raw[a][:].rearrange("p j (i t) -> p i t j", t=4)[:, :, 2 * u : 2 * u + 2])
+
+        def quantize_wr(first, count):
+            u, e = divmod(first, 2)
+            nc.vector.quantize_mx(
+                out=wrc[u][:, e : e + count].rearrange("p t a i -> p (t a i)").bitcast(FP8X4),
+                scales=wrs[u][:, e : e + count].rearrange("p t a i -> p (t a i)"),
+                in_=wr_grouped[u][:, e : e + count].rearrange("p e a i j -> p (e a i j)"),
+            )
 
         def product(out, jt, codes_of, scale_of):
             h, lo = divmod(jt * P, HALF)
@@ -176,170 +183,150 @@ def tile_list_handshake_anomaly_scores_kernel(
                 nc.tensor.matmul(bank[:, i * P : (i + 1) * P], block, ident[:], start=(start and i == 0),
                                  stop=(stop and i == len(blocks) - 1), is_transpose=True)
 
-        recs = [kept([P, H], F32, f"rec{jt}") for jt in range(S // P)]
+        recs = [kept([P, PAGES, P], F32, f"rec{jt}") for jt in range(S // P)]
+
+        def dealt(bank):
+            return bank[:].rearrange("p (i t) -> p t i", t=PAGES)
 
         def reconstruct(jt, bank_e, bank_d):
             acc_e = bank_tile(f"acc_e{jt}", bank_e)
             product(acc_e[:], jt, lambda a: wew[:, 2 * a * H : 2 * (a + 1) * H].bitcast(FP4X4), lambda a: planes[a][:, WE_AT:WD_AT])
             acc_d = bank_tile(f"acc_d{jt}", bank_d)
             product(acc_d[:], jt, lambda a: wdw[:, a].bitcast(FP8X4), lambda a: planes[a][:, WD_AT:PLANE])
-            e = ringed([P, H], F32, "e", bufs=4)
-            nc.scalar.activation(e[:], acc_e[:], ACT.Tanh, scale=-1.0)
-            nc.vector.tensor_tensor(recs[jt][:], acc_d[:], e[:], ALU.mult)
+            e = ringed([P, PAGES, P], F32, "e", bufs=4)
+            nc.scalar.activation(e[:], dealt(acc_e), ACT.Tanh, scale=-1.0)
+            nc.vector.tensor_tensor(recs[jt][:], dealt(acc_d), e[:], ALU.mult)
 
-        units = [(0, 0), (1, 0), (0, 1), (2, 0), (1, 1), (3, 0), (2, 1), (3, 1)]
+        units = [(2 * u + e, h) for u in range(2) for h in range(2) for e in range(2)]
+        RUN = PAGES * CHUNK
+        work = kept([P, CHUNKS * RUN + 384], F32, "work")
 
         def residual(u, parts=1):
-            s, h = units[u]
-            feat_bank, sum_bank = (1, 6) if u % 2 else (0, 2)
+            t, h = units[u]
+            feat_bank, sum_bank = (4, 6) if u % 2 else (0, 2)
             acc = bank_tile(f"acc_r{u}", feat_bank)
             for i in range(4):
-                product(acc[:, i * P : (i + 1) * P], 4 * h + i, lambda a: wrc[s][:, a * P : (a + 1) * P].bitcast(FP8X4),
-                        lambda a: wrs[s][:, a * P : (a + 1) * P])
-            feat = placed([P, HALF], F32, f"feat{u}", SWAP_AT + 2048 * u)
+                product(acc[:, i * P : (i + 1) * P], 4 * h + i, lambda a: wrc[t // 2][:, t % 2, a].bitcast(FP8X4), lambda a: wrs[t // 2][:, t % 2, a])
+            feat = placed([P, HALF], F32, f"feat{u}", HELD_AT[u]) if u in HELD_AT else ringed([P, HALF], F32, "feat", bufs=3)
             nc.scalar.copy(feat[:], acc[:])
             out = []
+            width = HALF // parts
+            if u + 1 == len(units):
+                mag = work[:, RUN : RUN + HALF]
+            elif u == 1:
+                mag = placed([P, HALF], F32, "mag1", MAG1_AT)[:]
+            else:
+                mag = kept([P, HALF], F32, f"mag{u}")[:]
             for part in range(parts):
                 blocks = range(part * 4 // parts, (part + 1) * 4 // parts)
-                bank = bank_tile(f"acc_h{u}_{part}", sum_bank + 2 * part)
-                add_turned(bank, [feat[:, i * P : (i + 1) * P] for i in blocks], True, False)
-                add_turned(bank, [recs[4 * h + i][:, s * P : (s + 1) * P] for i in blocks], False, True)
-                width = HALF // parts
-                res = ring.tile([P, width], F32, name="res", tag=f"res{width}", bufs=7 if parts == 1 else 2, align_bytes=64)
-                nc.scalar.copy(res[:], bank[:, 0:width])
-                out.append((h * HALF + part * width, res))
+                bank = bank_tile(f"acc_h{u}_{part}", sum_bank - 2 * part)
+                add_turned(bank, [recs[4 * h + i][:, t, :] for i in blocks], True, False)
+                add_turned(bank, [feat[:, i * P : (i + 1) * P] for i in blocks], False, True)
+                nc.scalar.activation(mag[:, part * width : (part + 1) * width], bank[:, 0:width], ACT.Abs)
+                out.append((part * width, width, mag))
             return out
 
-        def scatter(s, parts):
-            for lo, res in parts:
-                hi = lo + res.shape[1]
-                nc.vector.tensor_tensor(pages[s][:].indirect(idx2[:, lo // 16 : hi // 16]), res[:], wgs_sb[:, lo:hi], ALU.mult)
-
-        zt = [kept([P, 2, 2, P, 2], BF16, f"zt{c}") for c in range(CHUNKS)]
-
-        def negated_tol(s, h):
-            neg = ringed([P, HALF], F32, "tol_neg", bufs=8)
-            nc.scalar.activation(neg[:], tol_raw[s][:, h * HALF : (h + 1) * HALF], ACT.Copy, scale=-1.0)
-            return neg
-
-        def blocks_of(ap):
-            return [ap[:, lo : lo + P] for lo in range(0, ap.shape[1], P)]
-
-        def open_excess(name, at, negs):
-            bank = bank_tile(name, at)
-            add_turned(bank, [block for neg in negs for block in blocks_of(neg)], True, False)
-            return bank
-
-        def close_excess(bank, picks):
-            mags = []
-            for s, x, m0 in picks:
-                width = x.shape[1]
-                nc.vector.tensor_copy(x[:], pages[s][:].indirect(idx3[:, m0 // 16 : (m0 + width) // 16]))
-                mag = ring.tile([P, width], F32, name="mag", tag=f"mag{width}", align_bytes=64)
-                nc.scalar.activation(mag[:], x[:], ACT.Abs)
-                mags.append(mag)
-            col = 0
-            for n, mag in enumerate(mags):
-                add_turned(bank[:, col:HALF], blocks_of(mag[:]), False, n + 1 == len(mags))
-                col = col + mag.shape[1]
-            col = 0
-            for s, x, m0 in picks:
-                for c0 in range(0, x.shape[1], CHUNK):
-                    nc.scalar.copy(
-                        zt[(m0 + c0) // CHUNK][:, :, :, 32 * s : 32 * (s + 1), :].rearrange("m i u p e -> m u i p e"),
-                        bank[:, col : col + CHUNK].rearrange("m (i p u e) -> m u i p e", i=2, u=2, e=2),
-                    )
-                    col = col + CHUNK
-
-        woc = kept([P, N], U32, "woc")
-        wos = kept([P, N], U8, "wos")
-
-        def quantize_wo():
-            grouped = kept([P, 4, P, 4], BF16, "wo_grouped")
-            for t in range(4):
-                nc.scalar.copy(grouped[:, t], wo_raw[:].rearrange("p j (c t) -> p t c j", t=4)[:, t])
-            nc.vector.quantize_mx(out=woc[:].bitcast(FP8X4), scales=wos[:], in_=grouped[:].rearrange("p t c j -> p (t c j)"))
+        def scatter(u, parts):
+            t, h = units[u]
+            for lo, width, mag in parts:
+                first = h * HALF + lo
+                nc.vector.tensor_tensor(pages[t][:].indirect(idx2[:, first // 16 : (first + width) // 16]),
+                                        mag[:, lo : lo + width], wgs_sb[t // 2][:, t % 2, first : first + width], ALU.mult)
 
         yc = kept([P, M], U32, "yc")
         ys = kept([P, M], U8, "ys")
         out_rows = out_0.rearrange("(p t) m -> p t m", t=4)
         out_words = out_1[0].rearrange("p m t -> p (m t)").bitcast(I32)
 
-        def quantize_z(c):
-            words = zt[c][:].rearrange("m i u p e -> m (i u p e)").bitcast(F32)
-            bank = bank_tile(f"back{c}", 2 * (c % 2))
-            for j in range(4):
-                nc.tensor.transpose(bank[:, j * P : (j + 1) * P], words[:, j * P : (j + 1) * P], ident[:])
-            z = ringed([P, CHUNK * 4], BF16, "z")
-            (nc.scalar.copy if c == 1 else nc.vector.tensor_copy)(
-                z[:].bitcast(F32).rearrange("p (i m u) -> p i m u", i=2, u=2),
-                bank[:].rearrange("p (i u m) -> p i m u", i=2, u=2),
-            )
-            zc = ringed([P, CHUNK], U32, "zc")
-            zs = ringed([P, CHUNK], U8, "zs")
-            nc.vector.quantize_mx(out=zc[:].bitcast(FP8X4), scales=zs[:], in_=z[:])
-            return zc, zs
+        def excess(c, t):
+            cols = slice(c * CHUNK, (c + 1) * CHUNK)
+            nc.vector.tensor_tensor(work[:, c * RUN + t * CHUNK : c * RUN + (t + 1) * CHUNK],
+                                    pages[t][:].indirect(idx3[:, c * CHUNK // 16 : (c + 1) * CHUNK // 16]),
+                                    tol_sb[:, t, cols], ALU.subtract)
 
-        def scores(banks, zc, zs, m0, lo, width):
-            cols = slice(m0 + lo, m0 + lo + width)
-            y = ring.tile([P, 4, width], F32, name="y", bufs=3, align_bytes=64)
-            per_bank = HALF // width
-            for first, at in zip(range(0, 4, per_bank), banks):
-                acc = bank_tile(f"acc_y{m0 + lo}_{first}", at)
-                for i in range(per_bank):
-                    t = first + i
-                    nc.tensor.matmul_mx(
-                        out=acc[:, i * width : (i + 1) * width], lhsT=woc[:, t * P : (t + 1) * P].bitcast(FP8X4),
-                        lhsT_scale=wos[:, t * P : (t + 1) * P], rhs=zc[:, lo : lo + width].bitcast(FP8X4),
-                        rhs_scale=zs[:, lo : lo + width], start=True, stop=True,
-                    )
-                nc.scalar.copy(y[:, first : first + per_bank, :].rearrange("p t m -> p (t m)"), acc[:])
+        def rounded_at(c):
+            return ((c + 1) % CHUNKS) * RUN + 640
+
+        def round_z(c):
+            both = work[:, rounded_at(c) : rounded_at(c) + 768].bitcast(BF16)
+            for i in range(2):
+                (nc.vector.tensor_copy if (c, i) == (CHUNKS - 1, 1) else nc.scalar.copy)(
+                    both[:, 1024 * i : 1024 * i + 512].rearrange("p (m n t) -> p m t n", t=4, n=4),
+                    work[:, c * RUN : (c + 1) * RUN].rearrange("p (t m n) -> p m t n", t=4, n=4)[:, i * P // 4 : (i + 1) * P // 4],
+                )
+
+        def quantize_z(c, i):
+            zc = ringed([P, P], U32, "zc", bufs=4)
+            zs = ringed([P, P], U8, "zs", bufs=4)
+            at = rounded_at(c) + 512 * i
+            nc.vector.quantize_mx(out=zc[:].bitcast(FP8X4), scales=zs[:], in_=work[:, at : at + 256].bitcast(BF16))
+            acc = bank_tile(f"acc_y{c}_{i}", (0, 2, 1, 3, 5, 7, 4, 6)[2 * c + i])
+            for t in range(4):
+                nc.tensor.matmul_mx(
+                    out=acc[:, t * P : (t + 1) * P], lhsT=woc[:, t * P : (t + 1) * P].bitcast(FP8X4),
+                    lhsT_scale=wos[:, t * P : (t + 1) * P], rhs=zc[:].bitcast(FP8X4), rhs_scale=zs[:], start=True, stop=True,
+                )
+            return acc
+
+        def empty(c, acc, i, y, grouped):
+            cols = slice(i * P, (i + 1) * P)
+            nc.scalar.copy(y[:, :, cols], acc[:].rearrange("p (t m) -> p t m", t=4))
+            if c < 2:
+                nc.scalar.copy(grouped[:, cols, :], acc[:].rearrange("p (t m) -> p m t", t=4))
+            else:
+                nc.vector.tensor_copy(grouped[:, cols, :].rearrange("p (m n) t -> p m t n", n=4), y[:, :, cols].rearrange("p t (m n) -> p m t n", n=4))
+
+        def finish(c, y, grouped):
+            cols = slice(c * CHUNK, (c + 1) * CHUNK)
             nc.sync.dma_start(out=out_rows[:, :, cols], in_=y[:])
-            grouped = ringed([P, width, 4], BF16, "y_grouped")
-            nc.vector.tensor_copy(grouped[:], y[:].rearrange("p t m -> p m t"))
             nc.vector.quantize_mx(out=yc[:, cols].bitcast(FP8X4), scales=ys[:, cols], in_=grouped[:].rearrange("p m t -> p (m t)"))
-            nc.sync.dma_start(out=out_words[:, cols], in_=yc[:, cols].bitcast(I32))
+            (nc.sync if c + 1 < CHUNKS else nc.scalar).dma_start(out=out_words[:, cols], in_=yc[:, cols].bitcast(I32))
 
-        for jt in range(4):
+        for jt in range(2):
             reconstruct(jt, 2 * jt, 2 * jt + 1)
+        for a in range(PASSES):
+            group_wr(0, a, nc.vector.tensor_copy)
+        quantize_wr(0, 1)
+        for jt in range(2, 4):
+            reconstruct(jt, 2 * jt, 2 * jt + 1)
+        quantize_wr(1, 1)
+        for jt in range(4, 7):
+            reconstruct(jt, 2 * jt - 8, 2 * jt - 7)
         ready = [residual(0, parts=2)]
-        quantize_wr(1, [tile[:] for tile in wr_second], nc.scalar.copy)
-        for jt, bank_e, bank_d in ((4, 1, 3), (5, 6, 5), (6, 0, 7), (7, 2, 4)):
-            reconstruct(jt, bank_e, bank_d)
-        load_tol(0)
-        load_tol(1)
-        wo_raw = placed([P, 4, N], F32, "wo_raw", WO_AT)
-        nc.sync.dma_start(out=wo_raw[:], in_=wo.rearrange("(p j) n -> p j n", j=4))
-        load_tol(2)
+        reconstruct(7, 6, 7)
         ready.append(residual(1))
-        for u, (s, h) in enumerate(units):
-            scatter(s, ready[u])
-            if u in (0, 2):
-                quantize_wr(u // 2 + 2, [tile[:, :, u // 2 * P : (u // 2 + 1) * P] for tile in wr_rest], nc.scalar.copy)
-            if u == 4:
-                load_tol(3)
-                quantize_wo()
-            if u + 2 < len(units):
-                ready.append(residual(u + 2))
-        for n, slot in enumerate((4, 3, 6, 5, 7)):
-            s, half = divmod(n, 2)
-            bank = open_excess(f"acc_t{n}", (3, 5, 7, 4)[n % 4], [negated_tol(s, half)[:]])
-            close_excess(bank, [(s, placed([P, HALF], F32, f"x{n}", SWAP_AT + 2048 * slot), half * HALF)])
-        last = PAGES - 1
-        negs = {(s, h): negated_tol(s, h) for s, h in ((last, 0), (last - 1, 1), (last, 1))}
-        left = [[last] if c < 2 else [last - 1, last] for c in range(CHUNKS)]
-        banks = [
-            open_excess(f"acc_last{c}", (5, 7, 4, 3)[c], [negs[s, c // 2][:, (c % 2) * CHUNK : (c % 2 + 1) * CHUNK] for s in left[c]])
-            for c in range(CHUNKS)
-        ]
+        for a in range(PASSES):
+            group_wr(1, a, nc.scalar.copy)
+        tol_sb = placed([P, PAGES, M], F32, "tol_sb", WR_AT)
+        nc.sync.dma_start(out=tol_sb[:], in_=tol.rearrange("(p t) m -> p t m", t=PAGES))
+        ready.extend(residual(u) for u in range(2, 4))
+        nc.scalar.copy(wo_grouped[:].rearrange("p t i j -> p i t j"), wo_raw[:].rearrange("p j (i t) -> p i t j", t=4))
+        for u in range(len(units)):
+            scatter(u, ready[u])
+            if u == 1:
+                quantize_wr(2, 2)
+                ready.extend(residual(later) for later in range(4, len(units)))
+            if u == 3:
+                nc.vector.quantize_mx(out=woc[:].bitcast(FP8X4), scales=wos[:], in_=wo_grouped[:].rearrange("p t i j -> p (t i j)"))
+        for t in range(PAGES):
+            excess(0, t)
+        round_z(0)
         for c in range(CHUNKS):
-            close_excess(banks[c], [(s, ringed([P, CHUNK], F32, "x_last", bufs=6), c * CHUNK) for s in left[c]])
-        codes = [quantize_z(0)]
-        for c in range(CHUNKS - 1):
-            codes.append(quantize_z(c + 1))
-            scores(((1, 6), (5, 7), (4, 3))[c], *codes[c], c * CHUNK, 0, CHUNK)
-        for lo, at in ((0, 1), (P, 6)):
-            scores((at,), *codes[-1], M - CHUNK, lo, P)
+            if c + 1 < CHUNKS:
+                excess(c + 1, 0)
+                excess(c + 1, 1)
+            accs = {i: quantize_z(c, i) for i in ((0, 1) if c + 1 < CHUNKS else (1, 0))}
+            if c + 1 < CHUNKS:
+                excess(c + 1, 2)
+                excess(c + 1, 3)
+            y = ringed([P, 4, CHUNK], F32, "y", bufs=3)
+            grouped_y = ringed([P, CHUNK, 4], BF16, "grouped_y")
+            first, second = accs
+            empty(c, accs[first], first, y, grouped_y)
+            if c + 1 < CHUNKS:
+                round_z(c + 1)
+            empty(c, accs[second], second, y, grouped_y)
+            finish(c, y, grouped_y)
         for q in range(4):
             queue = nc.sync if q % 2 == 0 else nc.scalar
             queue.dma_start(out=out_2[0, 4 * q : 4 * q + 4, :].bitcast(I32), in_=ys[32 * q : 32 * q + 4, :].bitcast(I32))

@@ -124,14 +124,14 @@ def tile_list_handshake_anomaly_scores_kernel(
         move_scales(0)
         load_table(1, T // 2, T)
         move_scales(1)
-        nc.gpsimd.memset(pages[1][:], 0.0)
+        nc.vector.memset(pages[1][:], 0.0)
 
         gather_words(0, 0)
         gather_words(0, 1)
         wr_raw = [placed([P, 4, H], F32, f"wr_raw{a}", WR_AT + 8192 * a) for a in range(PASSES)]
         for a in range(PASSES):
             nc.sync.dma_start(out=wr_raw[a][:], in_=wr[512 * a : 512 * (a + 1), :].rearrange("(p j) c -> p j c", j=4))
-        nc.gpsimd.memset(pages[2][:], 0.0)
+        nc.vector.memset(pages[2][:], 0.0)
         nc.vector.memset(pages[3][:], 0.0)
         gather_words(1, 0)
         gather_words(1, 1)
@@ -159,8 +159,8 @@ def tile_list_handshake_anomaly_scores_kernel(
         wrs = [kept([P, 2, PASSES, P], U8, f"wrs{u}") for u in range(2)]
 
         def group_wr(u, a, copy):
-            copy(wr_grouped[u][:, :, a].rearrange("p e i j -> p i e j"),
-                 wr_raw[a][:].rearrange("p j (i t) -> p i t j", t=4)[:, :, 2 * u : 2 * u + 2])
+            copy(wr_grouped[u][:, :, a].rearrange("p e i j -> p i j e"),
+                 wr_raw[a][:].rearrange("p j (i t) -> p i j t", t=4)[:, :, :, 2 * u : 2 * u + 2])
 
         def quantize_wr(first, count):
             u, e = divmod(first, 2)
@@ -300,7 +300,7 @@ def tile_list_handshake_anomaly_scores_kernel(
         tol_sb = placed([P, PAGES, M], F32, "tol_sb", WR_AT)
         nc.sync.dma_start(out=tol_sb[:], in_=tol.rearrange("(p t) m -> p t m", t=PAGES))
         ready.extend(residual(u) for u in range(2, 4))
-        nc.scalar.copy(wo_grouped[:].rearrange("p t i j -> p i t j"), wo_raw[:].rearrange("p j (i t) -> p i t j", t=4))
+        nc.scalar.copy(wo_grouped[:].rearrange("p t i j -> p i j t"), wo_raw[:].rearrange("p j (i t) -> p i j t", t=4))
         for u in range(len(units)):
             scatter(u, ready[u])
             if u == 1:

@@ -59,21 +59,23 @@ def tile_list_handshake_anomaly_scores_kernel(
         PAGE2_AT = 0
         TW0_AT = PAGE2_AT + 8192 - LAP
         WR_AT = PAGE2_AT + 8192
-        PAGE3_AT = WR_AT + 16384
-        WO_AT = PAGE3_AT + 8192
+        WO_AT = WR_AT + 16384
         TW1_AT = WO_AT + 8192 - LAP
         WGS0_AT = WO_AT + 8192
         PICKED_AT = TW1_AT + 16384 - 512
-        PAGE1_AT = PICKED_AT + 1024 - LAP
-        STAGED_AT = PAGE1_AT + 8192
+        SECOND_AT = PICKED_AT + 1024 - LAP
+        STAGED_AT = SECOND_AT + 6 * H
         WGS1_AT = STAGED_AT + 2048 - LAP
         HELD_AT = {1: WGS1_AT + 12288, 3: WGS1_AT + 8192}
         MAG1_AT = WGS1_AT + 16384
-        tw = [placed([P, T + 2 * LAP // 4], U32, "tw0", TW0_AT), placed([P, T], U32, "tw1", TW1_AT)]
-        ts = kept([P, T], U8, "ts")
+        PAGE1_AT = MAG1_AT + 2048
+        TS_AT = PAGE1_AT + 8192 - LAP
+        E6_AT = TS_AT + T
+        PAGE3_AT = E6_AT + 2048 - LAP
+        tw = [placed([P, T], U32, "tw0", TW0_AT), placed([P, T], U32, "tw1", TW1_AT)]
+        ts = placed([P, T], U8, "ts", TS_AT)
         staged = placed([P, PLANE], U8, "staged", STAGED_AT)
-        wew = kept([P, PASSES * 2 * H], U8, "wew")
-        wdw = kept([P, PASSES, H], U32, "wdw")
+        packed = [kept([P, 6 * H], U8, "packed0"), placed([P, 6 * H], U8, "packed1", SECOND_AT)]
         pages = [kept([P, T2], F32, "page0")]
         pages.extend(placed([P, T2], F32, f"page{s + 1}", at) for s, at in enumerate((PAGE1_AT, PAGE2_AT, PAGE3_AT)))
         ident = kept([P, P], F32, "ident")
@@ -88,15 +90,14 @@ def tile_list_handshake_anomaly_scores_kernel(
         def load_table(a, lo, hi):
             nc.sync.dma_start(out=tw[a][:, lo:hi].bitcast(I32), in_=tab_words[a].rearrange("p t i -> p (t i)").bitcast(I32)[:, lo:hi])
 
+        def load_weights(a):
+            nc.sync.dma_start(out=packed[a][:, 0 : 2 * H].bitcast(I32), in_=we_words[a].bitcast(I32))
+            nc.sync.dma_start(out=packed[a][:, 2 * H : 6 * H].bitcast(I32), in_=wd_words[a].rearrange("p c i -> p (c i)").bitcast(I32))
+
         nc.sync.dma_start(idx[:], offs)
         stage_rows(ts[STAGE:P, :], tab_scales)
         load_table(0, 0, T)
-        nc.sync.dma_start(
-            out=wew[:].bitcast(I32).rearrange("p (a c) -> p a c", a=PASSES),
-            in_=we_words.rearrange("a p c -> p a c").bitcast(I32),
-        )
-
-        nc.sync.dma_start(out=wdw[:].bitcast(I32), in_=wd_words.rearrange("a p c i -> p a (c i)").bitcast(I32))
+        load_weights(0)
         stage_rows(staged[STAGE:P, WE_AT:WD_AT], we_scales)
         stage_rows(staged[STAGE:P, WD_AT:PLANE], wd_scales)
         nc.sync.dma_start(idx2[:], offs2)
@@ -123,6 +124,7 @@ def tile_list_handshake_anomaly_scores_kernel(
         load_table(1, 0, T // 2)
         move_scales(0)
         load_table(1, T // 2, T)
+        load_weights(1)
         move_scales(1)
         nc.vector.memset(pages[1][:], 0.0)
 
@@ -132,7 +134,6 @@ def tile_list_handshake_anomaly_scores_kernel(
         for a in range(PASSES):
             nc.sync.dma_start(out=wr_raw[a][:], in_=wr[512 * a : 512 * (a + 1), :].rearrange("(p j) c -> p j c", j=4))
         nc.vector.memset(pages[2][:], 0.0)
-        nc.vector.memset(pages[3][:], 0.0)
         gather_words(1, 0)
         gather_words(1, 1)
 
@@ -190,10 +191,10 @@ def tile_list_handshake_anomaly_scores_kernel(
 
         def reconstruct(jt, bank_e, bank_d):
             acc_e = bank_tile(f"acc_e{jt}", bank_e)
-            product(acc_e[:], jt, lambda a: wew[:, 2 * a * H : 2 * (a + 1) * H].bitcast(FP4X4), lambda a: planes[a][:, WE_AT:WD_AT])
+            product(acc_e[:], jt, lambda a: packed[a][:, 0 : 2 * H].bitcast(FP4X4), lambda a: planes[a][:, WE_AT:WD_AT])
             acc_d = bank_tile(f"acc_d{jt}", bank_d)
-            product(acc_d[:], jt, lambda a: wdw[:, a].bitcast(FP8X4), lambda a: planes[a][:, WD_AT:PLANE])
-            e = ringed([P, PAGES, P], F32, "e", bufs=4)
+            product(acc_d[:], jt, lambda a: packed[a][:, 2 * H : 6 * H].bitcast(FP8X4), lambda a: planes[a][:, WD_AT:PLANE])
+            e = placed([P, PAGES, P], F32, "e6", E6_AT) if jt == 6 else ringed([P, PAGES, P], F32, "e", bufs=4)
             nc.scalar.activation(e[:], dealt(acc_e), ACT.Tanh, scale=-1.0)
             nc.vector.tensor_tensor(recs[jt][:], dealt(acc_d), e[:], ALU.mult)
 
@@ -294,6 +295,7 @@ def tile_list_handshake_anomaly_scores_kernel(
             reconstruct(jt, 2 * jt - 8, 2 * jt - 7)
         ready = [residual(0, parts=2)]
         reconstruct(7, 6, 7)
+        nc.vector.memset(pages[3][:], 0.0)
         ready.append(residual(1))
         for a in range(PASSES):
             group_wr(1, a, nc.scalar.copy)

@@ -90,14 +90,17 @@ def tile_list_handshake_anomaly_scores_kernel(
         def load_table(a, lo, hi):
             nc.sync.dma_start(out=tw[a][:, lo:hi].bitcast(I32), in_=tab_words[a].rearrange("p t i -> p (t i)").bitcast(I32)[:, lo:hi])
 
-        def load_weights(a):
+        def load_we(a):
             nc.sync.dma_start(out=packed[a][:, 0 : 2 * H].bitcast(I32), in_=we_words[a].bitcast(I32))
+
+        def load_wd(a):
             nc.sync.dma_start(out=packed[a][:, 2 * H : 6 * H].bitcast(I32), in_=wd_words[a].rearrange("p c i -> p (c i)").bitcast(I32))
 
         nc.sync.dma_start(idx[:], offs)
         stage_rows(ts[STAGE:P, :], tab_scales)
         load_table(0, 0, T)
-        load_weights(0)
+        load_we(0)
+        load_wd(0)
         stage_rows(staged[STAGE:P, WE_AT:WD_AT], we_scales)
         stage_rows(staged[STAGE:P, WD_AT:PLANE], wd_scales)
         nc.sync.dma_start(idx2[:], offs2)
@@ -107,11 +110,11 @@ def tile_list_handshake_anomaly_scores_kernel(
         planes = [kept([P, PLANE], U8, f"plane{a}") for a in range(PASSES)]
         picked = placed([P, S], U8, "picked", PICKED_AT)
 
-        def half_of(lst, h):
-            return lst[:, h * (HALF // 16) : (h + 1) * (HALF // 16)]
-
-        def gather_words(a, h):
-            nc.vector.tensor_copy(vw[a][h][:], tw[a][:, 0:T].indirect(half_of(idx, h)))
+        def gather_words(a, h, parts=1):
+            width = HALF // parts
+            for lo in range(0, HALF, width):
+                first = h * HALF + lo
+                nc.vector.tensor_copy(vw[a][h][:, lo : lo + width], tw[a][:].indirect(idx[:, first // 16 : (first + width) // 16]))
 
         nc.vector.tensor_copy(picked[:], ts[:].indirect(idx[:]))
         nc.vector.tensor_copy(staged[STAGE:P, 0:S].bitcast(I32), picked[STAGE:P, :].bitcast(I32))
@@ -124,8 +127,9 @@ def tile_list_handshake_anomaly_scores_kernel(
         load_table(1, 0, T // 2)
         move_scales(0)
         load_table(1, T // 2, T)
-        load_weights(1)
+        load_we(1)
         move_scales(1)
+        load_wd(1)
         nc.vector.memset(pages[1][:], 0.0)
 
         gather_words(0, 0)
@@ -134,7 +138,7 @@ def tile_list_handshake_anomaly_scores_kernel(
         for a in range(PASSES):
             nc.sync.dma_start(out=wr_raw[a][:], in_=wr[512 * a : 512 * (a + 1), :].rearrange("(p j) c -> p j c", j=4))
         nc.vector.memset(pages[2][:], 0.0)
-        gather_words(1, 0)
+        gather_words(1, 0, parts=2)
         gather_words(1, 1)
 
         wgs_sb = [placed([P, 2, S], F32, f"wgs{u}", at) for u, at in enumerate((WGS0_AT, WGS1_AT))]
@@ -269,10 +273,12 @@ def tile_list_handshake_anomaly_scores_kernel(
                 )
             return acc
 
-        def empty(c, acc, i, y, grouped):
+        def empty(acc, i, y):
+            nc.scalar.copy(y[:, :, i * P : (i + 1) * P], acc[:].rearrange("p (t m) -> p t m", t=4))
+
+        def round_y(c, acc, i, y, grouped):
             cols = slice(i * P, (i + 1) * P)
-            nc.scalar.copy(y[:, :, cols], acc[:].rearrange("p (t m) -> p t m", t=4))
-            if c < 2:
+            if 2 * c + i < 5:
                 nc.scalar.copy(grouped[:, cols, :], acc[:].rearrange("p (t m) -> p m t", t=4))
             else:
                 nc.vector.tensor_copy(grouped[:, cols, :].rearrange("p (m n) t -> p m t n", n=4), y[:, :, cols].rearrange("p t (m n) -> p m t n", n=4))
@@ -324,10 +330,12 @@ def tile_list_handshake_anomaly_scores_kernel(
             y = ringed([P, 4, CHUNK], F32, "y", bufs=3)
             grouped_y = ringed([P, CHUNK, 4], BF16, "grouped_y")
             first, second = accs
-            empty(c, accs[first], first, y, grouped_y)
+            empty(accs[first], first, y)
             if c + 1 < CHUNKS:
                 round_z(c + 1)
-            empty(c, accs[second], second, y, grouped_y)
+            empty(accs[second], second, y)
+            for i in accs:
+                round_y(c, accs[i], i, y, grouped_y)
             finish(c, y, grouped_y)
         for q in range(4):
             queue = nc.sync if q % 2 == 0 else nc.scalar

@@ -56,33 +56,33 @@ def tile_list_handshake_anomaly_scores_kernel(
         def bank_tile(name, bank):
             return psum.tile([P, HALF], F32, name=name, offset=2048 * bank)
 
-        PAGE2_AT = 0
-        TW0_AT = PAGE2_AT + 8192 - LAP
-        WR_AT = PAGE2_AT + 8192
+        PAGE1_AT = 0
+        TW0_AT = PAGE1_AT + 8192 - LAP
+        WR_AT = PAGE1_AT + 8192
         WO_AT = WR_AT + 16384
         TW1_AT = WO_AT + 8192 - LAP
-        WGS0_AT = WO_AT + 8192
+        WGS_AT = WO_AT + 8192
         PICKED_AT = TW1_AT + 16384 - 512
         SECOND_AT = PICKED_AT + 1024 - LAP
         STAGED_AT = SECOND_AT + 6 * H
-        WGS1_AT = STAGED_AT + 2048 - LAP
-        HELD_AT = {1: WGS1_AT + 12288, 3: WGS1_AT + 8192}
-        MAG1_AT = WGS1_AT + 16384
-        PAGE1_AT = MAG1_AT + 2048
-        TS_AT = PAGE1_AT + 8192 - LAP
-        E6_AT = TS_AT + T
-        PAGE3_AT = E6_AT + 2048 - LAP
+        PAGE0_AT = STAGED_AT + 2048
+        TS_AT = PAGE0_AT + 8192 - LAP
+        FEAT1_AT = TS_AT + T
+        PAIR1_AT = FEAT1_AT + 2048 - LAP
+        FEAT3_AT = PAIR1_AT + 4096
+        WO_GROUPED_AT = FEAT3_AT + 2048 - LAP
         tw = [placed([P, T], U32, "tw0", TW0_AT), placed([P, T], U32, "tw1", TW1_AT)]
         ts = placed([P, T], U8, "ts", TS_AT)
         staged = placed([P, PLANE], U8, "staged", STAGED_AT)
         packed = [kept([P, 6 * H], U8, "packed0"), placed([P, 6 * H], U8, "packed1", SECOND_AT)]
-        pages = [kept([P, T2], F32, "page0")]
-        pages.extend(placed([P, T2], F32, f"page{s + 1}", at) for s, at in enumerate((PAGE1_AT, PAGE2_AT, PAGE3_AT)))
+        pages = [placed([P, T2], F32, f"page{s}", at) for s, at in enumerate((PAGE0_AT, PAGE1_AT))]
+        pages.extend(kept([P, T2], F32, f"page{s}") for s in (2, 3))
         ident = kept([P, P], F32, "ident")
 
         nc.vector.memset(ts[0:STAGE, :].bitcast(I32), 0)
         make_identity(nc, ident[:])
-        nc.vector.memset(pages[0][:], 0.0)
+        nc.vector.memset(pages[2][:], 0.0)
+        nc.vector.memset(pages[3][:], 0.0)
 
         def stage_rows(dst, src):
             nc.sync.dma_start(out=dst.bitcast(I32), in_=src.rearrange("a q c -> (a q) c").bitcast(I32))
@@ -118,6 +118,7 @@ def tile_list_handshake_anomaly_scores_kernel(
 
         nc.vector.tensor_copy(picked[:], ts[:].indirect(idx[:]))
         nc.vector.tensor_copy(staged[STAGE:P, 0:S].bitcast(I32), picked[STAGE:P, :].bitcast(I32))
+        nc.vector.memset(pages[0][:], 0.0)
 
         def move_scales(a):
             for r in range(4):
@@ -130,113 +131,101 @@ def tile_list_handshake_anomaly_scores_kernel(
         load_we(1)
         move_scales(1)
         load_wd(1)
-        nc.vector.memset(pages[1][:], 0.0)
 
         gather_words(0, 0)
         gather_words(0, 1)
+        nc.vector.memset(pages[1][:], 0.0)
         wr_raw = [placed([P, 4, H], F32, f"wr_raw{a}", WR_AT + 8192 * a) for a in range(PASSES)]
         for a in range(PASSES):
             nc.sync.dma_start(out=wr_raw[a][:], in_=wr[512 * a : 512 * (a + 1), :].rearrange("(p j) c -> p j c", j=4))
-        nc.vector.memset(pages[2][:], 0.0)
         gather_words(1, 0, parts=2)
         gather_words(1, 1)
 
-        wgs_sb = [placed([P, 2, S], F32, f"wgs{u}", at) for u, at in enumerate((WGS0_AT, WGS1_AT))]
+        wgs_sb = [[placed([P, 2, HALF], F32, f"wgs{u}{h}", WGS_AT + 4096 * (2 * u + h)) for h in range(2)] for u in range(2)]
 
-        def load_wgs(first, count):
-            u, e = divmod(first, 2)
-            rows = wgs.rearrange("(i t) j -> i t j", t=PAGES)[:, first : first + count, :]
+        def load_wgs(u, h):
+            rows = wgs.rearrange("(i t) j -> i t j", t=PAGES)[:, 2 * u : 2 * u + 2, h * HALF : (h + 1) * HALF]
             for q in (0, 2, 1, 3):
-                nc.sync.dma_start(out=wgs_sb[u][32 * q : 32 * (q + 1), e : e + count], in_=rows)
+                nc.sync.dma_start(out=wgs_sb[u][h][32 * q : 32 * (q + 1)], in_=rows)
 
+        load_wgs(0, 0)
         load_wgs(0, 1)
-        load_wgs(1, 1)
         wo_raw = placed([P, 4, N], F32, "wo_raw", WO_AT)
         nc.sync.dma_start(out=wo_raw[:], in_=wo.rearrange("(p j) n -> p j n", j=4))
-        load_wgs(2, 2)
+        load_wgs(1, 0)
+        load_wgs(1, 1)
 
-        wo_grouped = placed([P, 4, P, 4], BF16, "wo_grouped", HELD_AT[3])
-        woc = kept([P, N], U32, "woc")
+        woc = placed([P, N], U32, "woc", WO_GROUPED_AT + 4096)
         wos = kept([P, N], U8, "wos")
+        wrc = [kept([P, PASSES * 2 * P], U32, f"wrc{u}") for u in range(2)]
+        wrs = [kept([P, PASSES * 2 * P], U8, f"wrs{u}") for u in range(2)]
 
-        wr_grouped = [kept([P, 2, PASSES, P, 4], BF16, "wr_grouped0"), placed([P, 2, PASSES, P, 4], BF16, "wr_grouped1", HELD_AT[1])]
-        wrc = [kept([P, 2, PASSES, P], U32, "wrc0"), placed([P, 2, PASSES, P], U32, "wrc1", MAG1_AT)]
-        wrs = [kept([P, 2, PASSES, P], U8, f"wrs{u}") for u in range(2)]
-
-        def group_wr(u, a, copy):
-            copy(wr_grouped[u][:, :, a].rearrange("p e i j -> p i j e"),
+        def group_wr(u, a, grouped, copy):
+            copy(grouped.rearrange("p (e i j) -> p i j e", e=2, j=4),
                  wr_raw[a][:].rearrange("p j (i t) -> p i j t", t=4)[:, :, :, 2 * u : 2 * u + 2])
 
-        def quantize_wr(first, count):
-            u, e = divmod(first, 2)
-            nc.vector.quantize_mx(
-                out=wrc[u][:, e : e + count].rearrange("p t a i -> p (t a i)").bitcast(FP8X4),
-                scales=wrs[u][:, e : e + count].rearrange("p t a i -> p (t a i)"),
-                in_=wr_grouped[u][:, e : e + count].rearrange("p e a i j -> p (e a i j)"),
+        def quantize_wr(u, first, count, grouped):
+            nc.vector.quantize_mx(out=wrc[u][:, first : first + count].bitcast(FP8X4), scales=wrs[u][:, first : first + count], in_=grouped)
+
+        def table_pass(out, jt, a, codes, scales, start, stop):
+            h, lo = divmod(jt * P, HALF)
+            nc.tensor.matmul_mx(
+                out=out, lhsT=vw[a][h][:, lo : lo + P].bitcast(FP8X4), lhsT_scale=planes[a][:, jt * P : (jt + 1) * P],
+                rhs=codes, rhs_scale=scales, start=start, stop=stop,
             )
 
-        def product(out, jt, codes_of, scale_of):
-            h, lo = divmod(jt * P, HALF)
-            for a in range(PASSES):
-                nc.tensor.matmul_mx(
-                    out=out, lhsT=vw[a][h][:, lo : lo + P].bitcast(FP8X4), lhsT_scale=planes[a][:, jt * P : (jt + 1) * P],
-                    rhs=codes_of(a), rhs_scale=scale_of(a), start=(a == 0), stop=(a == PASSES - 1),
-                )
-
-        def add_turned(bank, blocks, start, stop):
-            for i, block in enumerate(blocks):
-                nc.tensor.matmul(bank[:, i * P : (i + 1) * P], block, ident[:], start=(start and i == 0),
-                                 stop=(stop and i == len(blocks) - 1), is_transpose=True)
-
-        recs = [kept([P, PAGES, P], F32, f"rec{jt}") for jt in range(S // P)]
+        shared = kept([P, 3 * HALF], F32, "shared")
+        first_pair = shared[:, HALF - 16 : 3 * HALF - 16].bitcast(BF16)
+        recs = [kept([P, PAGES, P], F32, f"rec{jt}")[:] for jt in (0, 1, 2, 3, 4)]
+        recs.extend(shared[:, at : at + HALF].rearrange("p (t i) -> p t i", t=PAGES) for at in (HALF, 0))
+        recs.append(kept([P, PAGES, P], F32, "rec7")[:])
 
         def dealt(bank):
             return bank[:].rearrange("p (i t) -> p t i", t=PAGES)
 
         def reconstruct(jt, bank_e, bank_d):
             acc_e = bank_tile(f"acc_e{jt}", bank_e)
-            product(acc_e[:], jt, lambda a: packed[a][:, 0 : 2 * H].bitcast(FP4X4), lambda a: planes[a][:, WE_AT:WD_AT])
+            for a in range(PASSES):
+                table_pass(acc_e[:], jt, a, packed[a][:, 0 : 2 * H].bitcast(FP4X4), planes[a][:, WE_AT:WD_AT], a == 0, a == 1)
             acc_d = bank_tile(f"acc_d{jt}", bank_d)
-            product(acc_d[:], jt, lambda a: packed[a][:, 2 * H : 6 * H].bitcast(FP8X4), lambda a: planes[a][:, WD_AT:PLANE])
-            e = placed([P, PAGES, P], F32, "e6", E6_AT) if jt == 6 else ringed([P, PAGES, P], F32, "e", bufs=4)
+            for a in range(PASSES):
+                table_pass(acc_d[:], jt, a, packed[a][:, 2 * H : 6 * H].bitcast(FP8X4), planes[a][:, WD_AT:PLANE], a == 0, a == 1)
+            e = ringed([P, PAGES, P], F32, "e", bufs=4)
             nc.scalar.activation(e[:], dealt(acc_e), ACT.Tanh, scale=-1.0)
-            nc.vector.tensor_tensor(recs[jt][:], dealt(acc_d), e[:], ALU.mult)
+            nc.vector.tensor_tensor(recs[jt], dealt(acc_d), e[:], ALU.mult)
 
-        units = [(2 * u + e, h) for u in range(2) for h in range(2) for e in range(2)]
         RUN = PAGES * CHUNK
         work = kept([P, CHUNKS * RUN + 384], F32, "work")
 
-        def residual(u, parts=1):
-            t, h = units[u]
-            feat_bank, sum_bank = (4, 6) if u % 2 else (0, 2)
-            acc = bank_tile(f"acc_r{u}", feat_bank)
-            for i in range(4):
-                product(acc[:, i * P : (i + 1) * P], 4 * h + i, lambda a: wrc[t // 2][:, t % 2, a].bitcast(FP8X4), lambda a: wrs[t // 2][:, t % 2, a])
-            feat = placed([P, HALF], F32, f"feat{u}", HELD_AT[u]) if u in HELD_AT else ringed([P, HALF], F32, "feat", bufs=3)
-            nc.scalar.copy(feat[:], acc[:])
-            out = []
-            width = HALF // parts
-            if u + 1 == len(units):
-                mag = work[:, RUN : RUN + HALF]
-            elif u == 1:
-                mag = placed([P, HALF], F32, "mag1", MAG1_AT)[:]
+        def residual(g, first_page, count, feat_bank, sum_bank, feat):
+            u, e0 = divmod(first_page, 2)
+            width = count * P
+            name = f"{g}_{first_page}"
+            acc = bank_tile("acc_r" + name, feat_bank)
+            for a in range(PASSES):
+                at = a * 2 * P + e0 * P
+                for k in range(2):
+                    table_pass(acc[:, k * width : (k + 1) * width], 2 * g + k, a, wrc[u][:, at : at + width].bitcast(FP8X4),
+                               wrs[u][:, at : at + width], (a, k) == (0, 0), (a, k) == (1, 1))
+            nc.scalar.copy(feat, acc[:, 0 : 2 * width])
+            bank = bank_tile("acc_h" + name, sum_bank)
+            places = [(e, k) for e in range(count) for k in range(2)]
+            for n, (e, k) in enumerate(places):
+                nc.tensor.matmul(bank[:, n * P : (n + 1) * P], recs[2 * g + k][:, first_page + e, :], ident[:], start=(n == 0), stop=False, is_transpose=True)
+            for n, (e, k) in enumerate(places):
+                at = k * width + e * P
+                nc.tensor.matmul(bank[:, n * P : (n + 1) * P], feat[:, at : at + P], ident[:], start=False, stop=(n + 1 == len(places)), is_transpose=True)
+            lo = g % 2 * CHUNK
+            if (u, g // 2) == (1, 0):
+                for e in range(2):
+                    nc.scalar.activation(third[e][:, lo : lo + CHUNK], bank[:, e * CHUNK : (e + 1) * CHUNK], ACT.Abs)
             else:
-                mag = kept([P, HALF], F32, f"mag{u}")[:]
-            for part in range(parts):
-                blocks = range(part * 4 // parts, (part + 1) * 4 // parts)
-                bank = bank_tile(f"acc_h{u}_{part}", sum_bank - 2 * part)
-                add_turned(bank, [recs[4 * h + i][:, t, :] for i in blocks], True, False)
-                add_turned(bank, [feat[:, i * P : (i + 1) * P] for i in blocks], False, True)
-                nc.scalar.activation(mag[:, part * width : (part + 1) * width], bank[:, 0:width], ACT.Abs)
-                out.append((part * width, width, mag))
-            return out
+                nc.scalar.activation(mags[u, g // 2][:, e0 : e0 + count, lo : lo + CHUNK], bank[:, 0 : 2 * width].rearrange("p (e j) -> p e j", e=count), ACT.Abs)
 
-        def scatter(u, parts):
-            t, h = units[u]
-            for lo, width, mag in parts:
-                first = h * HALF + lo
-                nc.vector.tensor_tensor(pages[t][:].indirect(idx2[:, first // 16 : (first + width) // 16]),
-                                        mag[:, lo : lo + width], wgs_sb[t // 2][:, t % 2, first : first + width], ALU.mult)
+        def scatter(first, width, t):
+            h, lo = divmod(first, HALF)
+            nc.vector.tensor_tensor(pages[t][:].indirect(idx2[:, first // 16 : (first + width) // 16]),
+                                    third[t % 2][:] if (t // 2, h) == (1, 0) else mags[t // 2, h][:, t % 2, lo : lo + width], wgs_sb[t // 2][h][:, t % 2, lo : lo + width], ALU.mult)
 
         yc = kept([P, M], U32, "yc")
         ys = kept([P, M], U8, "ys")
@@ -289,33 +278,47 @@ def tile_list_handshake_anomaly_scores_kernel(
             nc.vector.quantize_mx(out=yc[:, cols].bitcast(FP8X4), scales=ys[:, cols], in_=grouped[:].rearrange("p m t -> p (m t)"))
             (nc.sync if c + 1 < CHUNKS else nc.scalar).dma_start(out=out_words[:, cols], in_=yc[:, cols].bitcast(I32))
 
-        for jt in range(2):
+        for jt in range(4):
             reconstruct(jt, 2 * jt, 2 * jt + 1)
-        for a in range(PASSES):
-            group_wr(0, a, nc.vector.tensor_copy)
-        quantize_wr(0, 1)
-        for jt in range(2, 4):
-            reconstruct(jt, 2 * jt, 2 * jt + 1)
-        quantize_wr(1, 1)
-        for jt in range(4, 7):
-            reconstruct(jt, 2 * jt - 8, 2 * jt - 7)
-        ready = [residual(0, parts=2)]
-        reconstruct(7, 6, 7)
-        nc.vector.memset(pages[3][:], 0.0)
-        ready.append(residual(1))
-        for a in range(PASSES):
-            group_wr(1, a, nc.scalar.copy)
+        group_wr(0, 0, first_pair[:, 0 : 8 * P], nc.vector.tensor_copy)
+        reconstruct(4, 0, 1)
+        group_wr(0, 1, first_pair[:, 8 * P : 16 * P], nc.vector.tensor_copy)
+        quantize_wr(0, 0, 3 * P, first_pair[:, 0 : 12 * P])
+        quantize_wr(0, 3 * P, P, first_pair[:, 12 * P : 16 * P])
+        mags = {(u, h): kept([P, 2, HALF], F32, f"mag{u}{h}")[:] for u, h in ((0, 0), (0, 1))}
+        third = (placed([P, HALF], F32, "mag_page2", WO_GROUPED_AT + 4096), kept([P, HALF], F32, "mag_page3"))
+        mags[1, 1] = work[:, RUN - HALF : RUN + HALF].rearrange("p (e j) -> p e j", e=2)
+        for e in range(2):
+            feat = ringed([P, CHUNK], F32, "feat_first")
+            residual(0, e, 1, 4 + 2 * e, 5 + 2 * e, feat[:])
+            scatter(0, CHUNK, e)
+        reconstruct(5, 2, 3)
+        reconstruct(6, 0, 1)
+        reconstruct(7, 5, 7)
         tol_sb = placed([P, PAGES, M], F32, "tol_sb", WR_AT)
-        nc.sync.dma_start(out=tol_sb[:], in_=tol.rearrange("(p t) m -> p t m", t=PAGES))
-        ready.extend(residual(u) for u in range(2, 4))
-        nc.scalar.copy(wo_grouped[:].rearrange("p t i j -> p i j t"), wo_raw[:].rearrange("p j (i t) -> p i j t", t=4))
-        for u in range(len(units)):
-            scatter(u, ready[u])
-            if u == 1:
-                quantize_wr(2, 2)
-                ready.extend(residual(later) for later in range(4, len(units)))
-            if u == 3:
-                nc.vector.quantize_mx(out=woc[:].bitcast(FP8X4), scales=wos[:], in_=wo_grouped[:].rearrange("p t i j -> p (t i j)"))
+        for n, (u, g) in enumerate((u, g) for u in range(2) for g in range(4)):
+            if n == 0:
+                continue
+            if n in (1, 5):
+                feat = placed([P, HALF], F32, f"feat{n}", FEAT1_AT if n == 1 else FEAT3_AT)
+            else:
+                feat = ringed([P, HALF], F32, "feat", bufs=3)
+            residual(g, 2 * u, 2, *((2, 4), (0, 6), (3, 1))[(n - 1) % 3], feat[:])
+            for e in range(2):
+                if u == 0:
+                    scatter(g * CHUNK, CHUNK, e)
+                elif g % 2:
+                    scatter(g // 2 * HALF, HALF, 2 * u + e)
+            if n == 1:
+                pair1 = placed([P, 16 * P], BF16, "pair1", PAIR1_AT)
+                for a in range(PASSES):
+                    group_wr(1, a, pair1[:, 8 * P * a : 8 * P * (a + 1)], nc.scalar.copy)
+                quantize_wr(1, 0, 4 * P, pair1[:])
+                nc.sync.dma_start(out=tol_sb[:], in_=tol.rearrange("(p t) m -> p t m", t=PAGES))
+            if n == 6:
+                wo_grouped = placed([P, 4, P, 4], BF16, "wo_grouped", WO_GROUPED_AT)
+                nc.scalar.copy(wo_grouped[:].rearrange("p t i j -> p i j t"), wo_raw[:].rearrange("p j (i t) -> p i j t", t=4))
+        nc.vector.quantize_mx(out=woc[:].bitcast(FP8X4), scales=wos[:], in_=wo_grouped[:].rearrange("p t i j -> p (t i j)"))
         for t in range(PAGES):
             excess(0, t)
         round_z(0)
@@ -333,10 +336,22 @@ def tile_list_handshake_anomaly_scores_kernel(
             empty(accs[first], first, y)
             if c + 1 < CHUNKS:
                 round_z(c + 1)
+            else:
+                nc.scalar.copy(grouped_y[:, second * P : (second + 1) * P, :], accs[second][:].rearrange("p (t m) -> p m t", t=4))
             empty(accs[second], second, y)
-            for i in accs:
-                round_y(c, accs[i], i, y, grouped_y)
-            finish(c, y, grouped_y)
+            if c + 1 < CHUNKS:
+                for i in accs:
+                    round_y(c, accs[i], i, y, grouped_y)
+                finish(c, y, grouped_y)
+            else:
+                for i in accs:
+                    cols = slice(c * CHUNK + i * P, c * CHUNK + (i + 1) * P)
+                    nc.sync.dma_start(out=out_rows[:, :, cols], in_=y[:, :, i * P : (i + 1) * P])
+                    if i == first:
+                        round_y(c, accs[i], i, y, grouped_y)
+                    nc.vector.quantize_mx(out=yc[:, cols].bitcast(FP8X4), scales=ys[:, cols], in_=grouped_y[:, i * P : (i + 1) * P].rearrange("p m t -> p (m t)"))
+                cols = slice(c * CHUNK, M)
+                nc.scalar.dma_start(out=out_words[:, cols], in_=yc[:, cols].bitcast(I32))
         for q in range(4):
             queue = nc.sync if q % 2 == 0 else nc.scalar
             queue.dma_start(out=out_2[0, 4 * q : 4 * q + 4, :].bitcast(I32), in_=ys[32 * q : 32 * q + 4, :].bitcast(I32))

@@ -25,7 +25,8 @@ CHUNK = 256
 CHUNKS = M // CHUNK
 STAGE = 96
 WE_AT, WD_AT, PLANE = S, S + H, S + 2 * H
-LAP = 64
+GROUP = 256
+GROUPS = S // GROUP
 
 
 def tile_list_handshake_anomaly_scores_kernel(
@@ -56,33 +57,22 @@ def tile_list_handshake_anomaly_scores_kernel(
         def bank_tile(name, bank):
             return psum.tile([P, HALF], F32, name=name, offset=2048 * bank)
 
-        PAGE1_AT = 0
-        TW0_AT = PAGE1_AT + 8192 - LAP
-        WR_AT = PAGE1_AT + 8192
-        WO_AT = WR_AT + 16384
-        TW1_AT = WO_AT + 8192 - LAP
-        WGS_AT = WO_AT + 8192
-        PICKED_AT = TW1_AT + 16384 - 512
-        SECOND_AT = PICKED_AT + 1024 - LAP
-        STAGED_AT = SECOND_AT + 6 * H
-        PAGE0_AT = STAGED_AT + 2048
-        TS_AT = PAGE0_AT + 8192 - LAP
-        FEAT1_AT = TS_AT + T
-        PAIR1_AT = FEAT1_AT + 2048 - LAP
-        FEAT3_AT = PAIR1_AT + 4096
-        WO_GROUPED_AT = FEAT3_AT + 2048 - LAP
+        RUN = PAGES * CHUNK
+        TW0_AT = 0
+        TW1_AT = TW0_AT + 4 * T
+        WR_AT = TW1_AT + 4 * (CHUNKS * RUN + 384)
         tw = [placed([P, T], U32, "tw0", TW0_AT), placed([P, T], U32, "tw1", TW1_AT)]
-        ts = placed([P, T], U8, "ts", TS_AT)
-        staged = placed([P, PLANE], U8, "staged", STAGED_AT)
-        packed = [kept([P, 6 * H], U8, "packed0"), placed([P, 6 * H], U8, "packed1", SECOND_AT)]
-        pages = [placed([P, T2], F32, f"page{s}", at) for s, at in enumerate((PAGE0_AT, PAGE1_AT))]
-        pages.extend(kept([P, T2], F32, f"page{s}") for s in (2, 3))
+        ts = kept([P, T], U8, "ts")
+        staged = kept([P, PLANE], U8, "staged")
+        packed = [kept([P, 6 * H], U8, f"packed{a}") for a in range(PASSES)]
+        pages = [kept([P, T2], F32, f"page{t}") for t in range(PAGES)]
         ident = kept([P, P], F32, "ident")
+        wr_raw = [placed([P, 4, H], F32, f"wr_raw{a}", WR_AT + 8192 * a) for a in range(PASSES)]
 
         nc.vector.memset(ts[0:STAGE, :].bitcast(I32), 0)
         make_identity(nc, ident[:])
-        nc.vector.memset(pages[2][:], 0.0)
-        nc.vector.memset(pages[3][:], 0.0)
+        nc.vector.memset(pages[0][:], 0.0)
+        nc.vector.memset(pages[1][:], 0.0)
 
         def stage_rows(dst, src):
             nc.sync.dma_start(out=dst.bitcast(I32), in_=src.rearrange("a q c -> (a q) c").bitcast(I32))
@@ -99,16 +89,17 @@ def tile_list_handshake_anomaly_scores_kernel(
         nc.sync.dma_start(idx[:], offs)
         stage_rows(ts[STAGE:P, :], tab_scales)
         load_table(0, 0, T)
-        load_we(0)
-        load_wd(0)
         stage_rows(staged[STAGE:P, WE_AT:WD_AT], we_scales)
         stage_rows(staged[STAGE:P, WD_AT:PLANE], wd_scales)
+        for a in range(PASSES):
+            nc.sync.dma_start(out=wr_raw[a][:], in_=wr[512 * a : 512 * (a + 1), :].rearrange("(p j) c -> p j c", j=4))
         nc.sync.dma_start(idx2[:], offs2)
-        nc.sync.dma_start(idx3[:], offs3)
+        load_table(1, 0, T // 2)
+        load_we(0)
 
         vw = [[kept([P, HALF], U32, f"vw{a}{h}") for h in range(2)] for a in range(PASSES)]
         planes = [kept([P, PLANE], U8, f"plane{a}") for a in range(PASSES)]
-        picked = placed([P, S], U8, "picked", PICKED_AT)
+        picked = kept([P, S], U8, "picked")
 
         def gather_words(a, h, parts=1):
             width = HALF // parts
@@ -118,15 +109,15 @@ def tile_list_handshake_anomaly_scores_kernel(
 
         nc.vector.tensor_copy(picked[:], ts[:].indirect(idx[:]))
         nc.vector.tensor_copy(staged[STAGE:P, 0:S].bitcast(I32), picked[STAGE:P, :].bitcast(I32))
-        nc.vector.memset(pages[0][:], 0.0)
+        nc.vector.memset(pages[2][:], 0.0)
 
         def move_scales(a):
             for r in range(4):
                 rows = staged[STAGE + 16 * a + r : STAGE + 16 * (a + 1) : 4, :]
                 nc.sync.dma_start(out=planes[a][r:P:32, :].bitcast(I32), in_=rows.bitcast(I32))
 
-        load_table(1, 0, T // 2)
         move_scales(0)
+        load_wd(0)
         load_table(1, T // 2, T)
         load_we(1)
         move_scales(1)
@@ -134,98 +125,128 @@ def tile_list_handshake_anomaly_scores_kernel(
 
         gather_words(0, 0)
         gather_words(0, 1)
-        nc.vector.memset(pages[1][:], 0.0)
-        wr_raw = [placed([P, 4, H], F32, f"wr_raw{a}", WR_AT + 8192 * a) for a in range(PASSES)]
-        for a in range(PASSES):
-            nc.sync.dma_start(out=wr_raw[a][:], in_=wr[512 * a : 512 * (a + 1), :].rearrange("(p j) c -> p j c", j=4))
+        nc.vector.memset(pages[3][:], 0.0)
+
+        def by_pages(raw, name):
+            grouped = ringed([P, 4, P, 4], BF16, "grouped_w")
+            nc.scalar.copy(grouped[:].rearrange("p t i j -> p i j t"), raw[:].rearrange("p j (i t) -> p i j t", t=4))
+            codes = kept([P, H], U32, name + "_codes")
+            scales = kept([P, H], U8, name + "_scales")
+            nc.vector.quantize_mx(out=codes[:].bitcast(FP8X4), scales=scales[:], in_=grouped[:].rearrange("p t i j -> p (t i j)"))
+            return codes, scales
+
+        wr_mx = [by_pages(wr_raw[a], f"wr{a}") for a in range(PASSES)]
         gather_words(1, 0, parts=2)
-        gather_words(1, 1)
 
-        wgs_sb = [[placed([P, 2, HALF], F32, f"wgs{u}{h}", WGS_AT + 4096 * (2 * u + h)) for h in range(2)] for u in range(2)]
-
-        def load_wgs(u, h):
-            rows = wgs.rearrange("(i t) j -> i t j", t=PAGES)[:, 2 * u : 2 * u + 2, h * HALF : (h + 1) * HALF]
+        wgs_sb = [kept([P, PAGES, GROUP], F32, f"wgs{g}") for g in range(GROUPS)]
+        for g in range(GROUPS):
+            rows = wgs.rearrange("(i t) j -> i t j", t=PAGES)[:, :, g * GROUP : (g + 1) * GROUP]
             for q in (0, 2, 1, 3):
-                nc.sync.dma_start(out=wgs_sb[u][h][32 * q : 32 * (q + 1)], in_=rows)
-
-        load_wgs(0, 0)
-        load_wgs(0, 1)
-        wo_raw = placed([P, 4, N], F32, "wo_raw", WO_AT)
+                nc.sync.dma_start(out=wgs_sb[g][32 * q : 32 * (q + 1)], in_=rows)
+        wo_raw = placed([P, 4, N], F32, "wo_raw", WR_AT)
         nc.sync.dma_start(out=wo_raw[:], in_=wo.rearrange("(p j) n -> p j n", j=4))
-        load_wgs(1, 0)
-        load_wgs(1, 1)
+        tol_sb = placed([P, PAGES, M], F32, "tol_sb", TW0_AT)
+        nc.sync.dma_start(out=tol_sb[:], in_=tol.rearrange("(p t) m -> p t m", t=PAGES))
+        nc.sync.dma_start(idx3[:], offs3)
 
-        woc = placed([P, N], U32, "woc", WO_GROUPED_AT + 4096)
-        wos = kept([P, N], U8, "wos")
-        wrc = [kept([P, PASSES * 2 * P], U32, f"wrc{u}") for u in range(2)]
-        wrs = [kept([P, PASSES * 2 * P], U8, f"wrs{u}") for u in range(2)]
-
-        def group_wr(u, a, grouped, copy):
-            copy(grouped.rearrange("p (e i j) -> p i j e", e=2, j=4),
-                 wr_raw[a][:].rearrange("p j (i t) -> p i j t", t=4)[:, :, :, 2 * u : 2 * u + 2])
-
-        def quantize_wr(u, first, count, grouped):
-            nc.vector.quantize_mx(out=wrc[u][:, first : first + count].bitcast(FP8X4), scales=wrs[u][:, first : first + count], in_=grouped)
-
-        def table_pass(out, jt, a, codes, scales, start, stop):
+        def product(name, jt, bank, operands):
+            acc = bank_tile(f"{name}{jt}", bank)
             h, lo = divmod(jt * P, HALF)
-            nc.tensor.matmul_mx(
-                out=out, lhsT=vw[a][h][:, lo : lo + P].bitcast(FP8X4), lhsT_scale=planes[a][:, jt * P : (jt + 1) * P],
-                rhs=codes, rhs_scale=scales, start=start, stop=stop,
-            )
+            for a, (codes, scales) in enumerate(operands):
+                nc.tensor.matmul_mx(
+                    out=acc[:], lhsT=vw[a][h][:, lo : lo + P].bitcast(FP8X4), lhsT_scale=planes[a][:, jt * P : (jt + 1) * P],
+                    rhs=codes, rhs_scale=scales, start=a == 0, stop=a == 1,
+                )
+            return acc
 
-        shared = kept([P, 3 * HALF], F32, "shared")
-        first_pair = shared[:, HALF - 16 : 3 * HALF - 16].bitcast(BF16)
-        recs = [kept([P, PAGES, P], F32, f"rec{jt}")[:] for jt in (0, 1, 2, 3, 4)]
-        recs.extend(shared[:, at : at + HALF].rearrange("p (t i) -> p t i", t=PAGES) for at in (HALF, 0))
-        recs.append(kept([P, PAGES, P], F32, "rec7")[:])
+        we_mx = [(packed[a][:, 0 : 2 * H].bitcast(FP4X4), planes[a][:, WE_AT:WD_AT]) for a in range(PASSES)]
+        wd_mx = [(packed[a][:, 2 * H : 6 * H].bitcast(FP8X4), planes[a][:, WD_AT:PLANE]) for a in range(PASSES)]
+        wr_mx = [(codes[:].bitcast(FP8X4), scales[:]) for codes, scales in wr_mx]
 
         def dealt(bank):
             return bank[:].rearrange("p (i t) -> p t i", t=PAGES)
 
-        def reconstruct(jt, bank_e, bank_d):
-            acc_e = bank_tile(f"acc_e{jt}", bank_e)
-            for a in range(PASSES):
-                table_pass(acc_e[:], jt, a, packed[a][:, 0 : 2 * H].bitcast(FP4X4), planes[a][:, WE_AT:WD_AT], a == 0, a == 1)
-            acc_d = bank_tile(f"acc_d{jt}", bank_d)
-            for a in range(PASSES):
-                table_pass(acc_d[:], jt, a, packed[a][:, 2 * H : 6 * H].bitcast(FP8X4), planes[a][:, WD_AT:PLANE], a == 0, a == 1)
-            e = ringed([P, PAGES, P], F32, "e", bufs=4)
-            nc.scalar.activation(e[:], dealt(acc_e), ACT.Tanh, scale=-1.0)
-            nc.vector.tensor_tensor(recs[jt], dealt(acc_d), e[:], ALU.mult)
+        def paged(bank):
+            return bank[:].rearrange("p (t i) -> p t i", t=PAGES)
 
-        RUN = PAGES * CHUNK
-        work = kept([P, CHUNKS * RUN + 384], F32, "work")
+        def rows_tile(name, bufs):
+            return ringed([P, PAGES, P], F32, name, bufs=bufs)
 
-        def residual(g, first_page, count, feat_bank, sum_bank, feat):
-            u, e0 = divmod(first_page, 2)
-            width = count * P
-            name = f"{g}_{first_page}"
-            acc = bank_tile("acc_r" + name, feat_bank)
-            for a in range(PASSES):
-                at = a * 2 * P + e0 * P
-                for k in range(2):
-                    table_pass(acc[:, k * width : (k + 1) * width], 2 * g + k, a, wrc[u][:, at : at + width].bitcast(FP8X4),
-                               wrs[u][:, at : at + width], (a, k) == (0, 0), (a, k) == (1, 1))
-            nc.scalar.copy(feat, acc[:, 0 : 2 * width])
-            bank = bank_tile("acc_h" + name, sum_bank)
+        def magnitudes(g, first, count, bank, recs, feats):
+            acc = bank_tile(f"acc_h{g}_{first}", bank)
             places = [(e, k) for e in range(count) for k in range(2)]
             for n, (e, k) in enumerate(places):
-                nc.tensor.matmul(bank[:, n * P : (n + 1) * P], recs[2 * g + k][:, first_page + e, :], ident[:], start=(n == 0), stop=False, is_transpose=True)
+                nc.tensor.matmul(acc[:, n * P : (n + 1) * P], feats[k][:, first + e, :], ident[:], start=(n == 0), stop=False, is_transpose=True)
             for n, (e, k) in enumerate(places):
-                at = k * width + e * P
-                nc.tensor.matmul(bank[:, n * P : (n + 1) * P], feat[:, at : at + P], ident[:], start=False, stop=(n + 1 == len(places)), is_transpose=True)
-            lo = g % 2 * CHUNK
-            if (u, g // 2) == (1, 0):
-                for e in range(2):
-                    nc.scalar.activation(third[e][:, lo : lo + CHUNK], bank[:, e * CHUNK : (e + 1) * CHUNK], ACT.Abs)
-            else:
-                nc.scalar.activation(mags[u, g // 2][:, e0 : e0 + count, lo : lo + CHUNK], bank[:, 0 : 2 * width].rearrange("p (e j) -> p e j", e=count), ACT.Abs)
+                nc.tensor.matmul(acc[:, n * P : (n + 1) * P], recs[k][:, first + e, :], ident[:], start=False, stop=(n + 1 == len(places)), is_transpose=True)
+            mag = ringed([P, 2, GROUP], F32, "mag", bufs=4)
+            nc.scalar.activation(mag[:, 0:count, :], acc[:, 0 : count * GROUP].rearrange("p (e j) -> p e j", e=count), ACT.Abs)
+            return mag
 
-        def scatter(first, width, t):
-            h, lo = divmod(first, HALF)
-            nc.vector.tensor_tensor(pages[t][:].indirect(idx2[:, first // 16 : (first + width) // 16]),
-                                    third[t % 2][:] if (t // 2, h) == (1, 0) else mags[t // 2, h][:, t % 2, lo : lo + width], wgs_sb[t // 2][h][:, t % 2, lo : lo + width], ALU.mult)
+        def offsets2(g):
+            return idx2[:, g * GROUP // 16 : (g + 1) * GROUP // 16]
+
+        def weigh_and_put(g, first, count, mag, at, engine):
+            weighted = ringed([P, 2, GROUP], F32, "weighted", bufs=6)
+            engine.tensor_tensor(weighted[:, 0:count, :], mag[:, at : at + count, :], wgs_sb[g][:, first : first + count, :], ALU.mult)
+            for e in range(count):
+                nc.vector.tensor_copy(pages[first + e][:].indirect(offsets2(g)), weighted[:, e, :])
+
+        def put_fused(g, first, mag):
+            for e in range(2):
+                nc.vector.tensor_tensor(pages[first + e][:].indirect(offsets2(g)), mag[:, e, :], wgs_sb[g][:, first + e, :], ALU.mult)
+
+        acc_e = [product("acc_e", k, k, we_mx) for k in range(2)]
+        acc_c = [product("acc_c", k, 2 + k, wr_mx) for k in range(2)]
+        acc_d = [product("acc_d", k, 4 + k, wd_mx) for k in range(2)]
+        es = [rows_tile("e", 4) for k in range(2)]
+        feats = [rows_tile("feat", 4) for k in range(2)]
+        recs = [rows_tile("rec", 4) for k in range(2)]
+        for part in (slice(0, 1), slice(1, PAGES)):
+            for k in range(2):
+                nc.scalar.activation(es[k][:, part, :], dealt(acc_e[k])[:, part, :], ACT.Tanh, scale=-1.0)
+            for k in range(2):
+                nc.scalar.copy(feats[k][:, part, :], paged(acc_c[k])[:, part, :])
+            for k in range(2):
+                nc.vector.tensor_tensor(recs[k][:, part, :], dealt(acc_d[k])[:, part, :], es[k][:, part, :], ALU.mult)
+            if part.start == 0:
+                mag = magnitudes(0, 0, 1, 6, recs, feats)
+                gather_words(1, 1)
+                weigh_and_put(0, 0, 1, mag, 0, nc.vector)
+        weigh_and_put(0, 1, 1, magnitudes(0, 1, 1, 0, recs, feats), 0, nc.gpsimd)
+        weigh_and_put(0, 2, 2, magnitudes(0, 2, 2, 1, recs, feats), 0, nc.gpsimd)
+
+        for g in range(1, GROUPS):
+            feats, recs = [], []
+            for k in range(2):
+                jt = 2 * g + k
+                acc_e = product("acc_e", jt, 7 - k, we_mx)
+                acc_d = product("acc_d", jt, 4 + k, wd_mx)
+                acc_c = product("acc_c", jt, 2 + k, wr_mx)
+                e = rows_tile("e", 4)
+                nc.scalar.activation(e[:], dealt(acc_e), ACT.Tanh, scale=-1.0)
+                rec = rows_tile("rec", 4)
+                if jt == 2:
+                    nc.vector.tensor_tensor(rec[:], dealt(acc_d), e[:], ALU.mult)
+                else:
+                    decoded = rows_tile("decoded", 3)
+                    nc.scalar.copy(decoded[:], dealt(acc_d))
+                    nc.gpsimd.tensor_tensor(rec[:], decoded[:], e[:], ALU.mult)
+                feat = rows_tile("feat", 4)
+                nc.scalar.copy(feat[:], paged(acc_c))
+                recs.append(rec)
+                feats.append(feat)
+            for u in range(2):
+                mag = magnitudes(g, 2 * u, 2, u, recs, feats)
+                if g + 1 == GROUPS:
+                    put_fused(g, 2 * u, mag)
+                elif u == 0:
+                    for e in range(2):
+                        weigh_and_put(g, e, 1, mag, e, nc.gpsimd)
+                else:
+                    weigh_and_put(g, 2, 2, mag, 0, nc.gpsimd)
+        woc, wos = by_pages(wo_raw, "wo")
+        work = placed([P, CHUNKS * RUN + 384], F32, "work", TW1_AT)
 
         yc = kept([P, M], U32, "yc")
         ys = kept([P, M], U8, "ys")
@@ -278,47 +299,6 @@ def tile_list_handshake_anomaly_scores_kernel(
             nc.vector.quantize_mx(out=yc[:, cols].bitcast(FP8X4), scales=ys[:, cols], in_=grouped[:].rearrange("p m t -> p (m t)"))
             (nc.sync if c + 1 < CHUNKS else nc.scalar).dma_start(out=out_words[:, cols], in_=yc[:, cols].bitcast(I32))
 
-        for jt in range(4):
-            reconstruct(jt, 2 * jt, 2 * jt + 1)
-        group_wr(0, 0, first_pair[:, 0 : 8 * P], nc.vector.tensor_copy)
-        reconstruct(4, 0, 1)
-        group_wr(0, 1, first_pair[:, 8 * P : 16 * P], nc.vector.tensor_copy)
-        quantize_wr(0, 0, 3 * P, first_pair[:, 0 : 12 * P])
-        quantize_wr(0, 3 * P, P, first_pair[:, 12 * P : 16 * P])
-        mags = {(u, h): kept([P, 2, HALF], F32, f"mag{u}{h}")[:] for u, h in ((0, 0), (0, 1))}
-        third = (placed([P, HALF], F32, "mag_page2", WO_GROUPED_AT + 4096), kept([P, HALF], F32, "mag_page3"))
-        mags[1, 1] = work[:, RUN - HALF : RUN + HALF].rearrange("p (e j) -> p e j", e=2)
-        for e in range(2):
-            feat = ringed([P, CHUNK], F32, "feat_first")
-            residual(0, e, 1, 4 + 2 * e, 5 + 2 * e, feat[:])
-            scatter(0, CHUNK, e)
-        reconstruct(5, 2, 3)
-        reconstruct(6, 0, 1)
-        reconstruct(7, 5, 7)
-        tol_sb = placed([P, PAGES, M], F32, "tol_sb", WR_AT)
-        for n, (u, g) in enumerate((u, g) for u in range(2) for g in range(4)):
-            if n == 0:
-                continue
-            if n in (1, 5):
-                feat = placed([P, HALF], F32, f"feat{n}", FEAT1_AT if n == 1 else FEAT3_AT)
-            else:
-                feat = ringed([P, HALF], F32, "feat", bufs=3)
-            residual(g, 2 * u, 2, *((2, 4), (0, 6), (3, 1))[(n - 1) % 3], feat[:])
-            for e in range(2):
-                if u == 0:
-                    scatter(g * CHUNK, CHUNK, e)
-                elif g % 2:
-                    scatter(g // 2 * HALF, HALF, 2 * u + e)
-            if n == 1:
-                pair1 = placed([P, 16 * P], BF16, "pair1", PAIR1_AT)
-                for a in range(PASSES):
-                    group_wr(1, a, pair1[:, 8 * P * a : 8 * P * (a + 1)], nc.scalar.copy)
-                quantize_wr(1, 0, 4 * P, pair1[:])
-                nc.sync.dma_start(out=tol_sb[:], in_=tol.rearrange("(p t) m -> p t m", t=PAGES))
-            if n == 6:
-                wo_grouped = placed([P, 4, P, 4], BF16, "wo_grouped", WO_GROUPED_AT)
-                nc.scalar.copy(wo_grouped[:].rearrange("p t i j -> p i j t"), wo_raw[:].rearrange("p j (i t) -> p i j t", t=4))
-        nc.vector.quantize_mx(out=woc[:].bitcast(FP8X4), scales=wos[:], in_=wo_grouped[:].rearrange("p t i j -> p (t i j)"))
         for t in range(PAGES):
             excess(0, t)
         round_z(0)

@@ -226,12 +226,9 @@ def tile_list_handshake_anomaly_scores_kernel(
                 e = rows_tile("e", 4)
                 nc.scalar.activation(e[:], dealt(acc_e), ACT.Tanh, scale=-1.0)
                 rec = rows_tile("rec", 4)
-                if jt == 2:
-                    nc.vector.tensor_tensor(rec[:], dealt(acc_d), e[:], ALU.mult)
-                else:
-                    decoded = rows_tile("decoded", 3)
-                    nc.scalar.copy(decoded[:], dealt(acc_d))
-                    nc.gpsimd.tensor_tensor(rec[:], decoded[:], e[:], ALU.mult)
+                decoded = rows_tile("decoded", 3)
+                nc.scalar.copy(decoded[:], dealt(acc_d))
+                nc.gpsimd.tensor_tensor(rec[:], decoded[:], e[:], ALU.mult)
                 feat = rows_tile("feat", 4)
                 nc.scalar.copy(feat[:], paged(acc_c))
                 recs.append(rec)

@@ -61,6 +61,7 @@ def tile_list_handshake_anomaly_scores_kernel(
         TW0_AT = 0
         TW1_AT = TW0_AT + 4 * T
         WR_AT = TW1_AT + 4 * (CHUNKS * RUN + 384)
+        LAST_AT = WR_AT + 16384
         tw = [placed([P, T], U32, "tw0", TW0_AT), placed([P, T], U32, "tw1", TW1_AT)]
         ts = kept([P, T], U8, "ts")
         staged = kept([P, PLANE], U8, "staged")
@@ -127,15 +128,16 @@ def tile_list_handshake_anomaly_scores_kernel(
         gather_words(0, 1)
         nc.vector.memset(pages[3][:], 0.0)
 
-        def by_pages(raw, name):
-            grouped = ringed([P, 4, P, 4], BF16, "grouped_w")
+        def by_pages(raw, grouped):
             nc.scalar.copy(grouped[:].rearrange("p t i j -> p i j t"), raw[:].rearrange("p j (i t) -> p i j t", t=4))
-            codes = kept([P, H], U32, name + "_codes")
+            return grouped
+
+        def quantized(grouped, name, codes):
             scales = kept([P, H], U8, name + "_scales")
             nc.vector.quantize_mx(out=codes[:].bitcast(FP8X4), scales=scales[:], in_=grouped[:].rearrange("p t i j -> p (t i j)"))
             return codes, scales
 
-        wr_mx = [by_pages(wr_raw[a], f"wr{a}") for a in range(PASSES)]
+        wr_mx = [quantized(by_pages(wr_raw[a], kept([P, 4, P, 4], BF16, f"wr_grouped{a}")), f"wr{a}", kept([P, H], U32, f"wr_codes{a}")) for a in range(PASSES)]
         gather_words(1, 0, parts=2)
 
         wgs_sb = [kept([P, PAGES, GROUP], F32, f"wgs{g}") for g in range(GROUPS)]
@@ -145,8 +147,13 @@ def tile_list_handshake_anomaly_scores_kernel(
                 nc.sync.dma_start(out=wgs_sb[g][32 * q : 32 * (q + 1)], in_=rows)
         wo_raw = placed([P, 4, N], F32, "wo_raw", WR_AT)
         nc.sync.dma_start(out=wo_raw[:], in_=wo.rearrange("(p j) n -> p j n", j=4))
-        tol_sb = placed([P, PAGES, M], F32, "tol_sb", TW0_AT)
-        nc.sync.dma_start(out=tol_sb[:], in_=tol.rearrange("(p t) m -> p t m", t=PAGES))
+        tol_rows = tol.rearrange("(p t) m -> p t m", t=PAGES)
+        tol_first = placed([P, PAGES - 1, CHUNK], F32, "tol_first", TW0_AT)
+        tol_next = placed([P, CHUNK], F32, "tol_next", TW0_AT + 12 * CHUNK)
+        tol_rest = placed([P, PAGES, M - CHUNK], F32, "tol_rest", TW0_AT + 16 * CHUNK)
+        nc.sync.dma_start(out=tol_first[:], in_=tol_rows[:, 0 : PAGES - 1, 0:CHUNK])
+        nc.sync.dma_start(out=tol_next[:], in_=tol_rows[:, PAGES - 1, 0:CHUNK])
+        nc.sync.dma_start(out=tol_rest[:], in_=tol_rows[:, :, CHUNK:M])
         nc.sync.dma_start(idx3[:], offs3)
 
         def product(name, jt, bank, operands):
@@ -219,19 +226,19 @@ def tile_list_handshake_anomaly_scores_kernel(
         for g in range(1, GROUPS):
             feats, recs = [], []
             for k in range(2):
-                jt = 2 * g + k
-                acc_e = product("acc_e", jt, 7 - k, we_mx)
-                acc_d = product("acc_d", jt, 4 + k, wd_mx)
-                acc_c = product("acc_c", jt, 2 + k, wr_mx)
+                acc_e = product("acc_e", 2 * g + k, 7 - k, we_mx)
+                acc_d = product("acc_d", 2 * g + k, 4 + k, wd_mx)
                 e = rows_tile("e", 4)
                 nc.scalar.activation(e[:], dealt(acc_e), ACT.Tanh, scale=-1.0)
-                rec = rows_tile("rec", 4)
                 decoded = rows_tile("decoded", 3)
                 nc.scalar.copy(decoded[:], dealt(acc_d))
+                rec = rows_tile("rec", 4)
                 nc.gpsimd.tensor_tensor(rec[:], decoded[:], e[:], ALU.mult)
-                feat = rows_tile("feat", 4)
-                nc.scalar.copy(feat[:], paged(acc_c))
                 recs.append(rec)
+            for k in range(2):
+                acc_c = product("acc_c", 2 * g + k, 2 + k, wr_mx)
+                feat = placed([P, PAGES, P], F32, "feat_last", LAST_AT) if 2 * g + k == 2 * GROUPS - 1 else rows_tile("feat", 4)
+                nc.scalar.copy(feat[:], paged(acc_c))
                 feats.append(feat)
             for u in range(2):
                 mag = magnitudes(g, 2 * u, 2, u, recs, feats)
@@ -242,7 +249,7 @@ def tile_list_handshake_anomaly_scores_kernel(
                         weigh_and_put(g, e, 1, mag, e, nc.gpsimd)
                 else:
                     weigh_and_put(g, 2, 2, mag, 0, nc.gpsimd)
-        woc, wos = by_pages(wo_raw, "wo")
+        wo_grouped = by_pages(wo_raw, placed([P, 4, P, 4], BF16, "wo_grouped", LAST_AT))
         work = placed([P, CHUNKS * RUN + 384], F32, "work", TW1_AT)
 
         yc = kept([P, M], U32, "yc")
@@ -251,10 +258,13 @@ def tile_list_handshake_anomaly_scores_kernel(
         out_words = out_1[0].rearrange("p m t -> p (m t)").bitcast(I32)
 
         def excess(c, t):
-            cols = slice(c * CHUNK, (c + 1) * CHUNK)
+            if c:
+                bound = tol_rest[:, t, (c - 1) * CHUNK : c * CHUNK]
+            else:
+                bound = tol_first[:, t, :] if t + 1 < PAGES else tol_next[:]
             nc.vector.tensor_tensor(work[:, c * RUN + t * CHUNK : c * RUN + (t + 1) * CHUNK],
                                     pages[t][:].indirect(idx3[:, c * CHUNK // 16 : (c + 1) * CHUNK // 16]),
-                                    tol_sb[:, t, cols], ALU.subtract)
+                                    bound, ALU.subtract)
 
         def rounded_at(c):
             return ((c + 1) % CHUNKS) * RUN + 640
@@ -262,7 +272,7 @@ def tile_list_handshake_anomaly_scores_kernel(
         def round_z(c):
             both = work[:, rounded_at(c) : rounded_at(c) + 768].bitcast(BF16)
             for i in range(2):
-                (nc.vector.tensor_copy if (c, i) == (CHUNKS - 1, 1) else nc.scalar.copy)(
+                (nc.vector.tensor_copy if (c, i) == (CHUNKS - 1, 0) else nc.scalar.copy)(
                     both[:, 1024 * i : 1024 * i + 512].rearrange("p (m n t) -> p m t n", t=4, n=4),
                     work[:, c * RUN : (c + 1) * RUN].rearrange("p (t m n) -> p m t n", t=4, n=4)[:, i * P // 4 : (i + 1) * P // 4],
                 )
@@ -280,55 +290,66 @@ def tile_list_handshake_anomaly_scores_kernel(
                 )
             return acc
 
-        def empty(acc, i, y):
-            nc.scalar.copy(y[:, :, i * P : (i + 1) * P], acc[:].rearrange("p (t m) -> p t m", t=4))
+        y = placed([P, 4, M], F32, "y", WR_AT)
 
-        def round_y(c, acc, i, y, grouped):
-            cols = slice(i * P, (i + 1) * P)
-            if 2 * c + i < 5:
-                nc.scalar.copy(grouped[:, cols, :], acc[:].rearrange("p (t m) -> p m t", t=4))
-            else:
-                nc.vector.tensor_copy(grouped[:, cols, :].rearrange("p (m n) t -> p m t n", n=4), y[:, :, cols].rearrange("p t (m n) -> p m t n", n=4))
+        def half(c, i):
+            return slice(c * CHUNK + i * P, c * CHUNK + (i + 1) * P)
 
-        def finish(c, y, grouped):
-            cols = slice(c * CHUNK, (c + 1) * CHUNK)
-            nc.sync.dma_start(out=out_rows[:, :, cols], in_=y[:])
-            nc.vector.quantize_mx(out=yc[:, cols].bitcast(FP8X4), scales=ys[:, cols], in_=grouped[:].rearrange("p m t -> p (m t)"))
-            (nc.sync if c + 1 < CHUNKS else nc.scalar).dma_start(out=out_words[:, cols], in_=yc[:, cols].bitcast(I32))
+        def empty(acc, c, i):
+            nc.scalar.copy(y[:, :, half(c, i)], acc[:].rearrange("p (t m) -> p t m", t=4))
+
+        def round_from_bank(acc, grouped):
+            nc.scalar.copy(grouped, acc[:].rearrange("p (t m) -> p m t", t=4))
+
+        def round_from_rows(c, i, grouped):
+            nc.vector.tensor_copy(grouped.rearrange("p (m n) t -> p m t n", n=4), y[:, :, half(c, i)].rearrange("p t (m n) -> p m t n", n=4))
+
+        def store_y(lo, hi):
+            nc.sync.dma_start(out=out_rows[:, :, lo:hi], in_=y[:, :, lo:hi])
+
+        def quantize_y(cols, grouped):
+            nc.vector.quantize_mx(out=yc[:, cols].bitcast(FP8X4), scales=ys[:, cols], in_=grouped.rearrange("p m t -> p (m t)"))
 
         for t in range(PAGES):
             excess(0, t)
+        woc, wos = quantized(wo_grouped, "wo", placed([P, N], U32, "wo_codes", TW0_AT))
         round_z(0)
         for c in range(CHUNKS):
-            if c + 1 < CHUNKS:
+            last = c + 1 == CHUNKS
+            cols = slice(c * CHUNK, (c + 1) * CHUNK)
+            if not last:
                 excess(c + 1, 0)
                 excess(c + 1, 1)
-            accs = {i: quantize_z(c, i) for i in ((0, 1) if c + 1 < CHUNKS else (1, 0))}
-            if c + 1 < CHUNKS:
+            accs = [quantize_z(c, i) for i in range(2)]
+            if not last:
                 excess(c + 1, 2)
                 excess(c + 1, 3)
-            y = ringed([P, 4, CHUNK], F32, "y", bufs=3)
             grouped_y = ringed([P, CHUNK, 4], BF16, "grouped_y")
-            first, second = accs
-            empty(accs[first], first, y)
-            if c + 1 < CHUNKS:
+            parts = [grouped_y[:, i * P : (i + 1) * P, :] for i in range(2)]
+            empty(accs[0], c, 0)
+            if c >= 2:
+                store_y(cols.start - (P if last else 0), cols.start + P)
+            if last:
+                round_from_bank(accs[1], parts[1])
+            else:
                 round_z(c + 1)
+            empty(accs[1], c, 1)
+            if c < 2:
+                store_y(cols.start, cols.stop)
+                for i in range(2):
+                    round_from_bank(accs[i], parts[i])
+            elif last:
+                store_y(cols.start + P, cols.stop)
+                round_from_rows(c, 0, parts[0])
             else:
-                nc.scalar.copy(grouped_y[:, second * P : (second + 1) * P, :], accs[second][:].rearrange("p (t m) -> p m t", t=4))
-            empty(accs[second], second, y)
-            if c + 1 < CHUNKS:
-                for i in accs:
-                    round_y(c, accs[i], i, y, grouped_y)
-                finish(c, y, grouped_y)
+                for i in range(2):
+                    round_from_rows(c, i, parts[i])
+            if last:
+                for i in range(2):
+                    quantize_y(half(c, i), parts[i])
             else:
-                for i in accs:
-                    cols = slice(c * CHUNK + i * P, c * CHUNK + (i + 1) * P)
-                    nc.sync.dma_start(out=out_rows[:, :, cols], in_=y[:, :, i * P : (i + 1) * P])
-                    if i == first:
-                        round_y(c, accs[i], i, y, grouped_y)
-                    nc.vector.quantize_mx(out=yc[:, cols].bitcast(FP8X4), scales=ys[:, cols], in_=grouped_y[:, i * P : (i + 1) * P].rearrange("p m t -> p (m t)"))
-                cols = slice(c * CHUNK, M)
-                nc.scalar.dma_start(out=out_words[:, cols], in_=yc[:, cols].bitcast(I32))
+                quantize_y(cols, grouped_y[:])
+            (nc.scalar if last else nc.sync).dma_start(out=out_words[:, cols], in_=yc[:, cols].bitcast(I32))
         for q in range(4):
             queue = nc.sync if q % 2 == 0 else nc.scalar
             queue.dma_start(out=out_2[0, 4 * q : 4 * q + 4, :].bitcast(I32), in_=ys[32 * q : 32 * q + 4, :].bitcast(I32))

@@ -223,32 +223,37 @@ def tile_list_handshake_anomaly_scores_kernel(
         weigh_and_put(0, 1, 1, magnitudes(0, 1, 1, 0, recs, feats), 0, nc.gpsimd)
         weigh_and_put(0, 2, 2, magnitudes(0, 2, 2, 1, recs, feats), 0, nc.gpsimd)
 
+        def reconstruct(jt):
+            acc_e = product("acc_e", jt, 7 - jt % 2, we_mx)
+            acc_d = product("acc_d", jt, 4 + jt % 2, wd_mx)
+            e = rows_tile("e", 4)
+            nc.scalar.activation(e[:], dealt(acc_e), ACT.Tanh, scale=-1.0)
+            decoded = rows_tile("decoded", 3)
+            nc.scalar.copy(decoded[:], dealt(acc_d))
+            rec = rows_tile("rec", 4)
+            nc.gpsimd.tensor_tensor(rec[:], decoded[:], e[:], ALU.mult)
+            recs.append(rec)
+
+        reconstruct(2)
         for g in range(1, GROUPS):
-            feats, recs = [], []
-            for k in range(2):
-                acc_e = product("acc_e", 2 * g + k, 7 - k, we_mx)
-                acc_d = product("acc_d", 2 * g + k, 4 + k, wd_mx)
-                e = rows_tile("e", 4)
-                nc.scalar.activation(e[:], dealt(acc_e), ACT.Tanh, scale=-1.0)
-                decoded = rows_tile("decoded", 3)
-                nc.scalar.copy(decoded[:], dealt(acc_d))
-                rec = rows_tile("rec", 4)
-                nc.gpsimd.tensor_tensor(rec[:], decoded[:], e[:], ALU.mult)
-                recs.append(rec)
+            reconstruct(2 * g + 1)
+            feats = []
             for k in range(2):
                 acc_c = product("acc_c", 2 * g + k, 2 + k, wr_mx)
                 feat = placed([P, PAGES, P], F32, "feat_last", LAST_AT) if 2 * g + k == 2 * GROUPS - 1 else rows_tile("feat", 4)
                 nc.scalar.copy(feat[:], paged(acc_c))
                 feats.append(feat)
+            if g + 1 < GROUPS:
+                reconstruct(2 * g + 2)
             for u in range(2):
-                mag = magnitudes(g, 2 * u, 2, u, recs, feats)
+                mag = magnitudes(g, 2 * u, 2, u, recs[2 * g : 2 * g + 2], feats)
                 if g + 1 == GROUPS:
                     put_fused(g, 2 * u, mag)
-                elif u == 0:
+                elif (g, u) == (1, 0):
                     for e in range(2):
                         weigh_and_put(g, e, 1, mag, e, nc.gpsimd)
                 else:
-                    weigh_and_put(g, 2, 2, mag, 0, nc.gpsimd)
+                    weigh_and_put(g, 2 * u, 2, mag, 0, nc.gpsimd)
         wo_grouped = by_pages(wo_raw, placed([P, 4, P, 4], BF16, "wo_grouped", LAST_AT))
         work = placed([P, CHUNKS * RUN + 384], F32, "work", TW1_AT)
 

@@ -94,9 +94,9 @@ def tile_list_handshake_anomaly_scores_kernel(
         stage_rows(staged[STAGE:P, WD_AT:PLANE], wd_scales)
         for a in range(PASSES):
             nc.sync.dma_start(out=wr_raw[a][:], in_=wr[512 * a : 512 * (a + 1), :].rearrange("(p j) c -> p j c", j=4))
-        nc.sync.dma_start(idx2[:], offs2)
         load_table(1, 0, T // 2)
         load_we(0)
+        load_wd(0)
 
         vw = [[kept([P, HALF], U32, f"vw{a}{h}") for h in range(2)] for a in range(PASSES)]
         planes = [kept([P, PLANE], U8, f"plane{a}") for a in range(PASSES)]
@@ -118,7 +118,6 @@ def tile_list_handshake_anomaly_scores_kernel(
                 nc.sync.dma_start(out=planes[a][r:P:32, :].bitcast(I32), in_=rows.bitcast(I32))
 
         move_scales(0)
-        load_wd(0)
         load_table(1, T // 2, T)
         load_we(1)
         move_scales(1)
@@ -143,8 +142,11 @@ def tile_list_handshake_anomaly_scores_kernel(
         wgs_sb = [kept([P, PAGES, GROUP], F32, f"wgs{g}") for g in range(GROUPS)]
         for g in range(GROUPS):
             rows = wgs.rearrange("(i t) j -> i t j", t=PAGES)[:, :, g * GROUP : (g + 1) * GROUP]
-            for q in (0, 2, 1, 3):
-                nc.sync.dma_start(out=wgs_sb[g][32 * q : 32 * (q + 1)], in_=rows)
+            for part in ((slice(0, 2), slice(2, PAGES)) if g == 0 else (slice(0, PAGES),)):
+                for q in (0, 2, 1, 3):
+                    nc.sync.dma_start(out=wgs_sb[g][32 * q : 32 * (q + 1), part], in_=rows[:, part])
+            if g == 0:
+                nc.sync.dma_start(idx2[:], offs2)
         wo_raw = placed([P, 4, N], F32, "wo_raw", WR_AT)
         nc.sync.dma_start(out=wo_raw[:], in_=wo.rearrange("(p j) n -> p j n", j=4))
         tol_rows = tol.rearrange("(p t) m -> p t m", t=PAGES)

@@ -269,9 +269,11 @@ def tile_list_handshake_anomaly_scores_kernel(
                 bound = tol_rest[:, t, (c - 1) * CHUNK : c * CHUNK]
             else:
                 bound = tol_first[:, t, :] if t + 1 < PAGES else tol_next[:]
-            nc.vector.tensor_tensor(work[:, c * RUN + t * CHUNK : c * RUN + (t + 1) * CHUNK],
-                                    pages[t][:].indirect(idx3[:, c * CHUNK // 16 : (c + 1) * CHUNK // 16]),
-                                    bound, ALU.subtract)
+            width = P if (c, t) == (CHUNKS - 1, PAGES - 1) else CHUNK
+            for lo in range(0, CHUNK, width):
+                at, first = c * RUN + t * CHUNK + lo, c * CHUNK + lo
+                nc.vector.tensor_tensor(work[:, at : at + width], pages[t][:].indirect(idx3[:, first // 16 : (first + width) // 16]),
+                                        bound[:, lo : lo + width], ALU.subtract)
 
         def rounded_at(c):
             return ((c + 1) % CHUNKS) * RUN + 640
@@ -279,7 +281,7 @@ def tile_list_handshake_anomaly_scores_kernel(
         def round_z(c):
             both = work[:, rounded_at(c) : rounded_at(c) + 768].bitcast(BF16)
             for i in range(2):
-                (nc.vector.tensor_copy if (c, i) == (CHUNKS - 1, 0) else nc.scalar.copy)(
+                (nc.vector.tensor_copy if c == CHUNKS - 1 else nc.scalar.copy)(
                     both[:, 1024 * i : 1024 * i + 512].rearrange("p (m n t) -> p m t n", t=4, n=4),
                     work[:, c * RUN : (c + 1) * RUN].rearrange("p (t m n) -> p m t n", t=4, n=4)[:, i * P // 4 : (i + 1) * P // 4],
                 )
@@ -335,7 +337,7 @@ def tile_list_handshake_anomaly_scores_kernel(
             parts = [grouped_y[:, i * P : (i + 1) * P, :] for i in range(2)]
             empty(accs[0], c, 0)
             if c >= 2:
-                store_y(cols.start - (P if last else 0), cols.start + P)
+                store_y(cols.start, cols.start + P)
             if last:
                 round_from_bank(accs[1], parts[1])
             else:
@@ -349,6 +351,7 @@ def tile_list_handshake_anomaly_scores_kernel(
                 store_y(cols.start + P, cols.stop)
                 round_from_rows(c, 0, parts[0])
             else:
+                store_y(cols.start + P, cols.stop)
                 for i in range(2):
                     round_from_rows(c, i, parts[i])
             if last:

@@ -336,7 +336,7 @@ def tile_list_handshake_anomaly_scores_kernel(
             grouped_y = ringed([P, CHUNK, 4], BF16, "grouped_y")
             parts = [grouped_y[:, i * P : (i + 1) * P, :] for i in range(2)]
             empty(accs[0], c, 0)
-            if c >= 2:
+            if last:
                 store_y(cols.start, cols.start + P)
             if last:
                 round_from_bank(accs[1], parts[1])
@@ -351,7 +351,7 @@ def tile_list_handshake_anomaly_scores_kernel(
                 store_y(cols.start + P, cols.stop)
                 round_from_rows(c, 0, parts[0])
             else:
-                store_y(cols.start + P, cols.stop)
+                store_y(cols.start, cols.stop)
                 for i in range(2):
                     round_from_rows(c, i, parts[i])
             if last:
@@ -359,7 +359,10 @@ def tile_list_handshake_anomaly_scores_kernel(
                     quantize_y(half(c, i), parts[i])
             else:
                 quantize_y(cols, grouped_y[:])
-            (nc.scalar if last else nc.sync).dma_start(out=out_words[:, cols], in_=yc[:, cols].bitcast(I32))
+            if last:
+                cols = slice(cols.start - CHUNK, cols.stop)
+            if c != 2:
+                (nc.scalar if last else nc.sync).dma_start(out=out_words[:, cols], in_=yc[:, cols].bitcast(I32))
         for q in range(4):
             queue = nc.sync if q % 2 == 0 else nc.scalar
             queue.dma_start(out=out_2[0, 4 * q : 4 * q + 4, :].bitcast(I32), in_=ys[32 * q : 32 * q + 4, :].bitcast(I32))

@@ -338,9 +338,7 @@ def tile_list_handshake_anomaly_scores_kernel(
             empty(accs[0], c, 0)
             if last:
                 store_y(cols.start, cols.start + P)
-            if last:
-                round_from_bank(accs[1], parts[1])
-            else:
+            if not last:
                 round_z(c + 1)
             empty(accs[1], c, 1)
             if c < 2:
@@ -349,7 +347,8 @@ def tile_list_handshake_anomaly_scores_kernel(
                     round_from_bank(accs[i], parts[i])
             elif last:
                 store_y(cols.start + P, cols.stop)
-                round_from_rows(c, 0, parts[0])
+                for i in range(2):
+                    round_from_rows(c, i, parts[i])
             else:
                 store_y(cols.start, cols.stop)
                 for i in range(2):

@@ -23,7 +23,6 @@ PAGES = H // P
 HALF = 512
 CHUNK = 256
 CHUNKS = M // CHUNK
-STAGE = 96
 WE_AT, WD_AT, PLANE = S, S + H, S + 2 * H
 GROUP = 256
 GROUPS = S // GROUP
@@ -70,7 +69,7 @@ def tile_list_handshake_anomaly_scores_kernel(
         ident = kept([P, P], F32, "ident")
         wr_raw = [placed([P, 4, H], F32, f"wr_raw{a}", WR_AT + 8192 * a) for a in range(PASSES)]
 
-        nc.vector.memset(ts[0:STAGE, :].bitcast(I32), 0)
+        nc.vector.memset(ts[:].bitcast(I32), 0)
         make_identity(nc, ident[:])
         nc.vector.memset(pages[0][:], 0.0)
         nc.vector.memset(pages[1][:], 0.0)
@@ -88,10 +87,10 @@ def tile_list_handshake_anomaly_scores_kernel(
             nc.sync.dma_start(out=packed[a][:, 2 * H : 6 * H].bitcast(I32), in_=wd_words[a].rearrange("p c i -> p (c i)").bitcast(I32))
 
         nc.sync.dma_start(idx[:], offs)
-        stage_rows(ts[STAGE:P, :], tab_scales)
         load_table(0, 0, T)
-        stage_rows(staged[STAGE:P, WE_AT:WD_AT], we_scales)
-        stage_rows(staged[STAGE:P, WD_AT:PLANE], wd_scales)
+        stage_rows(ts[0:P:4, :], tab_scales)
+        stage_rows(staged[0:P:4, WE_AT:WD_AT], we_scales)
+        stage_rows(staged[0:P:4, WD_AT:PLANE], wd_scales)
         for a in range(PASSES):
             nc.sync.dma_start(out=wr_raw[a][:], in_=wr[512 * a : 512 * (a + 1), :].rearrange("(p j) c -> p j c", j=4))
         load_table(1, 0, T // 2)
@@ -109,12 +108,12 @@ def tile_list_handshake_anomaly_scores_kernel(
                 nc.vector.tensor_copy(vw[a][h][:, lo : lo + width], tw[a][:].indirect(idx[:, first // 16 : (first + width) // 16]))
 
         nc.vector.tensor_copy(picked[:], ts[:].indirect(idx[:]))
-        nc.vector.tensor_copy(staged[STAGE:P, 0:S].bitcast(I32), picked[STAGE:P, :].bitcast(I32))
+        nc.vector.tensor_copy(staged[:, 0:S].bitcast(I32), picked[:].bitcast(I32))
         nc.vector.memset(pages[2][:], 0.0)
 
         def move_scales(a):
             for r in range(4):
-                rows = staged[STAGE + 16 * a + r : STAGE + 16 * (a + 1) : 4, :]
+                rows = staged[64 * a + 4 * r : 64 * (a + 1) : 16, :]
                 nc.sync.dma_start(out=planes[a][r:P:32, :].bitcast(I32), in_=rows.bitcast(I32))
 
         move_scales(0)

@@ -23,7 +23,8 @@ PAGES = H // P
 HALF = 512
 CHUNK = 256
 CHUNKS = M // CHUNK
-WE_AT, WD_AT, PLANE = S, S + H, S + 2 * H
+WE_AT, PLANE = S, S + H
+WD_ROW = 4
 GROUP = 256
 GROUPS = S // GROUP
 
@@ -87,10 +88,14 @@ def tile_list_handshake_anomaly_scores_kernel(
             nc.sync.dma_start(out=packed[a][:, 2 * H : 6 * H].bitcast(I32), in_=wd_words[a].rearrange("p c i -> p (c i)").bitcast(I32))
 
         nc.sync.dma_start(idx[:], offs)
-        load_table(0, 0, T)
+        load_table(0, 0, T // 2)
         stage_rows(ts[0:P:4, :], tab_scales)
-        stage_rows(staged[0:P:4, WE_AT:WD_AT], we_scales)
-        stage_rows(staged[0:P:4, WD_AT:PLANE], wd_scales)
+        load_table(0, T // 2, T)
+        stage_rows(staged[0:P:4, WE_AT:PLANE], we_scales)
+        wd_planes = kept([P, PASSES, H], U8, "wd_planes")
+        for q in range(4):
+            rows = wd_scales.rearrange("a q c -> q a c")[4 * q : 4 * q + 4]
+            nc.sync.dma_start(out=wd_planes[32 * q + WD_ROW : 32 * q + WD_ROW + 4].bitcast(I32), in_=rows.bitcast(I32))
         for a in range(PASSES):
             nc.sync.dma_start(out=wr_raw[a][:], in_=wr[512 * a : 512 * (a + 1), :].rearrange("(p j) c -> p j c", j=4))
         load_table(1, 0, T // 2)
@@ -167,8 +172,8 @@ def tile_list_handshake_anomaly_scores_kernel(
                 )
             return acc
 
-        we_mx = [(packed[a][:, 0 : 2 * H].bitcast(FP4X4), planes[a][:, WE_AT:WD_AT]) for a in range(PASSES)]
-        wd_mx = [(packed[a][:, 2 * H : 6 * H].bitcast(FP8X4), planes[a][:, WD_AT:PLANE]) for a in range(PASSES)]
+        we_mx = [(packed[a][:, 0 : 2 * H].bitcast(FP4X4), planes[a][:, WE_AT:PLANE]) for a in range(PASSES)]
+        wd_mx = [(packed[a][:, 2 * H : 6 * H].bitcast(FP8X4), wd_planes[WD_ROW:P, a, :]) for a in range(PASSES)]
         wr_mx = [(codes[:].bitcast(FP8X4), scales[:]) for codes, scales in wr_mx]
 
         def dealt(bank):

from contextlib import ExitStack

import concourse.mybir as mybir
from concourse.masks import make_identity

K, H, N, T, S, T2, M = 1024, 512, 512, 4096, 1024, 2048, 1024
FLOPS = 2 * 3 * K * H * S + 2 * H * N * M

F32 = mybir.dt.float32
BF16 = mybir.dt.bfloat16
I32 = mybir.dt.int32
U32 = mybir.dt.uint32
U16 = mybir.dt.uint16
U8 = mybir.dt.uint8
FP8X4 = mybir.dt.float8_e4m3fn_x4
FP4X4 = mybir.dt.float4_e2m1fn_x4
ACT = mybir.ActivationFunctionType
ALU = mybir.AluOpType

P = 128
PASSES = K // 512
PAGES = H // P
HALF = 512
CHUNK = 256
CHUNKS = M // CHUNK
WE_AT, PLANE = S, S + H
WD_ROW = 4
GROUP = 256
GROUPS = S // GROUP


def tile_list_handshake_anomaly_scores_kernel(
    tc, tab_words, tab_scales, offs, offs2, offs3, we_words, we_scales,
    wd_words, wd_scales, wr, wgs, tol, wo, out_0, out_1, out_2,
):
    nc = tc.nc
    with ExitStack() as ctx:
        lists = ctx.enter_context(tc.tile_pool(name="lists", bufs=1))
        keep = ctx.enter_context(tc.tile_pool(name="keep", bufs=1))
        ring = ctx.enter_context(tc.tile_pool(name="ring", bufs=2))
        reuse = ctx.enter_context(tc.tile_pool(name="reuse", bufs=1))
        psum = ctx.enter_context(tc.psum_pool(name="psum", bufs=1))

        idx = lists.tile([P, S // 16], U16, name="idx")
        idx2 = lists.tile([P, S // 16], U16, name="idx2")
        idx3 = lists.tile([P, M // 16], U16, name="idx3")

        def kept(shape, dtype, name):
            return keep.tile(shape, dtype, name=name, align_bytes=64)

        def ringed(shape, dtype, name, bufs=2):
            return ring.tile(shape, dtype, name=name, bufs=bufs, align_bytes=64)

        def placed(shape, dtype, name, offset):
            return reuse.tile(shape, dtype, name=name, offset=offset, align_bytes=64)

        def bank_tile(name, bank):
            return psum.tile([P, HALF], F32, name=name, offset=2048 * bank)

        RUN = PAGES * CHUNK
        TW0_AT = 0
        TW1_AT = TW0_AT + 4 * T
        WR_AT = TW1_AT + 4 * (CHUNKS * RUN + 384)
        LAST_AT = WR_AT + 16384
        tw = [placed([P, T], U32, "tw0", TW0_AT), placed([P, T], U32, "tw1", TW1_AT)]
        ts = kept([P, T], U8, "ts")
        staged = kept([P, PLANE], U8, "staged")
        packed = [kept([P, 6 * H], U8, f"packed{a}") for a in range(PASSES)]
        pages = [kept([P, T2], F32, f"page{t}") for t in range(PAGES)]
        ident = kept([P, P], F32, "ident")
        wr_raw = [placed([P, 4, H], F32, f"wr_raw{a}", WR_AT + 8192 * a) for a in range(PASSES)]

        nc.vector.memset(ts[:].bitcast(I32), 0)
        make_identity(nc, ident[:])
        nc.vector.memset(pages[0][:], 0.0)
        nc.vector.memset(pages[1][:], 0.0)

        def stage_rows(dst, src):
            nc.sync.dma_start(out=dst.bitcast(I32), in_=src.rearrange("a q c -> (a q) c").bitcast(I32))

        def load_table(a, lo, hi):
            nc.sync.dma_start(out=tw[a][:, lo:hi].bitcast(I32), in_=tab_words[a].rearrange("p t i -> p (t i)").bitcast(I32)[:, lo:hi])

        def load_we(a):
            nc.sync.dma_start(out=packed[a][:, 0 : 2 * H].bitcast(I32), in_=we_words[a].bitcast(I32))

        def load_wd(a):
            nc.sync.dma_start(out=packed[a][:, 2 * H : 6 * H].bitcast(I32), in_=wd_words[a].rearrange("p c i -> p (c i)").bitcast(I32))

        nc.sync.dma_start(idx[:], offs)
        load_table(0, 0, T // 2)
        stage_rows(ts[0:P:4, :], tab_scales)
        load_table(0, T // 2, T)
        stage_rows(staged[0:P:4, WE_AT:PLANE], we_scales)
        wd_planes = kept([P, PASSES, H], U8, "wd_planes")
        for q in range(4):
            rows = wd_scales.rearrange("a q c -> q a c")[4 * q : 4 * q + 4]
            nc.sync.dma_start(out=wd_planes[32 * q + WD_ROW : 32 * q + WD_ROW + 4].bitcast(I32), in_=rows.bitcast(I32))
        for a in range(PASSES):
            nc.sync.dma_start(out=wr_raw[a][:], in_=wr[512 * a : 512 * (a + 1), :].rearrange("(p j) c -> p j c", j=4))
        load_table(1, 0, T // 2)
        load_we(0)
        load_wd(0)

        vw = [[kept([P, HALF], U32, f"vw{a}{h}") for h in range(2)] for a in range(PASSES)]
        planes = [kept([P, PLANE], U8, f"plane{a}") for a in range(PASSES)]
        picked = kept([P, S], U8, "picked")

        def gather_words(a, h, parts=1):
            width = HALF // parts
            for lo in range(0, HALF, width):
                first = h * HALF + lo
                nc.vector.tensor_copy(vw[a][h][:, lo : lo + width], tw[a][:].indirect(idx[:, first // 16 : (first + width) // 16]))

        nc.vector.tensor_copy(picked[:], ts[:].indirect(idx[:]))
        nc.vector.tensor_copy(staged[:, 0:S].bitcast(I32), picked[:].bitcast(I32))
        nc.vector.memset(pages[2][:], 0.0)

        def move_scales(a):
            for r in range(4):
                rows = staged[64 * a + 4 * r : 64 * (a + 1) : 16, :]
                nc.sync.dma_start(out=planes[a][r:P:32, :].bitcast(I32), in_=rows.bitcast(I32))

        move_scales(0)
        load_table(1, T // 2, T)
        load_we(1)
        move_scales(1)
        load_wd(1)

        gather_words(0, 0)
        gather_words(0, 1)
        nc.vector.memset(pages[3][:], 0.0)

        def by_pages(raw, grouped):
            nc.scalar.copy(grouped[:].rearrange("p t i j -> p i j t"), raw[:].rearrange("p j (i t) -> p i j t", t=4))
            return grouped

        def quantized(grouped, name, codes):
            scales = kept([P, H], U8, name + "_scales")
            nc.vector.quantize_mx(out=codes[:].bitcast(FP8X4), scales=scales[:], in_=grouped[:].rearrange("p t i j -> p (t i j)"))
            return codes, scales

        wr_mx = [quantized(by_pages(wr_raw[a], kept([P, 4, P, 4], BF16, f"wr_grouped{a}")), f"wr{a}", kept([P, H], U32, f"wr_codes{a}")) for a in range(PASSES)]
        gather_words(1, 0, parts=2)

        wgs_sb = [kept([P, PAGES, GROUP], F32, f"wgs{g}") for g in range(GROUPS)]
        for g in range(GROUPS):
            rows = wgs.rearrange("(i t) j -> i t j", t=PAGES)[:, :, g * GROUP : (g + 1) * GROUP]
            for part in ((slice(0, 2), slice(2, PAGES)) if g == 0 else (slice(0, PAGES),)):
                for q in (0, 2, 1, 3):
                    nc.sync.dma_start(out=wgs_sb[g][32 * q : 32 * (q + 1), part], in_=rows[:, part])
            if g == 0:
                nc.sync.dma_start(idx2[:], offs2)
        wo_raw = placed([P, 4, N], F32, "wo_raw", WR_AT)
        nc.sync.dma_start(out=wo_raw[:], in_=wo.rearrange("(p j) n -> p j n", j=4))
        tol_rows = tol.rearrange("(p t) m -> p t m", t=PAGES)
        tol_first = placed([P, PAGES - 1, CHUNK], F32, "tol_first", TW0_AT)
        tol_next = placed([P, CHUNK], F32, "tol_next", TW0_AT + 12 * CHUNK)
        tol_rest = placed([P, PAGES, M - CHUNK], F32, "tol_rest", TW0_AT + 16 * CHUNK)
        nc.sync.dma_start(out=tol_first[:], in_=tol_rows[:, 0 : PAGES - 1, 0:CHUNK])
        nc.sync.dma_start(out=tol_next[:], in_=tol_rows[:, PAGES - 1, 0:CHUNK])
        nc.sync.dma_start(out=tol_rest[:], in_=tol_rows[:, :, CHUNK:M])
        nc.sync.dma_start(idx3[:], offs3)

        def product(name, jt, bank, operands):
            acc = bank_tile(f"{name}{jt}", bank)
            h, lo = divmod(jt * P, HALF)
            for a, (codes, scales) in enumerate(operands):
                nc.tensor.matmul_mx(
                    out=acc[:], lhsT=vw[a][h][:, lo : lo + P].bitcast(FP8X4), lhsT_scale=planes[a][:, jt * P : (jt + 1) * P],
                    rhs=codes, rhs_scale=scales, start=a == 0, stop=a == 1,
                )
            return acc

        we_mx = [(packed[a][:, 0 : 2 * H].bitcast(FP4X4), planes[a][:, WE_AT:PLANE]) for a in range(PASSES)]
        wd_mx = [(packed[a][:, 2 * H : 6 * H].bitcast(FP8X4), wd_planes[WD_ROW:P, a, :]) for a in range(PASSES)]
        wr_mx = [(codes[:].bitcast(FP8X4), scales[:]) for codes, scales in wr_mx]

        def dealt(bank):
            return bank[:].rearrange("p (i t) -> p t i", t=PAGES)

        def paged(bank):
            return bank[:].rearrange("p (t i) -> p t i", t=PAGES)

        def rows_tile(name, bufs):
            return ringed([P, PAGES, P], F32, name, bufs=bufs)

        def magnitudes(g, first, count, bank, recs, feats):
            acc = bank_tile(f"acc_h{g}_{first}", bank)
            places = [(e, k) for e in range(count) for k in range(2)]
            for n, (e, k) in enumerate(places):
                nc.tensor.matmul(acc[:, n * P : (n + 1) * P], feats[k][:, first + e, :], ident[:], start=(n == 0), stop=False, is_transpose=True)
            for n, (e, k) in enumerate(places):
                nc.tensor.matmul(acc[:, n * P : (n + 1) * P], recs[k][:, first + e, :], ident[:], start=False, stop=(n + 1 == len(places)), is_transpose=True)
            mag = ringed([P, 2, GROUP], F32, "mag", bufs=4)
            nc.scalar.activation(mag[:, 0:count, :], acc[:, 0 : count * GROUP].rearrange("p (e j) -> p e j", e=count), ACT.Abs)
            return mag

        def offsets2(g):
            return idx2[:, g * GROUP // 16 : (g + 1) * GROUP // 16]

        def weigh_and_put(g, first, count, mag, at, engine):
            weighted = ringed([P, 2, GROUP], F32, "weighted", bufs=6)
            engine.tensor_tensor(weighted[:, 0:count, :], mag[:, at : at + count, :], wgs_sb[g][:, first : first + count, :], ALU.mult)
            for e in range(count):
                nc.vector.tensor_copy(pages[first + e][:].indirect(offsets2(g)), weighted[:, e, :])

        def put_fused(g, first, mag):
            for e in range(2):
                nc.vector.tensor_tensor(pages[first + e][:].indirect(offsets2(g)), mag[:, e, :], wgs_sb[g][:, first + e, :], ALU.mult)

        acc_e = [product("acc_e", k, k, we_mx) for k in range(2)]
        acc_c = [product("acc_c", k, 2 + k, wr_mx) for k in range(2)]
        acc_d = [product("acc_d", k, 4 + k, wd_mx) for k in range(2)]
        es = [rows_tile("e", 4) for k in range(2)]
        feats = [rows_tile("feat", 4) for k in range(2)]
        recs = [rows_tile("rec", 4) for k in range(2)]
        for part in (slice(0, 1), slice(1, PAGES)):
            for k in range(2):
                nc.scalar.activation(es[k][:, part, :], dealt(acc_e[k])[:, part, :], ACT.Tanh, scale=-1.0)
            for k in range(2):
                nc.scalar.copy(feats[k][:, part, :], paged(acc_c[k])[:, part, :])
            for k in range(2):
                nc.vector.tensor_tensor(recs[k][:, part, :], dealt(acc_d[k])[:, part, :], es[k][:, part, :], ALU.mult)
            if part.start == 0:
                mag = magnitudes(0, 0, 1, 6, recs, feats)
                gather_words(1, 1)
                weigh_and_put(0, 0, 1, mag, 0, nc.vector)
        weigh_and_put(0, 1, 1, magnitudes(0, 1, 1, 0, recs, feats), 0, nc.gpsimd)
        weigh_and_put(0, 2, 2, magnitudes(0, 2, 2, 1, recs, feats), 0, nc.gpsimd)

        def reconstruct(jt):
            acc_e = product("acc_e", jt, 7 - jt % 2, we_mx)
            acc_d = product("acc_d", jt, 4 + jt % 2, wd_mx)
            e = rows_tile("e", 4)
            nc.scalar.activation(e[:], dealt(acc_e), ACT.Tanh, scale=-1.0)
            decoded = rows_tile("decoded", 3)
            nc.scalar.copy(decoded[:], dealt(acc_d))
            rec = rows_tile("rec", 4)
            nc.gpsimd.tensor_tensor(rec[:], decoded[:], e[:], ALU.mult)
            recs.append(rec)

        reconstruct(2)
        for g in range(1, GROUPS):
            reconstruct(2 * g + 1)
            feats = []
            for k in range(2):
                acc_c = product("acc_c", 2 * g + k, 2 + k, wr_mx)
                feat = placed([P, PAGES, P], F32, "feat_last", LAST_AT) if 2 * g + k == 2 * GROUPS - 1 else rows_tile("feat", 4)
                nc.scalar.copy(feat[:], paged(acc_c))
                feats.append(feat)
            if g + 1 < GROUPS:
                reconstruct(2 * g + 2)
            for u in range(2):
                mag = magnitudes(g, 2 * u, 2, u, recs[2 * g : 2 * g + 2], feats)
                if g + 1 == GROUPS:
                    put_fused(g, 2 * u, mag)
                elif (g, u) == (1, 0):
                    for e in range(2):
                        weigh_and_put(g, e, 1, mag, e, nc.gpsimd)
                else:
                    weigh_and_put(g, 2 * u, 2, mag, 0, nc.gpsimd)
        wo_grouped = by_pages(wo_raw, placed([P, 4, P, 4], BF16, "wo_grouped", LAST_AT))
        work = placed([P, CHUNKS * RUN + 384], F32, "work", TW1_AT)

        yc = kept([P, M], U32, "yc")
        ys = kept([P, M], U8, "ys")
        out_rows = out_0.rearrange("(p t) m -> p t m", t=4)
        out_words = out_1[0].rearrange("p m t -> p (m t)").bitcast(I32)

        def excess(c, t):
            if c:
                bound = tol_rest[:, t, (c - 1) * CHUNK : c * CHUNK]
            else:
                bound = tol_first[:, t, :] if t + 1 < PAGES else tol_next[:]
            width = P if (c, t) == (CHUNKS - 1, PAGES - 1) else CHUNK
            for lo in range(0, CHUNK, width):
                at, first = c * RUN + t * CHUNK + lo, c * CHUNK + lo
                nc.vector.tensor_tensor(work[:, at : at + width], pages[t][:].indirect(idx3[:, first // 16 : (first + width) // 16]),
                                        bound[:, lo : lo + width], ALU.subtract)

        def rounded_at(c):
            return ((c + 1) % CHUNKS) * RUN + 640

        def round_z(c):
            both = work[:, rounded_at(c) : rounded_at(c) + 768].bitcast(BF16)
            for i in range(2):
                (nc.vector.tensor_copy if c == CHUNKS - 1 else nc.scalar.copy)(
                    both[:, 1024 * i : 1024 * i + 512].rearrange("p (m n t) -> p m t n", t=4, n=4),
                    work[:, c * RUN : (c + 1) * RUN].rearrange("p (t m n) -> p m t n", t=4, n=4)[:, i * P // 4 : (i + 1) * P // 4],
                )

        def quantize_z(c, i):
            zc = ringed([P, P], U32, "zc", bufs=4)
            zs = ringed([P, P], U8, "zs", bufs=4)
            at = rounded_at(c) + 512 * i
            nc.vector.quantize_mx(out=zc[:].bitcast(FP8X4), scales=zs[:], in_=work[:, at : at + 256].bitcast(BF16))
            acc = bank_tile(f"acc_y{c}_{i}", (0, 2, 1, 3, 5, 7, 4, 6)[2 * c + i])
            for t in range(4):
                nc.tensor.matmul_mx(
                    out=acc[:, t * P : (t + 1) * P], lhsT=woc[:, t * P : (t + 1) * P].bitcast(FP8X4),
                    lhsT_scale=wos[:, t * P : (t + 1) * P], rhs=zc[:].bitcast(FP8X4), rhs_scale=zs[:], start=True, stop=True,
                )
            return acc

        y = placed([P, 4, M], F32, "y", WR_AT)

        def half(c, i):
            return slice(c * CHUNK + i * P, c * CHUNK + (i + 1) * P)

        def empty(acc, c, i):
            nc.scalar.copy(y[:, :, half(c, i)], acc[:].rearrange("p (t m) -> p t m", t=4))

        def round_from_bank(acc, grouped):
            nc.scalar.copy(grouped, acc[:].rearrange("p (t m) -> p m t", t=4))

        def round_from_rows(c, i, grouped):
            nc.vector.tensor_copy(grouped.rearrange("p (m n) t -> p m t n", n=4), y[:, :, half(c, i)].rearrange("p t (m n) -> p m t n", n=4))

        def store_y(lo, hi):
            nc.sync.dma_start(out=out_rows[:, :, lo:hi], in_=y[:, :, lo:hi])

        def quantize_y(cols, grouped):
            nc.vector.quantize_mx(out=yc[:, cols].bitcast(FP8X4), scales=ys[:, cols], in_=grouped.rearrange("p m t -> p (m t)"))

        for t in range(PAGES):
            excess(0, t)
        woc, wos = quantized(wo_grouped, "wo", placed([P, N], U32, "wo_codes", TW0_AT))
        round_z(0)
        for c in range(CHUNKS):
            last = c + 1 == CHUNKS
            cols = slice(c * CHUNK, (c + 1) * CHUNK)
            if not last:
                excess(c + 1, 0)
                excess(c + 1, 1)
            accs = [quantize_z(c, i) for i in range(2)]
            if not last:
                excess(c + 1, 2)
                excess(c + 1, 3)
            grouped_y = ringed([P, CHUNK, 4], BF16, "grouped_y")
            parts = [grouped_y[:, i * P : (i + 1) * P, :] for i in range(2)]
            empty(accs[0], c, 0)
            if last:
                store_y(cols.start, cols.start + P)
            if not last:
                round_z(c + 1)
            empty(accs[1], c, 1)
            if c < 2:
                store_y(cols.start, cols.stop)
                for i in range(2):
                    round_from_bank(accs[i], parts[i])
            elif last:
                store_y(cols.start + P, cols.stop)
                for i in range(2):
                    round_from_rows(c, i, parts[i])
            else:
                store_y(cols.start, cols.stop)
                for i in range(2):
                    round_from_rows(c, i, parts[i])
            if last:
                for i in range(2):
                    quantize_y(half(c, i), parts[i])
            else:
                quantize_y(cols, grouped_y[:])
            if last:
                cols = slice(cols.start - CHUNK, cols.stop)
            if c != 2:
                (nc.scalar if last else nc.sync).dma_start(out=out_words[:, cols], in_=yc[:, cols].bitcast(I32))
        for q in range(4):
            queue = nc.sync if q % 2 == 0 else nc.scalar
            queue.dma_start(out=out_2[0, 4 * q : 4 * q + 4, :].bitcast(I32), in_=ys[32 * q : 32 * q + 4, :].bitcast(I32))
